import numpy as np
import ml_dtypes


def mxq(x, axis, fmt="e4m3"):
    dtype, down = {"e4m3": (ml_dtypes.float8_e4m3fn, 7), "e5m2": (ml_dtypes.float8_e5m2, 14)}[fmt]
    v = np.moveaxis(np.asarray(x, np.float32).astype(ml_dtypes.bfloat16).astype(np.float64), axis, -1)
    blocks = v.reshape(v.shape[:-1] + (-1, 32))
    amax = np.abs(blocks).max(-1, keepdims=True)
    byte = np.maximum(np.where(amax > 0, np.frexp(amax)[1] - 1 + 127, 0) - down, 1)
    scale = np.exp2(byte - 127.0)
    codes = (blocks / scale).astype(np.float32).astype(dtype).astype(np.float64)
    return np.moveaxis((codes * scale).reshape(v.shape), -1, axis)


WIDE = False


def mx_kscale(k):
    if not WIDE:
        return np.ones(k)
    levels = np.array([18, -18])
    if k % 512:
        return np.exp2(np.random.permutation(np.resize(levels, k // 32))).repeat(32)
    a = np.empty((k // 512, 16))
    for p in range(k // 512):
        a[p, :8] = np.random.permutation(np.resize(levels, 8))
        for g in range(8):
            far = levels[np.abs(levels - a[p, g]) >= 10]
            a[p, g + 8] = far[np.random.randint(len(far))]
    return np.exp2(a.ravel()).repeat(32)


def f64(x):
    return np.asarray(x).astype(np.float64)


def striped(idx):
    return np.tile(np.asarray(idx).reshape(-1, 16).T, (8, 1)).astype(np.uint16)


def unstriped(offs):
    return offs[:16].T.reshape(-1).astype(np.int64)

def planes(y):
    n, m = y.shape
    v = y.astype(np.float32).astype(ml_dtypes.bfloat16).astype(np.float64).reshape(n // 32, 32, m)
    top = np.abs(v).max(1)
    byte = np.clip(np.where(top > 0, np.frexp(top)[1] - 1 + 127 - 7, 1), 1, 254)
    codes = (v * np.exp2(127.0 - byte)[:, None, :]).reshape(n, m).astype(np.float32).astype(ml_dtypes.float8_e4m3fn).view(np.uint8)
    words = codes.reshape(n // 512, 128, 4, m).transpose(0, 1, 3, 2)
    return np.ascontiguousarray(words), np.ascontiguousarray(byte.astype(np.uint8).reshape(n // 512, 16, m))


def sig(x):
    return 1.0 / (1.0 + np.exp(-x))


def setup_inputs():
    n = np.random.standard_normal
    uni = np.random.uniform
    idx = np.random.permutation(2048)[:512]
    f_d = mx_kscale(512)
    f_e = mx_kscale(512)
    f_i = np.ones(2048)
    f_i[idx] = mx_kscale(512)
    return {
        "xT": (n((512, 512)) * f_d[:, None]).astype(np.float32),
        "wg": (n((512, 2048)) / np.sqrt(512) / f_d[:, None] * f_i[None, :]).astype(np.float32),
        "wu": (n((512, 2048)) / np.sqrt(512) / f_d[:, None] * f_i[None, :]).astype(np.float32),
        "dyT": (n((512, 512)) * f_e[:, None]).astype(np.float32),
        "wd": (n((512, 2048)) / np.sqrt(512) / f_e[:, None]).astype(np.float32),
        "us": (uni(0.75, 1.3, (512, 1))).astype(np.float32),
        "tg": np.tile(uni(0.75, 1.3, 2048) / f_i, (128, 1)).astype(np.float32),
        "tu": np.tile(uni(0.75, 1.3, 2048) / f_i, (128, 1)).astype(np.float32),
        "wt": (uni(0.75, 1.3, (512, 1)) / np.sqrt(512)).astype(np.float32),
        "offs": striped(idx),
    }


def reference(xT, wg, wu, dyT, wd, us, tg, tu, wt, offs):
    idx = unstriped(offs)
    wg_i = f64(wg)[:, idx]
    wu_i = f64(wu)[:, idx]
    wd_i = f64(wd)[:, idx]
    tg_i = f64(tg)[:1][:, idx]
    tu_i = f64(tu)[:1][:, idx]
    q_xT = mxq(f64(xT), 0, "e4m3")
    ag = q_xT.T @ mxq(wg_i, 0, "e4m3")
    au = q_xT.T @ mxq(wu_i, 0, "e4m3")
    z = f64(us) * tg_i * ag
    b = f64(us) * tu_i * au
    dh = mxq(f64(dyT), 0, "e5m2").T @ mxq(wd_i, 0, "e4m3")
    s = sig(z)
    dg = f64(wt) * f64(us) * tg_i * dh * b * s * (1.0 + z * (1.0 - s))
    du = f64(wt) * f64(us) * tu_i * dh * z * s
    x1 = mxq(dg, 1, "e5m2") @ mxq(wg_i, 1, "e4m3").T
    x2 = mxq(du, 1, "e5m2") @ mxq(wu_i, 1, "e4m3").T
    out_0 = x1 + x2
    return (out_0,) + planes(out_0)

@@ -1,0 +1,286 @@
+from contextlib import ExitStack
+
+import concourse.mybir as mybir
+from concourse.masks import make_identity
+
+F32 = mybir.dt.float32
+BF16 = mybir.dt.bfloat16
+I32 = mybir.dt.int32
+U32 = mybir.dt.uint32
+U16 = mybir.dt.uint16
+U8 = mybir.dt.uint8
+E4 = mybir.dt.float8_e4m3fn_x4
+E5 = mybir.dt.float8_e5m2_x4
+ACT = mybir.ActivationFunctionType
+ALU = mybir.AluOpType
+
+P = 128
+N = 512
+T = 2048
+FLOPS = 5 * 2 * 512 * 512 * 512
+
+F_ENG = "v"
+K_ENG = "v"
+WD23_ENG = "v"
+
+
+def tile_attend_gglu_x_pl_kernel(tc, xT, wg, wu, dyT, wd, us, tg, tu, wt, offs, out_0, out_1, out_2):
+    nc = tc.nc
+    with ExitStack() as ctx:
+        sb = ctx.enter_context(tc.tile_pool(name="sb", bufs=1))
+        ps = ctx.enter_context(tc.psum_pool(name="ps", bufs=1))
+
+        def tile(name, shape, dtype, tag=None):
+            return sb.tile(shape, dtype, name=name, tag=tag or name, align_bytes=64)
+
+        def bank(b):
+            return ps.tile([P, N], F32, name="bank%d" % b)
+
+        def move(eng, out, in_):
+            if eng == "v":
+                nc.vector.tensor_copy(out=out, in_=in_)
+            else:
+                nc.scalar.copy(out=out, in_=in_)
+
+        def quantise(name, src, width, fmt):
+            codes = tile(name + "_codes", [P, width], U32)
+            scales = tile(name + "_scales", [P, width], U8)
+            nc.vector.quantize_mx(out=codes[:].bitcast(fmt), scales=scales[:], in_=src)
+            return codes, scales, fmt
+
+        def mm(out, lhs, cols, rhs, start=True, stop=True):
+            nc.tensor.matmul_mx(out=out, lhsT=lhs[0][:, cols].bitcast(lhs[2]), lhsT_scale=lhs[1][:, cols],
+                                rhs=rhs[0][:].bitcast(rhs[2]), rhs_scale=rhs[1][:], start=start, stop=stop)
+
+        def blk(k):
+            return slice(P * k, P * (k + 1))
+
+        offsets = sb.tile([P, N // 16], U16, name="offsets")
+        tg_win = tile("tg_win", [P, T], F32)
+        tu_win = tile("tu_win", [P, T], F32)
+        nc.vector.memset(tg_win[0:127, :], 0.0)
+        nc.vector.memset(tu_win[0:127, :], 0.0)
+        ident = tile("ident", [P, P], F32)
+        make_identity(nc, ident[:])
+        warm = tile("warm", [P, 8], F32)
+        nc.scalar.activation(out=warm[:], in_=ident[:, 0:8], func=ACT.Sigmoid)
+
+        x_raw = tile("x_raw", [P, 4, N], F32)
+        dy_raw = tile("dy_raw", [P, 4, N], F32)
+        us_c = tile("us_c", [P, 4], F32)
+        wt_c = tile("wt_c", [P, 4], F32)
+
+        def load_planes(name, w, tags):
+            wins = []
+            for t in range(4):
+                win = tile("%s_win%d" % (name, t), [P, T], F32, tags + str(t))
+                nc.sync.dma_start(out=win[:], in_=w.rearrange("(p t) c -> p t c", t=4)[:, t, :])
+                wins.append(win)
+            return wins
+
+        nc.sync.dma_start(out=x_raw[:], in_=xT.rearrange("(p j) r -> p j r", j=4))
+        nc.sync.dma_start(offsets[:], offs)
+        nc.sync.dma_start(out=tg_win[127:128, :], in_=tg[127:128, :])
+        nc.sync.dma_start(out=tu_win[127:128, :], in_=tu[127:128, :])
+        wg_win = load_planes("wg", wg, "a")
+        nc.sync.dma_start(out=us_c[:], in_=us.rearrange("(m t) o -> m (t o)", t=4))
+        nc.sync.dma_start(out=wt_c[:], in_=wt.rearrange("(m t) o -> m (t o)", t=4))
+        nc.sync.dma_start(out=dy_raw[:], in_=dyT.rearrange("(p j) r -> p j r", j=4))
+        wd_win = load_planes("wd", wd, "b")
+
+        def gather_plane(pair, win, e):
+            nc.vector.tensor_copy(out=pair[:, e, :], in_=win[:].indirect(offsets[:]))
+
+        def weave_pair(eng, woven, pair, h):
+            move(eng, woven[:, :, 2 * h : 2 * h + 2].rearrange("p (c i) t -> p c t i", i=4),
+                 pair[:].rearrange("p t (c i) -> p c t i", i=4))
+
+        def turn_pair(b, turned, pair, h):
+            acc = bank(b)
+            words = pair[:].rearrange("p t c -> p (t c)").bitcast(F32)
+            for e in range(2):
+                for u in range(2):
+                    nc.tensor.transpose(acc[:, blk(2 * e + u)], words[:, 256 * e + u : 256 * (e + 1) : 2], ident[:])
+            dst = turned[:].bitcast(F32).rearrange("q (p t u) -> q p t u", t=4, u=2)[:, :, 2 * h : 2 * h + 2, :]
+            nc.scalar.copy(out=dst, in_=acc[:].rearrange("q (e u p) -> q p e u", e=2, u=2))
+
+        def flat(t3):
+            return t3[:].rearrange("p c t -> p (c t)")
+
+        def deal(woven, raw):
+            nc.scalar.copy(out=woven[:].rearrange("p (t m) j -> p m j t", t=4), in_=raw[:].rearrange("p j (m t) -> p m j t", t=4))
+
+        x_woven = tile("x_woven", [P, N, 4], BF16, "hold_x")
+        deal(x_woven, x_raw)
+
+        cols = {}
+        for name, win, b in (("tg", tg_win, 0), ("tu", tu_win, 1)):
+            row = tile(name + "_row", [P, N], F32)
+            nc.vector.tensor_copy(out=row[:], in_=win[:].indirect(offsets[:]))
+            acc = bank(b)
+            for k in range(4):
+                nc.tensor.transpose(acc[:, blk(k)], row[:, blk(k)], ident[:])
+            col = tile(name + "_col", [P, 4], F32)
+            nc.scalar.copy(out=col[:], in_=acc[:, P - 1 : N : P])
+            cols[name] = col
+
+        def spread(name, col, b, tag):
+            acc = bank(b)
+            for k in range(4):
+                nc.tensor.transpose(acc[:, blk(k)], col[:, k : k + 1].to_broadcast([P, P]), ident[:])
+            full = tile(name, [P, N], F32, tag)
+            nc.scalar.copy(out=full[:], in_=acc[:])
+            return full
+
+        wg_pairs = [tile("wg_pair0", [P, 2, N], BF16)]
+        wg_woven = tile("wg_woven", [P, N, 4], BF16)
+        wg_turned = tile("wg_turned", [P, 4 * N], BF16)
+        gather_plane(wg_pairs[0], wg_win[0], 0)
+        xq = quantise("x", flat(x_woven), N, E4)
+        tgtu = tile("tgtu", [P, 4], F32)
+        nc.vector.tensor_tensor(out=tgtu[:], in0=cols["tg"][:], in1=cols["tu"][:], op=ALU.mult)
+        gather_plane(wg_pairs[0], wg_win[1], 1)
+        tg_full = spread("tg_full", cols["tg"], 2, "hold_z")
+        tgtu_full = spread("tgtu_full", tgtu, 3, "hold_f")
+        weave_pair("s", wg_woven, wg_pairs[0], 0)
+        turn_pair(4, wg_turned, wg_pairs[0], 0)
+        wg_pairs.append(tile("wg_pair1", [P, 2, N], BF16, "hold_x"))
+        gather_plane(wg_pairs[1], wg_win[2], 0)
+        gather_plane(wg_pairs[1], wg_win[3], 1)
+        weave_pair("v", wg_woven, wg_pairs[1], 1)
+        wgq = quantise("wg", flat(wg_woven), N, E4)
+        wu_win = load_planes("wu", wu, "a")
+
+        c1 = tile("c1", [P, 4], F32)
+        c2 = tile("c2", [P, 4], F32, "hold_p")
+        nc.gpsimd.tensor_tensor(out=c1[:], in0=us_c[:], in1=wt_c[:], op=ALU.mult)
+        nc.gpsimd.tensor_tensor(out=c2[:], in0=c1[:], in1=us_c[:], op=ALU.mult)
+
+        ag = []
+        z = [tile("z%d" % t, [P, N], F32) for t in range(4)]
+        for t in range(4):
+            acc = bank(t)
+            mm(acc[:], xq, blk(t), wgq)
+            ag.append(acc)
+            nc.vector.scalar_tensor_tensor(out=z[t][:], in0=acc[:], scalar=us_c[:, t : t + 1], in1=tg_full[:], op0=ALU.mult, op1=ALU.mult)
+        turn_pair(5, wg_turned, wg_pairs[1], 1)
+
+        dy_woven = tile("dy_woven", [P, N, 4], BF16, "hold_x")
+        deal(dy_woven, dy_raw)
+        s = [tile("s%d" % t, [P, N], F32) for t in range(4)]
+        for t in range(4):
+            nc.scalar.activation(out=s[t][:], in_=z[t][:], func=ACT.Sigmoid)
+
+        wd_pairs = [tile("wd_pair0", [P, 2, N], BF16, "hold_z")]
+        wd_woven = tile("wd_woven", [P, N, 4], BF16, "hold_w")
+        gather_plane(wd_pairs[0], wd_win[0], 0)
+        wgtq = quantise("wgt", wg_turned[:], N, E4)
+        dyq = quantise("dy", flat(dy_woven), N, E5)
+        gather_plane(wd_pairs[0], wd_win[1], 1)
+        weave_pair("s", wd_woven, wd_pairs[0], 0)
+
+        g_all = tile("g_all", [P, 4, N], F32, "hold_z")
+        g = [g_all[:, t, :] for t in range(4)]
+        for t in range(4):
+            nc.scalar.activation(out=g[t], in_=z[t][:], func=ACT.Silu, scale=-1.0)
+        if K_ENG == "g":
+            g1 = [tile("g1_%d" % t, [P, N], F32, "z%d" % t) for t in range(4)]
+            for t in range(4):
+                nc.scalar.activation(out=g1[t][:], in_=g[t], func=ACT.Copy, bias=-1.0)
+
+        f = [tile("f%d" % t, [P, N], F32) for t in range(4)]
+        for t in range(4):
+            eng = nc.vector if F_ENG == "v" else nc.gpsimd
+            eng.tensor_tensor(out=f[t][:], in0=s[t][:], in1=tgtu_full[:], op=ALU.mult)
+
+        wd_pairs.append(tile("wd_pair1", [P, 2, N], BF16, "hold_f"))
+        gather_plane(wd_pairs[1], wd_win[2], 0)
+        gather_plane(wd_pairs[1], wd_win[3], 1)
+        weave_pair(WD23_ENG, wd_woven, wd_pairs[1], 1)
+        wdq = quantise("wd", flat(wd_woven), N, E4)
+        wu_pairs = [tile("wu_pair0", [P, 2, N], BF16, "hold_w")]
+        wu_woven = tile("wu_woven", [P, N, 4], BF16)
+        wu_turned = tile("wu_turned", [P, 4 * N], BF16)
+        pp = [tile("pp%d" % t, [P, N], F32, "s%d" % t) for t in range(4)]
+        for t in range(4):
+            acc = bank(4 + t)
+            mm(acc[:], dyq, blk(t), wdq)
+            nc.vector.scalar_tensor_tensor(out=pp[t][:], in0=acc[:], scalar=c2[:, t : t + 1], in1=f[t][:], op0=ALU.mult, op1=ALU.mult)
+
+        gather_plane(wu_pairs[0], wu_win[0], 0)
+        gather_plane(wu_pairs[0], wu_win[1], 1)
+        weave_pair("s", wu_woven, wu_pairs[0], 0)
+        turn_pair(4, wu_turned, wu_pairs[0], 0)
+        wu_pairs.append(tile("wu_pair1", [P, 2, N], BF16, "hold_p"))
+        gather_plane(wu_pairs[1], wu_win[2], 0)
+        gather_plane(wu_pairs[1], wu_win[3], 1)
+        weave_pair("s", wu_woven, wu_pairs[1], 1)
+        wuq = quantise("wu", flat(wu_woven), N, E4)
+        turn_pair(5, wu_turned, wu_pairs[1], 1)
+        wutq = quantise("wut", wu_turned[:], N, E4)
+        def turn_grad(name, grad, b):
+            acc = bank(b)
+            words = grad[:].bitcast(F32)
+            for u in range(2):
+                nc.tensor.transpose(acc[:, blk(u)], words[:, u:256:2], ident[:])
+            turned = tile(name + "_turned", [P, N], BF16)
+            nc.scalar.copy(out=turned[:].bitcast(F32).rearrange("q (m u) -> q m u", u=2),
+                           in_=acc[:, 0:256].rearrange("q (u m) -> q m u", u=2))
+            return turned
+
+        res = [tile("res%d" % h, [P, 2, N], F32) for h in range(2)]
+        res_woven = tile("res_woven", [P, N, 4], BF16)
+        rows = out_0.rearrange("(m t) d -> m t d", t=4)
+        fk = [tile("fk%d" % t, [P, N], F32, "f%d" % t) for t in range(4)]
+        du_turned, dg_turned, duq = [], [], []
+
+        def up_side(t):
+            du = tile("du%d" % t, [P, N], BF16)
+            nc.vector.tensor_tensor(out=du[:], in0=ag[t][:], in1=pp[t][:], op=ALU.mult)
+            du_turned.append(turn_grad("du%d" % t, du, 6 + t % 2))
+            if K_ENG == "v":
+                nc.vector.scalar_tensor_tensor(out=fk[t][:], in0=g[t], scalar=-1.0, in1=pp[t][:], op0=ALU.add, op1=ALU.mult)
+            else:
+                nc.gpsimd.tensor_tensor(out=fk[t][:], in0=g1[t][:], in1=pp[t][:], op=ALU.mult)
+
+        def gate_side(t):
+            acc = bank(t)
+            mm(acc[:], xq, blk(t), wuq)
+            dg = tile("dg%d" % t, [P, N], BF16)
+            nc.vector.scalar_tensor_tensor(out=dg[:], in0=acc[:], scalar=-1.0, in1=fk[t][:], op0=ALU.mult, op1=ALU.mult)
+            dg_turned.append(turn_grad("dg%d" % t, dg, 6 + t % 2))
+            duq.append(quantise("du%d" % t, du_turned[t][:], P, E5))
+
+        def finish(t):
+            dgq = quantise("dg%d" % t, dg_turned[t][:], P, E5)
+            acc = bank(t)
+            mm(acc[:], duq[t], blk(0), wutq, True, False)
+            mm(acc[:], dgq, blk(0), wgtq, False, True)
+            nc.scalar.copy(out=res[t // 2][:, t % 2, :], in_=acc[:])
+            nc.sync.dma_start(out=rows[:, t, :], in_=res[t // 2][:, t % 2, :])
+
+        for t in range(4):
+            up_side(t)
+        for step in range(5):
+            if step < 4:
+                gate_side(step)
+            if step > 0:
+                finish(step - 1)
+
+        weave_pair("s", res_woven, res[0], 0)
+        codes = tile("res_codes", [P, N], U32)
+        scales = tile("res_scales", [P, N], U8)
+        words_out = out_1[0].rearrange("p c l -> p (c l)").bitcast(I32)
+        H = N // 2
+        for a in range(2):
+            c = slice(a * H, (a + 1) * H)
+            nc.vector.tensor_copy(out=res_woven[:, c, 2:4].rearrange("p (c i) t -> p c t i", i=4),
+                                  in_=res[1][:, :, c].rearrange("p t (c i) -> p c t i", i=4))
+        for a in range(2):
+            c = slice(a * H, (a + 1) * H)
+            nc.vector.quantize_mx(out=codes[:, c].bitcast(E4), scales=scales[:, c], in_=res_woven[:, c, :].rearrange("p c t -> p (c t)"))
+            nc.sync.dma_start(out=words_out[:, c], in_=codes[:, c].bitcast(I32))
+        scales_out = out_2[0].bitcast(I32)
+        for q in range(4):
+            eng = nc.scalar if q % 2 else nc.sync
+            eng.dma_start(out=scales_out[4 * q : 4 * q + 4, :], in_=scales[32 * q : 32 * q + 4, :].bitcast(I32))

@@ -19,9 +19,9 @@ N = 512
 T = 2048
 FLOPS = 5 * 2 * 512 * 512 * 512
 
-F_ENG = "v"
-K_ENG = "v"
-WD23_ENG = "v"
+F_ENG = "g"
+K_ENG = "g"
+WD23_ENG = "s"
 
 
 def tile_attend_gglu_x_pl_kernel(tc, xT, wg, wu, dyT, wd, us, tg, tu, wt, offs, out_0, out_1, out_2):
@@ -193,7 +193,7 @@ def tile_attend_gglu_x_pl_kernel(tc, xT, wg, wu, dyT, wd, us, tg, tu, wt, offs, 
             eng = nc.vector if F_ENG == "v" else nc.gpsimd
             eng.tensor_tensor(out=f[t][:], in0=s[t][:], in1=tgtu_full[:], op=ALU.mult)
 
-        wd_pairs.append(tile("wd_pair1", [P, 2, N], BF16, "hold_f"))
+        wd_pairs.append(tile("wd_pair1", [P, 2, N], BF16, "hold_x"))
         gather_plane(wd_pairs[1], wd_win[2], 0)
         gather_plane(wd_pairs[1], wd_win[3], 1)
         weave_pair(WD23_ENG, wd_woven, wd_pairs[1], 1)

@@ -9,23 +9,23 @@ I32 = mybir.dt.int32
 U32 = mybir.dt.uint32
 U16 = mybir.dt.uint16
 U8 = mybir.dt.uint8
-E4 = mybir.dt.float8_e4m3fn_x4
-E5 = mybir.dt.float8_e5m2_x4
+E4M3 = mybir.dt.float8_e4m3fn_x4
+E5M2 = mybir.dt.float8_e5m2_x4
 ACT = mybir.ActivationFunctionType
 ALU = mybir.AluOpType
 
 P = 128
-N = 512
-T = 2048
-FLOPS = 5 * 2 * 512 * 512 * 512
-
-F_ENG = "g"
-K_ENG = "g"
-WD23_ENG = "s"
+LANES = 4
+N = P * LANES
+UNITS = 2048
+WORDS = N // 2
+RUN = 4
+FLOPS = 5 * 2 * N * N * N
 
 
 def tile_attend_gglu_x_pl_kernel(tc, xT, wg, wu, dyT, wd, us, tg, tu, wt, offs, out_0, out_1, out_2):
     nc = tc.nc
+    on_vector, on_scalar = nc.vector.tensor_copy, nc.scalar.copy
     with ExitStack() as ctx:
         sb = ctx.enter_context(tc.tile_pool(name="sb", bufs=1))
         ps = ctx.enter_context(tc.psum_pool(name="ps", bufs=1))
@@ -36,251 +36,240 @@ def tile_attend_gglu_x_pl_kernel(tc, xT, wg, wu, dyT, wd, us, tg, tu, wt, offs, 
         def bank(b):
             return ps.tile([P, N], F32, name="bank%d" % b)
 
-        def move(eng, out, in_):
-            if eng == "v":
-                nc.vector.tensor_copy(out=out, in_=in_)
-            else:
-                nc.scalar.copy(out=out, in_=in_)
-
-        def quantise(name, src, width, fmt):
-            codes = tile(name + "_codes", [P, width], U32)
-            scales = tile(name + "_scales", [P, width], U8)
-            nc.vector.quantize_mx(out=codes[:].bitcast(fmt), scales=scales[:], in_=src)
-            return codes, scales, fmt
-
-        def mm(out, lhs, cols, rhs, start=True, stop=True):
-            nc.tensor.matmul_mx(out=out, lhsT=lhs[0][:, cols].bitcast(lhs[2]), lhsT_scale=lhs[1][:, cols],
-                                rhs=rhs[0][:].bitcast(rhs[2]), rhs_scale=rhs[1][:], start=start, stop=stop)
-
-        def blk(k):
+        def block(k):
             return slice(P * k, P * (k + 1))
 
-        offsets = sb.tile([P, N // 16], U16, name="offsets")
-        tg_win = tile("tg_win", [P, T], F32)
-        tu_win = tile("tu_win", [P, T], F32)
-        nc.vector.memset(tg_win[0:127, :], 0.0)
-        nc.vector.memset(tu_win[0:127, :], 0.0)
-        ident = tile("ident", [P, P], F32)
-        make_identity(nc, ident[:])
-        warm = tile("warm", [P, 8], F32)
-        nc.scalar.activation(out=warm[:], in_=ident[:, 0:8], func=ACT.Sigmoid)
+        def flat(woven):
+            return woven[:].rearrange("p c j -> p (c j)")
 
-        x_raw = tile("x_raw", [P, 4, N], F32)
-        dy_raw = tile("dy_raw", [P, 4, N], F32)
-        us_c = tile("us_c", [P, 4], F32)
-        wt_c = tile("wt_c", [P, 4], F32)
+        def quantise(name, woven, columns, fmt, tag=None):
+            codes = tile(name + "_codes", [P, columns], U32, tag)
+            scales = tile(name + "_scales", [P, columns], U8)
+            nc.vector.quantize_mx(out=codes[:].bitcast(fmt), scales=scales[:], in_=woven)
+            return codes, scales, fmt
 
-        def load_planes(name, w, tags):
-            wins = []
-            for t in range(4):
-                win = tile("%s_win%d" % (name, t), [P, T], F32, tags + str(t))
-                nc.sync.dma_start(out=win[:], in_=w.rearrange("(p t) c -> p t c", t=4)[:, t, :])
-                wins.append(win)
-            return wins
+        def product(acc, stationary, k, moving, start=True, stop=True):
+            s_codes, s_scales, s_fmt = stationary
+            m_codes, m_scales, m_fmt = moving
+            nc.tensor.matmul_mx(out=acc[:], lhsT=s_codes[:, block(k)].bitcast(s_fmt), lhsT_scale=s_scales[:, block(k)],
+                                rhs=m_codes[:].bitcast(m_fmt), rhs_scale=m_scales[:], start=start, stop=stop)
 
-        nc.sync.dma_start(out=x_raw[:], in_=xT.rearrange("(p j) r -> p j r", j=4))
-        nc.sync.dma_start(offsets[:], offs)
-        nc.sync.dma_start(out=tg_win[127:128, :], in_=tg[127:128, :])
-        nc.sync.dma_start(out=tu_win[127:128, :], in_=tu[127:128, :])
-        wg_win = load_planes("wg", wg, "a")
-        nc.sync.dma_start(out=us_c[:], in_=us.rearrange("(m t) o -> m (t o)", t=4))
-        nc.sync.dma_start(out=wt_c[:], in_=wt.rearrange("(m t) o -> m (t o)", t=4))
-        nc.sync.dma_start(out=dy_raw[:], in_=dyT.rearrange("(p j) r -> p j r", j=4))
-        wd_win = load_planes("wd", wd, "b")
+        def load_planes(name, w, tag):
+            windows = []
+            for j in range(LANES):
+                window = tile("%s_window%d" % (name, j), [P, UNITS], F32, tag + str(j))
+                nc.sync.dma_start(out=window[:], in_=w.rearrange("(p j) c -> p j c", j=LANES)[:, j, :])
+                windows.append(window)
+            return windows
 
-        def gather_plane(pair, win, e):
-            nc.vector.tensor_copy(out=pair[:, e, :], in_=win[:].indirect(offsets[:]))
+        def gather_plane(pair, window, e):
+            nc.vector.tensor_copy(out=pair[:, e, :], in_=window[:].indirect(offsets[:]))
 
-        def weave_pair(eng, woven, pair, h):
-            move(eng, woven[:, :, 2 * h : 2 * h + 2].rearrange("p (c i) t -> p c t i", i=4),
-                 pair[:].rearrange("p t (c i) -> p c t i", i=4))
+        def weave_pair(copy, woven, pair, h, columns=slice(0, N)):
+            copy(out=woven[:, columns, 2 * h : 2 * h + 2].rearrange("p (c i) j -> p c j i", i=RUN),
+                 in_=pair[:, :, columns].rearrange("p j (c i) -> p c j i", i=RUN))
 
         def turn_pair(b, turned, pair, h):
             acc = bank(b)
-            words = pair[:].rearrange("p t c -> p (t c)").bitcast(F32)
+            words = pair[:].rearrange("p e c -> p (e c)").bitcast(F32)
             for e in range(2):
                 for u in range(2):
-                    nc.tensor.transpose(acc[:, blk(2 * e + u)], words[:, 256 * e + u : 256 * (e + 1) : 2], ident[:])
-            dst = turned[:].bitcast(F32).rearrange("q (p t u) -> q p t u", t=4, u=2)[:, :, 2 * h : 2 * h + 2, :]
-            nc.scalar.copy(out=dst, in_=acc[:].rearrange("q (e u p) -> q p e u", e=2, u=2))
+                    nc.tensor.transpose(acc[:, block(2 * e + u)], words[:, WORDS * e + u : WORDS * (e + 1) : 2], ident[:])
+            by_feature = turned[:].bitcast(F32).rearrange("q (p j u) -> q p j u", j=LANES, u=2)
+            nc.scalar.copy(out=by_feature[:, :, 2 * h : 2 * h + 2, :], in_=acc[:].rearrange("q (e u p) -> q p e u", e=2, u=2))
 
-        def flat(t3):
-            return t3[:].rearrange("p c t -> p (c t)")
-
-        def deal(woven, raw):
-            nc.scalar.copy(out=woven[:].rearrange("p (t m) j -> p m j t", t=4), in_=raw[:].rearrange("p j (m t) -> p m j t", t=4))
-
-        x_woven = tile("x_woven", [P, N, 4], BF16, "hold_x")
-        deal(x_woven, x_raw)
-
-        cols = {}
-        for name, win, b in (("tg", tg_win, 0), ("tu", tu_win, 1)):
-            row = tile(name + "_row", [P, N], F32)
-            nc.vector.tensor_copy(out=row[:], in_=win[:].indirect(offsets[:]))
-            acc = bank(b)
-            for k in range(4):
-                nc.tensor.transpose(acc[:, blk(k)], row[:, blk(k)], ident[:])
-            col = tile(name + "_col", [P, 4], F32)
-            nc.scalar.copy(out=col[:], in_=acc[:, P - 1 : N : P])
-            cols[name] = col
-
-        def spread(name, col, b, tag):
-            acc = bank(b)
-            for k in range(4):
-                nc.tensor.transpose(acc[:, blk(k)], col[:, k : k + 1].to_broadcast([P, P]), ident[:])
-            full = tile(name, [P, N], F32, tag)
-            nc.scalar.copy(out=full[:], in_=acc[:])
-            return full
-
-        wg_pairs = [tile("wg_pair0", [P, 2, N], BF16)]
-        wg_woven = tile("wg_woven", [P, N, 4], BF16)
-        wg_turned = tile("wg_turned", [P, 4 * N], BF16)
-        gather_plane(wg_pairs[0], wg_win[0], 0)
-        xq = quantise("x", flat(x_woven), N, E4)
-        tgtu = tile("tgtu", [P, 4], F32)
-        nc.vector.tensor_tensor(out=tgtu[:], in0=cols["tg"][:], in1=cols["tu"][:], op=ALU.mult)
-        gather_plane(wg_pairs[0], wg_win[1], 1)
-        tg_full = spread("tg_full", cols["tg"], 2, "hold_z")
-        tgtu_full = spread("tgtu_full", tgtu, 3, "hold_f")
-        weave_pair("s", wg_woven, wg_pairs[0], 0)
-        turn_pair(4, wg_turned, wg_pairs[0], 0)
-        wg_pairs.append(tile("wg_pair1", [P, 2, N], BF16, "hold_x"))
-        gather_plane(wg_pairs[1], wg_win[2], 0)
-        gather_plane(wg_pairs[1], wg_win[3], 1)
-        weave_pair("v", wg_woven, wg_pairs[1], 1)
-        wgq = quantise("wg", flat(wg_woven), N, E4)
-        wu_win = load_planes("wu", wu, "a")
-
-        c1 = tile("c1", [P, 4], F32)
-        c2 = tile("c2", [P, 4], F32, "hold_p")
-        nc.gpsimd.tensor_tensor(out=c1[:], in0=us_c[:], in1=wt_c[:], op=ALU.mult)
-        nc.gpsimd.tensor_tensor(out=c2[:], in0=c1[:], in1=us_c[:], op=ALU.mult)
-
-        ag = []
-        z = [tile("z%d" % t, [P, N], F32) for t in range(4)]
-        for t in range(4):
-            acc = bank(t)
-            mm(acc[:], xq, blk(t), wgq)
-            ag.append(acc)
-            nc.vector.scalar_tensor_tensor(out=z[t][:], in0=acc[:], scalar=us_c[:, t : t + 1], in1=tg_full[:], op0=ALU.mult, op1=ALU.mult)
-        turn_pair(5, wg_turned, wg_pairs[1], 1)
-
-        dy_woven = tile("dy_woven", [P, N, 4], BF16, "hold_x")
-        deal(dy_woven, dy_raw)
-        s = [tile("s%d" % t, [P, N], F32) for t in range(4)]
-        for t in range(4):
-            nc.scalar.activation(out=s[t][:], in_=z[t][:], func=ACT.Sigmoid)
-
-        wd_pairs = [tile("wd_pair0", [P, 2, N], BF16, "hold_z")]
-        wd_woven = tile("wd_woven", [P, N, 4], BF16, "hold_w")
-        gather_plane(wd_pairs[0], wd_win[0], 0)
-        wgtq = quantise("wgt", wg_turned[:], N, E4)
-        dyq = quantise("dy", flat(dy_woven), N, E5)
-        gather_plane(wd_pairs[0], wd_win[1], 1)
-        weave_pair("s", wd_woven, wd_pairs[0], 0)
-
-        g_all = tile("g_all", [P, 4, N], F32, "hold_z")
-        g = [g_all[:, t, :] for t in range(4)]
-        for t in range(4):
-            nc.scalar.activation(out=g[t], in_=z[t][:], func=ACT.Silu, scale=-1.0)
-        if K_ENG == "g":
-            g1 = [tile("g1_%d" % t, [P, N], F32, "z%d" % t) for t in range(4)]
-            for t in range(4):
-                nc.scalar.activation(out=g1[t][:], in_=g[t], func=ACT.Copy, bias=-1.0)
-
-        f = [tile("f%d" % t, [P, N], F32) for t in range(4)]
-        for t in range(4):
-            eng = nc.vector if F_ENG == "v" else nc.gpsimd
-            eng.tensor_tensor(out=f[t][:], in0=s[t][:], in1=tgtu_full[:], op=ALU.mult)
-
-        wd_pairs.append(tile("wd_pair1", [P, 2, N], BF16, "hold_x"))
-        gather_plane(wd_pairs[1], wd_win[2], 0)
-        gather_plane(wd_pairs[1], wd_win[3], 1)
-        weave_pair(WD23_ENG, wd_woven, wd_pairs[1], 1)
-        wdq = quantise("wd", flat(wd_woven), N, E4)
-        wu_pairs = [tile("wu_pair0", [P, 2, N], BF16, "hold_w")]
-        wu_woven = tile("wu_woven", [P, N, 4], BF16)
-        wu_turned = tile("wu_turned", [P, 4 * N], BF16)
-        pp = [tile("pp%d" % t, [P, N], F32, "s%d" % t) for t in range(4)]
-        for t in range(4):
-            acc = bank(4 + t)
-            mm(acc[:], dyq, blk(t), wdq)
-            nc.vector.scalar_tensor_tensor(out=pp[t][:], in0=acc[:], scalar=c2[:, t : t + 1], in1=f[t][:], op0=ALU.mult, op1=ALU.mult)
-
-        gather_plane(wu_pairs[0], wu_win[0], 0)
-        gather_plane(wu_pairs[0], wu_win[1], 1)
-        weave_pair("s", wu_woven, wu_pairs[0], 0)
-        turn_pair(4, wu_turned, wu_pairs[0], 0)
-        wu_pairs.append(tile("wu_pair1", [P, 2, N], BF16, "hold_p"))
-        gather_plane(wu_pairs[1], wu_win[2], 0)
-        gather_plane(wu_pairs[1], wu_win[3], 1)
-        weave_pair("s", wu_woven, wu_pairs[1], 1)
-        wuq = quantise("wu", flat(wu_woven), N, E4)
-        turn_pair(5, wu_turned, wu_pairs[1], 1)
-        wutq = quantise("wut", wu_turned[:], N, E4)
-        def turn_grad(name, grad, b):
+        def turn_gradient(name, grad, b):
             acc = bank(b)
             words = grad[:].bitcast(F32)
             for u in range(2):
-                nc.tensor.transpose(acc[:, blk(u)], words[:, u:256:2], ident[:])
+                nc.tensor.transpose(acc[:, block(u)], words[:, u:WORDS:2], ident[:])
             turned = tile(name + "_turned", [P, N], BF16)
             nc.scalar.copy(out=turned[:].bitcast(F32).rearrange("q (m u) -> q m u", u=2),
-                           in_=acc[:, 0:256].rearrange("q (u m) -> q m u", u=2))
+                           in_=acc[:, 0:WORDS].rearrange("q (u m) -> q m u", u=2))
             return turned
 
-        res = [tile("res%d" % h, [P, 2, N], F32) for h in range(2)]
-        res_woven = tile("res_woven", [P, N, 4], BF16)
-        rows = out_0.rearrange("(m t) d -> m t d", t=4)
-        fk = [tile("fk%d" % t, [P, N], F32, "f%d" % t) for t in range(4)]
-        du_turned, dg_turned, duq = [], [], []
+        def weave_by_row_tile(woven, raw):
+            nc.scalar.copy(out=woven[:].rearrange("p (t m) j -> p m j t", t=LANES),
+                           in_=raw[:].rearrange("p j (m t) -> p m j t", t=LANES))
 
-        def up_side(t):
+        def spread(name, columns, b):
+            acc = bank(b)
+            for k in range(LANES):
+                nc.tensor.transpose(acc[:, block(k)], columns[:, k : k + 1].to_broadcast([P, P]), ident[:])
+            full = tile(name, [P, N], F32)
+            nc.scalar.copy(out=full[:], in_=acc[:])
+            return full
+
+        offsets = sb.tile([P, N // 16], U16, name="offsets")
+        tg_window = tile("tg_window", [P, UNITS], F32)
+        tu_window = tile("tu_window", [P, UNITS], F32)
+        nc.vector.memset(tg_window[0 : P - 1, :], 0.0)
+        nc.vector.memset(tu_window[0 : P - 1, :], 0.0)
+        ident = tile("ident", [P, P], F32)
+        make_identity(nc, ident[:])
+
+        x_raw = tile("x_raw", [P, LANES, N], F32)
+        dy_raw = tile("dy_raw", [P, LANES, N], F32)
+        us_rows = tile("us_rows", [P, LANES], F32)
+        wt_rows = tile("wt_rows", [P, LANES], F32)
+
+        nc.sync.dma_start(out=x_raw[:], in_=xT.rearrange("(p j) r -> p j r", j=LANES))
+        nc.sync.dma_start(offsets[:], offs)
+        nc.sync.dma_start(out=tg_window[P - 1 : P, :], in_=tg[P - 1 : P, :])
+        nc.sync.dma_start(out=tu_window[P - 1 : P, :], in_=tu[P - 1 : P, :])
+        wg_window = load_planes("wg", wg, "gate_up")
+        nc.sync.dma_start(out=us_rows[:], in_=us.rearrange("(m t) o -> m (t o)", t=LANES))
+        nc.sync.dma_start(out=wt_rows[:], in_=wt.rearrange("(m t) o -> m (t o)", t=LANES))
+        nc.sync.dma_start(out=dy_raw[:], in_=dyT.rearrange("(p j) r -> p j r", j=LANES))
+        wd_window = load_planes("wd", wd, "down")
+
+        x_woven = tile("x_woven", [P, N, LANES], BF16, "x_wg_dy")
+        weave_by_row_tile(x_woven, x_raw)
+
+        listed = {}
+        for name, window, b in (("tg", tg_window, 0), ("tu", tu_window, 1)):
+            row = tile(name + "_row", [P, N], F32)
+            nc.vector.tensor_copy(out=row[:], in_=window[:].indirect(offsets[:]))
+            acc = bank(b)
+            for k in range(LANES):
+                nc.tensor.transpose(acc[:, block(k)], row[:, block(k)], ident[:])
+            listed[name] = tile(name + "_columns", [P, LANES], F32)
+            nc.scalar.copy(out=listed[name][:], in_=acc[:, P - 1 : N : P])
+
+        wg_low = tile("wg_low", [P, 2, N], BF16)
+        wg_woven = tile("wg_woven", [P, N, LANES], BF16)
+        wg_turned = tile("wg_turned", [P, LANES * N], BF16)
+        gather_plane(wg_low, wg_window[0], 0)
+        x_q = quantise("x", flat(x_woven), N, E4M3)
+        tgtu = tile("tgtu", [P, LANES], F32)
+        nc.vector.tensor_tensor(out=tgtu[:], in0=listed["tg"][:], in1=listed["tu"][:], op=ALU.mult)
+        gather_plane(wg_low, wg_window[1], 1)
+        tg_full = spread("tg_full", listed["tg"], 2)
+        tgtu_full = spread("tgtu_full", tgtu, 3)
+        weave_pair(on_scalar, wg_woven, wg_low, 0)
+        turn_pair(4, wg_turned, wg_low, 0)
+        wg_high = tile("wg_high", [P, 2, N], BF16, "x_wg_dy")
+        gather_plane(wg_high, wg_window[2], 0)
+        gather_plane(wg_high, wg_window[3], 1)
+        weave_pair(on_vector, wg_woven, wg_high, 1)
+        wg_q = quantise("wg", flat(wg_woven), N, E4M3)
+        wu_window = load_planes("wu", wu, "gate_up")
+
+        wt_us = tile("wt_us", [P, LANES], F32)
+        wt_us2 = tile("wt_us2", [P, LANES], F32)
+        nc.gpsimd.tensor_tensor(out=wt_us[:], in0=us_rows[:], in1=wt_rows[:], op=ALU.mult)
+        nc.gpsimd.tensor_tensor(out=wt_us2[:], in0=wt_us[:], in1=us_rows[:], op=ALU.mult)
+
+        turn_pair(5, wg_turned, wg_high, 1)
+        ag = []
+        z = [tile("z%d" % t, [P, N], F32) for t in range(LANES)]
+        sig = [tile("sig%d" % t, [P, N], F32) for t in range(LANES)]
+        sig_tgtu = [tile("sig_tgtu%d" % t, [P, N], F32) for t in range(LANES)]
+        for t in range(LANES):
+            ag.append(bank(t))
+            product(ag[t], x_q, t, wg_q)
+            nc.vector.scalar_tensor_tensor(out=z[t][:], in0=ag[t][:], scalar=us_rows[:, t : t + 1], in1=tg_full[:],
+                                           op0=ALU.mult, op1=ALU.mult)
+            nc.scalar.activation(out=sig[t][:], in_=z[t][:], func=ACT.Sigmoid)
+            nc.gpsimd.tensor_tensor(out=sig_tgtu[t][:], in0=sig[t][:], in1=tgtu_full[:], op=ALU.mult)
+
+        dy_woven = tile("dy_woven", [P, N, LANES], BF16, "x_wg_dy")
+        weave_by_row_tile(dy_woven, dy_raw)
+
+        wd_low = tile("wd_low", [P, 2, N], BF16)
+        wd_woven = tile("wd_woven", [P, N, LANES], BF16)
+        gather_plane(wd_low, wd_window[0], 0)
+        gather_plane(wd_low, wd_window[1], 1)
+        weave_pair(on_scalar, wd_woven, wd_low, 0)
+
+        wd_high = tile("wd_high", [P, 2, N], BF16, "wd_silu")
+        gather_plane(wd_high, wd_window[2], 0)
+        wg_turned_q = quantise("wg_turned", wg_turned[:], N, E4M3, "down2")
+        gather_plane(wd_high, wd_window[3], 1)
+        weave_pair(on_scalar, wd_woven, wd_high, 1)
+        dy_q = quantise("dy", flat(dy_woven), N, E5M2, "down3")
+
+        silu = tile("silu", [P, LANES, N], F32, "wd_silu")
+        silu_less_1 = [tile("silu_less_1_%d" % t, [P, N], F32, "z%d" % t) for t in range(LANES)]
+        for t in range(LANES):
+            nc.scalar.activation(out=silu[:, t, :], in_=z[t][:], func=ACT.Silu, scale=-1.0)
+            nc.scalar.activation(out=silu_less_1[t][:], in_=silu[:, t, :], func=ACT.Copy, bias=-1.0)
+
+        wu_low = tile("wu_low", [P, 2, N], BF16)
+        wu_high = tile("wu_high", [P, 2, N], BF16)
+        gather_plane(wu_low, wu_window[0], 0)
+        wd_q = quantise("wd", flat(wd_woven), N, E4M3, "gate_up0")
+        wu_woven = tile("wu_woven", [P, N, LANES], BF16)
+        wu_turned = tile("wu_turned", [P, LANES * N], BF16)
+        gather_plane(wu_low, wu_window[1], 1)
+        common = tile("common", [P, LANES, N], F32, "gate_up1")
+        gate_factor = [tile("gate_factor%d" % t, [P, N], F32) for t in range(LANES)]
+        for t in range(LANES):
+            dh = bank(LANES + t)
+            product(dh, dy_q, t, wd_q)
+            nc.vector.scalar_tensor_tensor(out=common[:, t, :], in0=dh[:], scalar=wt_us2[:, t : t + 1], in1=sig_tgtu[t][:],
+                                           op0=ALU.mult, op1=ALU.mult)
+            nc.gpsimd.tensor_tensor(out=gate_factor[t][:], in0=silu_less_1[t][:], in1=common[:, t, :], op=ALU.mult)
+
+        du_turned = []
+        for t in range(LANES):
             du = tile("du%d" % t, [P, N], BF16)
-            nc.vector.tensor_tensor(out=du[:], in0=ag[t][:], in1=pp[t][:], op=ALU.mult)
-            du_turned.append(turn_grad("du%d" % t, du, 6 + t % 2))
-            if K_ENG == "v":
-                nc.vector.scalar_tensor_tensor(out=fk[t][:], in0=g[t], scalar=-1.0, in1=pp[t][:], op0=ALU.add, op1=ALU.mult)
-            else:
-                nc.gpsimd.tensor_tensor(out=fk[t][:], in0=g1[t][:], in1=pp[t][:], op=ALU.mult)
+            nc.vector.tensor_tensor(out=du[:], in0=ag[t][:], in1=common[:, t, :], op=ALU.mult)
+            du_turned.append(turn_gradient("du%d" % t, du, 4 + t % 2))
 
-        def gate_side(t):
-            acc = bank(t)
-            mm(acc[:], xq, blk(t), wuq)
+        weave_pair(on_scalar, wu_woven, wu_low, 0)
+        turn_pair(6, wu_turned, wu_low, 0)
+        gather_plane(wu_high, wu_window[2], 0)
+        du_q = [quantise("du0", du_turned[0][:], P, E5M2, "gate_up2")]
+        gather_plane(wu_high, wu_window[3], 1)
+        weave_pair(on_vector, wu_woven, wu_high, 1)
+        wu_q = quantise("wu", flat(wu_woven), N, E4M3)
+        turn_pair(7, wu_turned, wu_high, 1)
+        du_q.append(quantise("du1", du_turned[1][:], P, E5M2, "gate_up3"))
+        du_q.append(quantise("du2", du_turned[2][:], P, E5M2, "wu_woven"))
+        wu_turned_q = quantise("wu_turned", wu_turned[:], N, E4M3)
+        du_q.append(quantise("du3", du_turned[3][:], P, E5M2, "wu_turned"))
+
+        result = [tile("result%d" % h, [P, 2, N], F32) for h in range(2)]
+        result_woven = tile("result_woven", [P, N, LANES], BF16)
+        out_rows = out_0.rearrange("(m t) d -> m t d", t=LANES)
+        sum_banks = (6, 7, 0, 1)
+        halves = [slice(0, N // 2), slice(N // 2, N)]
+        dg_turned, sums = [], []
+
+        def gate_gradient(t):
+            au = bank(t)
+            product(au, x_q, t, wu_q)
             dg = tile("dg%d" % t, [P, N], BF16)
-            nc.vector.scalar_tensor_tensor(out=dg[:], in0=acc[:], scalar=-1.0, in1=fk[t][:], op0=ALU.mult, op1=ALU.mult)
-            dg_turned.append(turn_grad("dg%d" % t, dg, 6 + t % 2))
-            duq.append(quantise("du%d" % t, du_turned[t][:], P, E5))
+            nc.vector.scalar_tensor_tensor(out=dg[:], in0=au[:], scalar=-1.0, in1=gate_factor[t][:], op0=ALU.mult, op1=ALU.mult)
+            dg_turned.append(turn_gradient("dg%d" % t, dg, 4 + t % 2))
+            sums.append(bank(sum_banks[t]))
+            product(sums[t], du_q[t], 0, wu_turned_q, start=True, stop=False)
 
         def finish(t):
-            dgq = quantise("dg%d" % t, dg_turned[t][:], P, E5)
-            acc = bank(t)
-            mm(acc[:], duq[t], blk(0), wutq, True, False)
-            mm(acc[:], dgq, blk(0), wgtq, False, True)
-            nc.scalar.copy(out=res[t // 2][:, t % 2, :], in_=acc[:])
-            nc.sync.dma_start(out=rows[:, t, :], in_=res[t // 2][:, t % 2, :])
+            dg_q = quantise("dg%d" % t, dg_turned[t][:], P, E5M2)
+            product(sums[t], dg_q, 0, wg_turned_q, start=False, stop=True)
+            for columns in halves if t == LANES - 1 else [slice(0, N)]:
+                nc.scalar.copy(out=result[t // 2][:, t % 2, columns], in_=sums[t][:, columns])
+            nc.sync.dma_start(out=out_rows[:, t, :], in_=result[t // 2][:, t % 2, :])
 
-        for t in range(4):
-            up_side(t)
-        for step in range(5):
-            if step < 4:
-                gate_side(step)
+        for step in range(LANES + 1):
+            if step < LANES:
+                gate_gradient(step)
             if step > 0:
                 finish(step - 1)
 
-        weave_pair("s", res_woven, res[0], 0)
-        codes = tile("res_codes", [P, N], U32)
-        scales = tile("res_scales", [P, N], U8)
-        words_out = out_1[0].rearrange("p c l -> p (c l)").bitcast(I32)
-        H = N // 2
-        for a in range(2):
-            c = slice(a * H, (a + 1) * H)
-            nc.vector.tensor_copy(out=res_woven[:, c, 2:4].rearrange("p (c i) t -> p c t i", i=4),
-                                  in_=res[1][:, :, c].rearrange("p t (c i) -> p c t i", i=4))
-        for a in range(2):
-            c = slice(a * H, (a + 1) * H)
-            nc.vector.quantize_mx(out=codes[:, c].bitcast(E4), scales=scales[:, c], in_=res_woven[:, c, :].rearrange("p c t -> p (c t)"))
-            nc.sync.dma_start(out=words_out[:, c], in_=codes[:, c].bitcast(I32))
-        scales_out = out_2[0].bitcast(I32)
+        weave_pair(on_vector, result_woven, result[0], 0)
+        out_codes = tile("out_codes", [P, N], U32)
+        out_scales = tile("out_scales", [P, N], U8)
+        codes_hbm = out_1[0].rearrange("p c lane -> p (c lane)").bitcast(I32)
+        for columns in halves:
+            weave_pair(on_vector, result_woven, result[1], 1, columns)
+        for columns in halves:
+            nc.vector.quantize_mx(out=out_codes[:, columns].bitcast(E4M3), scales=out_scales[:, columns],
+                                  in_=result_woven[:, columns, :].rearrange("p c j -> p (c j)"))
+            nc.sync.dma_start(out=codes_hbm[:, columns], in_=out_codes[:, columns].bitcast(I32))
+        scales_hbm = out_2[0].bitcast(I32)
         for q in range(4):
-            eng = nc.scalar if q % 2 else nc.sync
-            eng.dma_start(out=scales_out[4 * q : 4 * q + 4, :], in_=scales[32 * q : 32 * q + 4, :].bitcast(I32))
+            queue = nc.scalar if q % 2 else nc.sync
+            queue.dma_start(out=scales_hbm[4 * q : 4 * q + 4, :], in_=out_scales[32 * q : 32 * q + 4, :].bitcast(I32))

@@ -40,32 +40,43 @@ def tile_attend_gglu_x_pl_kernel(tc, xT, wg, wu, dyT, wd, us, tg, tu, wt, offs, 
             return slice(P * k, P * (k + 1))
 
         def flat(woven):
-            return woven[:].rearrange("p c j -> p (c j)")
+            return woven.rearrange("p c j -> p (c j)")
 
-        def quantise(name, woven, columns, fmt, tag=None):
-            codes = tile(name + "_codes", [P, columns], U32, tag)
-            scales = tile(name + "_scales", [P, columns], U8)
-            nc.vector.quantize_mx(out=codes[:].bitcast(fmt), scales=scales[:], in_=woven)
-            return codes, scales, fmt
+        def operand(name, fmt, tag=None):
+            return tile(name + "_codes", [P, N], U32, tag), tile(name + "_scales", [P, N], U8), fmt
 
-        def product(acc, stationary, k, moving, start=True, stop=True):
+        def quantise(q, woven, columns=slice(0, N)):
+            codes, scales, fmt = q
+            nc.vector.quantize_mx(out=codes[:, columns].bitcast(fmt), scales=scales[:, columns], in_=flat(woven[:, columns, :]))
+
+        def product(acc, stationary, k, moving, columns=slice(0, N), start=True, stop=True):
             s_codes, s_scales, s_fmt = stationary
             m_codes, m_scales, m_fmt = moving
-            nc.tensor.matmul_mx(out=acc[:], lhsT=s_codes[:, block(k)].bitcast(s_fmt), lhsT_scale=s_scales[:, block(k)],
-                                rhs=m_codes[:].bitcast(m_fmt), rhs_scale=m_scales[:], start=start, stop=stop)
+            nc.tensor.matmul_mx(out=acc, lhsT=s_codes[:, block(k)].bitcast(s_fmt), lhsT_scale=s_scales[:, block(k)],
+                                rhs=m_codes[:, columns].bitcast(m_fmt), rhs_scale=m_scales[:, columns], start=start, stop=stop)
+
+        def load_plane(name, w, tag, j):
+            window = tile("%s_window%d" % (name, j), [P, UNITS], F32, tag + str(j))
+            nc.sync.dma_start(out=window[:], in_=w.rearrange("(p j) c -> p j c", j=LANES)[:, j, :])
+            return window
 
         def load_planes(name, w, tag):
-            windows = []
-            for j in range(LANES):
-                window = tile("%s_window%d" % (name, j), [P, UNITS], F32, tag + str(j))
-                nc.sync.dma_start(out=window[:], in_=w.rearrange("(p j) c -> p j c", j=LANES)[:, j, :])
-                windows.append(window)
-            return windows
+            return [load_plane(name, w, tag, j) for j in range(LANES)]
+
+        def load_rows(name, a):
+            raw = [tile("%s_raw%d" % (name, h), [P, LANES, N // 2], F32) for h in range(2)]
+            for h in range(2):
+                nc.sync.dma_start(out=raw[h][:], in_=a.rearrange("(p j) r -> p j r", j=LANES)[:, :, halves[h]])
+            return raw
 
         def gather_plane(pair, window, e):
             nc.vector.tensor_copy(out=pair[:, e, :], in_=window[:].indirect(offsets[:]))
 
-        def weave_pair(copy, woven, pair, h, columns=slice(0, N)):
+        def deal_pair(copy, woven, pair, h):
+            copy(out=woven[:, :, 2 * h : 2 * h + 2].rearrange("p (t q) j -> p q j t", t=LANES),
+                 in_=pair[:].rearrange("p j (q t) -> p q j t", t=LANES))
+
+        def weave_pair(copy, woven, pair, h, columns):
             copy(out=woven[:, columns, 2 * h : 2 * h + 2].rearrange("p (c i) j -> p c j i", i=RUN),
                  in_=pair[:, :, columns].rearrange("p j (c i) -> p c j i", i=RUN))
 
@@ -75,22 +86,13 @@ def tile_attend_gglu_x_pl_kernel(tc, xT, wg, wu, dyT, wd, us, tg, tu, wt, offs, 
             for e in range(2):
                 for u in range(2):
                     nc.tensor.transpose(acc[:, block(2 * e + u)], words[:, WORDS * e + u : WORDS * (e + 1) : 2], ident[:])
-            by_feature = turned[:].bitcast(F32).rearrange("q (p j u) -> q p j u", j=LANES, u=2)
-            nc.scalar.copy(out=by_feature[:, :, 2 * h : 2 * h + 2, :], in_=acc[:].rearrange("q (e u p) -> q p e u", e=2, u=2))
+            half = flat(turned[:, halves[h], :]).bitcast(F32).rearrange("q (e p u) -> q e p u", e=2, u=2)
+            nc.scalar.copy(out=half, in_=acc[:].rearrange("q (e u p) -> q e p u", e=2, u=2))
 
-        def turn_gradient(name, grad, b):
-            acc = bank(b)
-            words = grad[:].bitcast(F32)
-            for u in range(2):
-                nc.tensor.transpose(acc[:, block(u)], words[:, u:WORDS:2], ident[:])
-            turned = tile(name + "_turned", [P, N], BF16)
-            nc.scalar.copy(out=turned[:].bitcast(F32).rearrange("q (m u) -> q m u", u=2),
-                           in_=acc[:, 0:WORDS].rearrange("q (u m) -> q m u", u=2))
-            return turned
-
-        def weave_by_row_tile(woven, raw):
-            nc.scalar.copy(out=woven[:].rearrange("p (t m) j -> p m j t", t=LANES),
-                           in_=raw[:].rearrange("p j (m t) -> p m j t", t=LANES))
+        def deal_rows(woven, raw):
+            for h in range(2):
+                nc.scalar.copy(out=woven[:].rearrange("p (t m) j -> p m j t", t=LANES)[:, h * P // 2 : (h + 1) * P // 2, :, :],
+                               in_=raw[h][:].rearrange("p j (m t) -> p m j t", t=LANES))
 
         def spread(name, columns, b):
             acc = bank(b)
@@ -100,158 +102,194 @@ def tile_attend_gglu_x_pl_kernel(tc, xT, wg, wu, dyT, wd, us, tg, tu, wt, offs, 
             nc.scalar.copy(out=full[:], in_=acc[:])
             return full
 
+        def runs(x):
+            return x.rearrange("q (a i) -> q a i", i=RUN)
+
+        halves = [slice(0, N // 2), slice(N // 2, N)]
+
         offsets = sb.tile([P, N // 16], U16, name="offsets")
         tg_window = tile("tg_window", [P, UNITS], F32)
         tu_window = tile("tu_window", [P, UNITS], F32)
         nc.vector.memset(tg_window[0 : P - 1, :], 0.0)
-        nc.vector.memset(tu_window[0 : P - 1, :], 0.0)
         ident = tile("ident", [P, P], F32)
         make_identity(nc, ident[:])
+        nc.gpsimd.memset(tu_window[0 : P - 1, :], 0.0)
 
-        x_raw = tile("x_raw", [P, LANES, N], F32)
-        dy_raw = tile("dy_raw", [P, LANES, N], F32)
         us_rows = tile("us_rows", [P, LANES], F32)
         wt_rows = tile("wt_rows", [P, LANES], F32)
 
-        nc.sync.dma_start(out=x_raw[:], in_=xT.rearrange("(p j) r -> p j r", j=LANES))
+        wg_window = [load_plane("wg", wg, "gate_up", 0)]
         nc.sync.dma_start(offsets[:], offs)
         nc.sync.dma_start(out=tg_window[P - 1 : P, :], in_=tg[P - 1 : P, :])
         nc.sync.dma_start(out=tu_window[P - 1 : P, :], in_=tu[P - 1 : P, :])
-        wg_window = load_planes("wg", wg, "gate_up")
         nc.sync.dma_start(out=us_rows[:], in_=us.rearrange("(m t) o -> m (t o)", t=LANES))
         nc.sync.dma_start(out=wt_rows[:], in_=wt.rearrange("(m t) o -> m (t o)", t=LANES))
-        nc.sync.dma_start(out=dy_raw[:], in_=dyT.rearrange("(p j) r -> p j r", j=LANES))
+        wg_window.extend(load_plane("wg", wg, "gate_up", j) for j in range(1, LANES))
+        x_raw = load_rows("x", xT)
+        dy_raw = load_rows("dy", dyT)
         wd_window = load_planes("wd", wd, "down")
 
-        x_woven = tile("x_woven", [P, N, LANES], BF16, "x_wg_dy")
-        weave_by_row_tile(x_woven, x_raw)
-
+        wg_low = tile("wg_low", [P, 2, N], BF16)
+        gather_plane(wg_low, wg_window[0], 0)
         listed = {}
         for name, window, b in (("tg", tg_window, 0), ("tu", tu_window, 1)):
             row = tile(name + "_row", [P, N], F32)
             nc.vector.tensor_copy(out=row[:], in_=window[:].indirect(offsets[:]))
             acc = bank(b)
-            for k in range(LANES):
-                nc.tensor.transpose(acc[:, block(k)], row[:, block(k)], ident[:])
+            for t in range(LANES):
+                nc.tensor.transpose(acc[:, block(t)], row[:, t:N:LANES], ident[:])
             listed[name] = tile(name + "_columns", [P, LANES], F32)
             nc.scalar.copy(out=listed[name][:], in_=acc[:, P - 1 : N : P])
 
-        wg_low = tile("wg_low", [P, 2, N], BF16)
+        wg_high = tile("wg_high", [P, 2, N], BF16)
         wg_woven = tile("wg_woven", [P, N, LANES], BF16)
-        wg_turned = tile("wg_turned", [P, LANES * N], BF16)
-        gather_plane(wg_low, wg_window[0], 0)
-        x_q = quantise("x", flat(x_woven), N, E4M3)
+        wg_turned = tile("wg_turned", [P, N, LANES], BF16)
         tgtu = tile("tgtu", [P, LANES], F32)
         nc.vector.tensor_tensor(out=tgtu[:], in0=listed["tg"][:], in1=listed["tu"][:], op=ALU.mult)
+        less_tgtu = tile("less_tgtu", [P, LANES], F32)
+        nc.vector.tensor_scalar(out=less_tgtu[:], in0=tgtu[:], scalar1=-1.0, scalar2=None, op0=ALU.mult)
         gather_plane(wg_low, wg_window[1], 1)
-        tg_full = spread("tg_full", listed["tg"], 2)
-        tgtu_full = spread("tgtu_full", tgtu, 3)
-        weave_pair(on_scalar, wg_woven, wg_low, 0)
+        deal_pair(on_scalar, wg_woven, wg_low, 0)
         turn_pair(4, wg_turned, wg_low, 0)
-        wg_high = tile("wg_high", [P, 2, N], BF16, "x_wg_dy")
         gather_plane(wg_high, wg_window[2], 0)
         gather_plane(wg_high, wg_window[3], 1)
-        weave_pair(on_vector, wg_woven, wg_high, 1)
-        wg_q = quantise("wg", flat(wg_woven), N, E4M3)
+        deal_pair(on_vector, wg_woven, wg_high, 1)
+        wg_q = operand("wg", E4M3)
+        quantise(wg_q, wg_woven)
         wu_window = load_planes("wu", wu, "gate_up")
 
         wt_us = tile("wt_us", [P, LANES], F32)
         wt_us2 = tile("wt_us2", [P, LANES], F32)
         nc.gpsimd.tensor_tensor(out=wt_us[:], in0=us_rows[:], in1=wt_rows[:], op=ALU.mult)
         nc.gpsimd.tensor_tensor(out=wt_us2[:], in0=wt_us[:], in1=us_rows[:], op=ALU.mult)
-
+        us_full = spread("us_full", us_rows, 6)
         turn_pair(5, wg_turned, wg_high, 1)
+
+        wg_turned_q = operand("wg_turned", E4M3)
+        quantise(wg_turned_q, wg_turned)
+        x_woven = tile("x_woven", [P, N, LANES], BF16)
+        deal_rows(x_woven, x_raw)
+        x_q = operand("x", E4M3)
+        quantise(x_q, x_woven)
+
+        dy_woven = tile("dy_woven", [P, N, LANES], BF16)
+        deal_rows(dy_woven, dy_raw)
+
         ag = []
         z = [tile("z%d" % t, [P, N], F32) for t in range(LANES)]
         sig = [tile("sig%d" % t, [P, N], F32) for t in range(LANES)]
-        sig_tgtu = [tile("sig_tgtu%d" % t, [P, N], F32) for t in range(LANES)]
         for t in range(LANES):
             ag.append(bank(t))
-            product(ag[t], x_q, t, wg_q)
-            nc.vector.scalar_tensor_tensor(out=z[t][:], in0=ag[t][:], scalar=us_rows[:, t : t + 1], in1=tg_full[:],
+            product(ag[t][:], wg_q, t, x_q)
+            nc.vector.scalar_tensor_tensor(out=z[t][:], in0=ag[t][:], scalar=listed["tg"][:, t : t + 1], in1=us_full[:],
                                            op0=ALU.mult, op1=ALU.mult)
             nc.scalar.activation(out=sig[t][:], in_=z[t][:], func=ACT.Sigmoid)
-            nc.gpsimd.tensor_tensor(out=sig_tgtu[t][:], in0=sig[t][:], in1=tgtu_full[:], op=ALU.mult)
-
-        dy_woven = tile("dy_woven", [P, N, LANES], BF16, "x_wg_dy")
-        weave_by_row_tile(dy_woven, dy_raw)
 
         wd_low = tile("wd_low", [P, 2, N], BF16)
+        wd_high = tile("wd_high", [P, 2, N], BF16)
         wd_woven = tile("wd_woven", [P, N, LANES], BF16)
         gather_plane(wd_low, wd_window[0], 0)
+        dy_q = operand("dy", E5M2)
+        quantise(dy_q, dy_woven)
         gather_plane(wd_low, wd_window[1], 1)
-        weave_pair(on_scalar, wd_woven, wd_low, 0)
-
-        wd_high = tile("wd_high", [P, 2, N], BF16, "wd_silu")
+        deal_pair(on_scalar, wd_woven, wd_low, 0)
         gather_plane(wd_high, wd_window[2], 0)
-        wg_turned_q = quantise("wg_turned", wg_turned[:], N, E4M3, "down2")
-        gather_plane(wd_high, wd_window[3], 1)
-        weave_pair(on_scalar, wd_woven, wd_high, 1)
-        dy_q = quantise("dy", flat(dy_woven), N, E5M2, "down3")
 
-        silu = tile("silu", [P, LANES, N], F32, "wd_silu")
-        silu_less_1 = [tile("silu_less_1_%d" % t, [P, N], F32, "z%d" % t) for t in range(LANES)]
+        up_factor = tile("up_factor", [P, N // RUN, LANES, RUN], F32, "down2")
+        for t in range(LANES):
+            nc.vector.scalar_tensor_tensor(out=up_factor[:, :, t, :], in0=runs(ag[t][:]), scalar=tgtu[:, t : t + 1],
+                                           in1=runs(sig[t][:]), op0=ALU.mult, op1=ALU.mult)
+        gather_plane(wd_high, wd_window[3], 1)
+        deal_pair(on_vector, wd_woven, wd_high, 1)
+        wd_q = operand("wd", E4M3)
+        quantise(wd_q, wd_woven)
+
+        gate_part = tile("gate_part", [P, N // RUN, LANES, RUN], F32)
+        silu = tile("silu", [P, LANES, N], F32, "wd_low")
         for t in range(LANES):
             nc.scalar.activation(out=silu[:, t, :], in_=z[t][:], func=ACT.Silu, scale=-1.0)
-            nc.scalar.activation(out=silu_less_1[t][:], in_=silu[:, t, :], func=ACT.Copy, bias=-1.0)
+            slope = tile("slope%d" % t, [P, N], F32, "z%d" % t)
+            nc.scalar.activation(out=slope[:], in_=silu[:, t, :], func=ACT.Identity,
+                                 scale=less_tgtu[:, t : t + 1], bias=tgtu[:, t : t + 1])
+            nc.gpsimd.tensor_tensor(out=gate_part[:, :, t, :], in0=runs(slope[:]), in1=runs(sig[t][:]), op=ALU.mult)
 
         wu_low = tile("wu_low", [P, 2, N], BF16)
         wu_high = tile("wu_high", [P, 2, N], BF16)
-        gather_plane(wu_low, wu_window[0], 0)
-        wd_q = quantise("wd", flat(wd_woven), N, E4M3, "gate_up0")
         wu_woven = tile("wu_woven", [P, N, LANES], BF16)
-        wu_turned = tile("wu_turned", [P, LANES * N], BF16)
+        wu_turned = tile("wu_turned", [P, N, LANES], BF16)
+        dh_scaled = tile("dh_scaled", [P, N // RUN, LANES, RUN], F32, "tg_window")
+
+        def by_runs(woven, k):
+            return woven[:, block(k), :].rearrange("q (c i) t -> q c t i", i=RUN)
+
+        def groups(k):
+            return slice(k * P // RUN, (k + 1) * P // RUN)
+
+        def bank_runs(acc):
+            return acc[:].rearrange("q (t c i) -> q c t i", t=LANES, i=RUN)
+
+        dh = []
+        for k in range(LANES):
+            acc = bank(LANES + k)
+            product(acc[:], dy_q, k, wd_q)
+            rows = tile("dh_rows%d" % k, [P, N], F32)
+            nc.scalar.activation(out=rows[:], in_=acc[:], func=ACT.Copy, scale=wt_us2[:, k : k + 1])
+            dh.append(bank(k))
+            for t in range(LANES):
+                nc.tensor.transpose(dh[k][:, block(t)], rows[:, block(t)], ident[:])
+            nc.scalar.copy(out=dh_scaled[:, groups(k), :, :], in_=bank_runs(dh[k]))
+        gather_plane(wu_low, wu_window[0], 0)
         gather_plane(wu_low, wu_window[1], 1)
-        common = tile("common", [P, LANES, N], F32, "gate_up1")
-        gate_factor = [tile("gate_factor%d" % t, [P, N], F32) for t in range(LANES)]
-        for t in range(LANES):
-            dh = bank(LANES + t)
-            product(dh, dy_q, t, wd_q)
-            nc.vector.scalar_tensor_tensor(out=common[:, t, :], in0=dh[:], scalar=wt_us2[:, t : t + 1], in1=sig_tgtu[t][:],
-                                           op0=ALU.mult, op1=ALU.mult)
-            nc.gpsimd.tensor_tensor(out=gate_factor[t][:], in0=silu_less_1[t][:], in1=common[:, t, :], op=ALU.mult)
+        gate_factor = tile("gate_factor", [P, N // RUN, LANES, RUN], F32, "gate_up1")
+        for k in range(LANES):
+            nc.vector.tensor_tensor(out=gate_factor[:, groups(k), :, :], in0=bank_runs(dh[k]), in1=gate_part[:, groups(k), :, :], op=ALU.mult)
 
-        du_turned = []
-        for t in range(LANES):
-            du = tile("du%d" % t, [P, N], BF16)
-            nc.vector.tensor_tensor(out=du[:], in0=ag[t][:], in1=common[:, t, :], op=ALU.mult)
-            du_turned.append(turn_gradient("du%d" % t, du, 4 + t % 2))
+        du = tile("du", [P, N, LANES], BF16)
+        for k in range(LANES):
+            nc.gpsimd.tensor_tensor(out=by_runs(du, k), in0=dh_scaled[:, groups(k), :, :], in1=up_factor[:, groups(k), :, :], op=ALU.mult)
 
-        weave_pair(on_scalar, wu_woven, wu_low, 0)
-        turn_pair(6, wu_turned, wu_low, 0)
+        deal_pair(on_scalar, wu_woven, wu_low, 0)
+        turn_pair(4, wu_turned, wu_low, 0)
+        wu_turned_q = operand("wu_turned", E4M3)
+        quantise(wu_turned_q, wu_turned, halves[0])
         gather_plane(wu_high, wu_window[2], 0)
-        du_q = [quantise("du0", du_turned[0][:], P, E5M2, "gate_up2")]
         gather_plane(wu_high, wu_window[3], 1)
-        weave_pair(on_vector, wu_woven, wu_high, 1)
-        wu_q = quantise("wu", flat(wu_woven), N, E4M3)
+        deal_pair(on_vector, wu_woven, wu_high, 1)
+        wu_q = operand("wu", E4M3)
+        quantise(wu_q, wu_woven)
         turn_pair(7, wu_turned, wu_high, 1)
-        du_q.append(quantise("du1", du_turned[1][:], P, E5M2, "gate_up3"))
-        du_q.append(quantise("du2", du_turned[2][:], P, E5M2, "wu_woven"))
-        wu_turned_q = quantise("wu_turned", wu_turned[:], N, E4M3)
-        du_q.append(quantise("du3", du_turned[3][:], P, E5M2, "wu_turned"))
+        du_q = operand("du", E5M2, "wu_woven")
+        quantise(du_q, du)
+        quantise(wu_turned_q, wu_turned, halves[1])
+
+        au = []
+        for k in range(LANES):
+            au.append(bank(k))
+            for t in range(LANES):
+                product(au[k][:, block(t)], wu_q, t, x_q, block(k))
+        sums = []
+        for k in range(LANES):
+            sums.append(bank(LANES + k))
+            product(sums[k][:], du_q, k, wu_turned_q, start=True, stop=False)
 
         result = [tile("result%d" % h, [P, 2, N], F32) for h in range(2)]
         result_woven = tile("result_woven", [P, N, LANES], BF16)
         out_rows = out_0.rearrange("(m t) d -> m t d", t=LANES)
-        sum_banks = (6, 7, 0, 1)
-        halves = [slice(0, N // 2), slice(N // 2, N)]
-        dg_turned, sums = [], []
+        dg = tile("dg", [P, N, LANES], BF16)
+        dg_q = operand("dg", E5M2)
 
-        def gate_gradient(t):
-            au = bank(t)
-            product(au, x_q, t, wu_q)
-            dg = tile("dg%d" % t, [P, N], BF16)
-            nc.vector.scalar_tensor_tensor(out=dg[:], in0=au[:], scalar=-1.0, in1=gate_factor[t][:], op0=ALU.mult, op1=ALU.mult)
-            dg_turned.append(turn_gradient("dg%d" % t, dg, 4 + t % 2))
-            sums.append(bank(sum_banks[t]))
-            product(sums[t], du_q[t], 0, wu_turned_q, start=True, stop=False)
+        def gate_gradient(k):
+            nc.vector.tensor_tensor(out=by_runs(dg, k), in0=bank_runs(au[k]),
+                                    in1=gate_factor[:, groups(k), :, :], op=ALU.mult)
 
-        def finish(t):
-            dg_q = quantise("dg%d" % t, dg_turned[t][:], P, E5M2)
-            product(sums[t], dg_q, 0, wg_turned_q, start=False, stop=True)
-            for columns in halves if t == LANES - 1 else [slice(0, N)]:
-                nc.scalar.copy(out=result[t // 2][:, t % 2, columns], in_=sums[t][:, columns])
-            nc.sync.dma_start(out=out_rows[:, t, :], in_=result[t // 2][:, t % 2, :])
+        def finish(k):
+            quantise(dg_q, dg, block(k))
+            product(sums[k][:], dg_q, k, wg_turned_q, start=False, stop=True)
+            by_feature = result[k // 2][:, k % 2, :].rearrange("m (p j) -> m p j", j=LANES)
+            by_plane = sums[k][:].rearrange("m (j p) -> m p j", j=LANES)
+            for rows in [slice(0, P // 2), slice(P // 2, P)] if k == LANES - 1 else [slice(0, P)]:
+                nc.scalar.copy(out=by_feature[:, rows, :], in_=by_plane[:, rows, :])
+            nc.sync.dma_start(out=out_rows[:, k, :], in_=result[k // 2][:, k % 2, :])
 
         for step in range(LANES + 1):
             if step < LANES:
@@ -259,15 +297,14 @@ def tile_attend_gglu_x_pl_kernel(tc, xT, wg, wu, dyT, wd, us, tg, tu, wt, offs, 
             if step > 0:
                 finish(step - 1)
 
-        weave_pair(on_vector, result_woven, result[0], 0)
+        weave_pair(on_vector, result_woven, result[0], 0, slice(0, N))
         out_codes = tile("out_codes", [P, N], U32)
         out_scales = tile("out_scales", [P, N], U8)
         codes_hbm = out_1[0].rearrange("p c lane -> p (c lane)").bitcast(I32)
         for columns in halves:
             weave_pair(on_vector, result_woven, result[1], 1, columns)
         for columns in halves:
-            nc.vector.quantize_mx(out=out_codes[:, columns].bitcast(E4M3), scales=out_scales[:, columns],
-                                  in_=result_woven[:, columns, :].rearrange("p c j -> p (c j)"))
+            quantise((out_codes, out_scales, E4M3), result_woven, columns)
             nc.sync.dma_start(out=codes_hbm[:, columns], in_=out_codes[:, columns].bitcast(I32))
         scales_hbm = out_2[0].bitcast(I32)
         for q in range(4):

@@ -20,6 +20,7 @@ N = P * LANES
 UNITS = 2048
 WORDS = N // 2
 RUN = 4
+SPLIT = 84
 FLOPS = 5 * 2 * N * N * N
 
 
@@ -72,26 +73,23 @@ def tile_attend_gglu_x_pl_kernel(tc, xT, wg, wu, dyT, wd, us, tg, tu, wt, offs, 
         def gather_plane(pair, window, e):
             nc.vector.tensor_copy(out=pair[:, e, :], in_=window[:].indirect(offsets[:]))
 
-        def deal_pair(copy, woven, pair, h):
-            copy(out=woven[:, :, 2 * h : 2 * h + 2].rearrange("p (t q) j -> p q j t", t=LANES),
-                 in_=pair[:].rearrange("p j (q t) -> p q j t", t=LANES))
-
-        def weave_pair(copy, woven, pair, h, columns):
-            copy(out=woven[:, columns, 2 * h : 2 * h + 2].rearrange("p (c i) j -> p c j i", i=RUN),
-                 in_=pair[:, :, columns].rearrange("p j (c i) -> p c j i", i=RUN))
+        def deal(woven, planes, split):
+            for copy, share in ((on_vector, slice(0, split)), (on_scalar, slice(split, P)))[split == 0 :]:
+                copy(out=woven[:].rearrange("p (t q) j -> p q j t", t=LANES)[:, share, :, :],
+                     in_=planes[:].rearrange("p j (q t) -> p q j t", t=LANES)[:, share, :, :])
 
         def turn_pair(b, turned, pair, h):
             acc = bank(b)
-            words = pair[:].rearrange("p e c -> p (e c)").bitcast(F32)
+            words = pair[:, 2 * h : 2 * h + 2, :].rearrange("p e c -> p (e c)").bitcast(F32)
             for e in range(2):
                 for u in range(2):
                     nc.tensor.transpose(acc[:, block(2 * e + u)], words[:, WORDS * e + u : WORDS * (e + 1) : 2], ident[:])
             half = flat(turned[:, halves[h], :]).bitcast(F32).rearrange("q (e p u) -> q e p u", e=2, u=2)
             nc.scalar.copy(out=half, in_=acc[:].rearrange("q (e u p) -> q e p u", e=2, u=2))
 
-        def deal_rows(woven, raw):
+        def deal_rows(woven, raw, copies):
             for h in range(2):
-                nc.scalar.copy(out=woven[:].rearrange("p (t m) j -> p m j t", t=LANES)[:, h * P // 2 : (h + 1) * P // 2, :, :],
+                copies[h](out=woven[:].rearrange("p (t m) j -> p m j t", t=LANES)[:, h * P // 2 : (h + 1) * P // 2, :, :],
                                in_=raw[h][:].rearrange("p j (m t) -> p m j t", t=LANES))
 
         def spread(name, columns, b):
@@ -129,8 +127,8 @@ def tile_attend_gglu_x_pl_kernel(tc, xT, wg, wu, dyT, wd, us, tg, tu, wt, offs, 
         dy_raw = load_rows("dy", dyT)
         wd_window = load_planes("wd", wd, "down")
 
-        wg_low = tile("wg_low", [P, 2, N], BF16)
-        gather_plane(wg_low, wg_window[0], 0)
+        wg_planes = tile("wg_planes", [P, LANES, N], BF16)
+        gather_plane(wg_planes, wg_window[0], 0)
         listed = {}
         for name, window, b in (("tg", tg_window, 0), ("tu", tu_window, 1)):
             row = tile(name + "_row", [P, N], F32)
@@ -141,19 +139,17 @@ def tile_attend_gglu_x_pl_kernel(tc, xT, wg, wu, dyT, wd, us, tg, tu, wt, offs, 
             listed[name] = tile(name + "_columns", [P, LANES], F32)
             nc.scalar.copy(out=listed[name][:], in_=acc[:, P - 1 : N : P])
 
-        wg_high = tile("wg_high", [P, 2, N], BF16)
         wg_woven = tile("wg_woven", [P, N, LANES], BF16)
         wg_turned = tile("wg_turned", [P, N, LANES], BF16)
         tgtu = tile("tgtu", [P, LANES], F32)
         nc.vector.tensor_tensor(out=tgtu[:], in0=listed["tg"][:], in1=listed["tu"][:], op=ALU.mult)
-        less_tgtu = tile("less_tgtu", [P, LANES], F32)
-        nc.vector.tensor_scalar(out=less_tgtu[:], in0=tgtu[:], scalar1=-1.0, scalar2=None, op0=ALU.mult)
-        gather_plane(wg_low, wg_window[1], 1)
-        deal_pair(on_scalar, wg_woven, wg_low, 0)
-        turn_pair(4, wg_turned, wg_low, 0)
-        gather_plane(wg_high, wg_window[2], 0)
-        gather_plane(wg_high, wg_window[3], 1)
-        deal_pair(on_vector, wg_woven, wg_high, 1)
+        less_tg = tile("less_tg", [P, LANES], F32)
+        nc.vector.tensor_scalar(out=less_tg[:], in0=listed["tg"][:], scalar1=-1.0, scalar2=None, op0=ALU.mult)
+        gather_plane(wg_planes, wg_window[1], 1)
+        turn_pair(4, wg_turned, wg_planes, 0)
+        gather_plane(wg_planes, wg_window[2], 2)
+        gather_plane(wg_planes, wg_window[3], 3)
+        deal(wg_woven, wg_planes, SPLIT)
         wg_q = operand("wg", E4M3)
         quantise(wg_q, wg_woven)
         wu_window = load_planes("wu", wu, "gate_up")
@@ -163,58 +159,52 @@ def tile_attend_gglu_x_pl_kernel(tc, xT, wg, wu, dyT, wd, us, tg, tu, wt, offs, 
         nc.gpsimd.tensor_tensor(out=wt_us[:], in0=us_rows[:], in1=wt_rows[:], op=ALU.mult)
         nc.gpsimd.tensor_tensor(out=wt_us2[:], in0=wt_us[:], in1=us_rows[:], op=ALU.mult)
         us_full = spread("us_full", us_rows, 6)
-        turn_pair(5, wg_turned, wg_high, 1)
+        wt_us2_full = spread("wt_us2_full", wt_us2, 7)
+        turn_pair(5, wg_turned, wg_planes, 1)
 
         wg_turned_q = operand("wg_turned", E4M3)
         quantise(wg_turned_q, wg_turned)
         x_woven = tile("x_woven", [P, N, LANES], BF16)
-        deal_rows(x_woven, x_raw)
+        deal_rows(x_woven, x_raw, (on_scalar, on_vector))
         x_q = operand("x", E4M3)
         quantise(x_q, x_woven)
 
         dy_woven = tile("dy_woven", [P, N, LANES], BF16)
-        deal_rows(dy_woven, dy_raw)
+        deal_rows(dy_woven, dy_raw, (on_scalar, on_scalar))
 
         ag = []
-        z = [tile("z%d" % t, [P, N], F32) for t in range(LANES)]
-        sig = [tile("sig%d" % t, [P, N], F32) for t in range(LANES)]
+        z = tile("z", [P, LANES, N], F32)
+        sig = tile("sig", [P, LANES, N], F32)
+        sig_row = tile("sig_row", [P, LANES, N], F32)
         for t in range(LANES):
             ag.append(bank(t))
             product(ag[t][:], wg_q, t, x_q)
-            nc.vector.scalar_tensor_tensor(out=z[t][:], in0=ag[t][:], scalar=listed["tg"][:, t : t + 1], in1=us_full[:],
-                                           op0=ALU.mult, op1=ALU.mult)
-            nc.scalar.activation(out=sig[t][:], in_=z[t][:], func=ACT.Sigmoid)
+            nc.vector.tensor_tensor(out=z[:, t, :], in0=ag[t][:], in1=us_full[:], op=ALU.mult)
+            nc.scalar.activation(out=sig[:, t, :], in_=z[:, t, :], func=ACT.Sigmoid, scale=listed["tg"][:, t : t + 1])
+            nc.gpsimd.tensor_tensor(out=sig_row[:, t, :], in0=sig[:, t, :], in1=wt_us2_full[:], op=ALU.mult)
 
-        wd_low = tile("wd_low", [P, 2, N], BF16)
-        wd_high = tile("wd_high", [P, 2, N], BF16)
+        wd_planes = tile("wd_planes", [P, LANES, N], BF16)
         wd_woven = tile("wd_woven", [P, N, LANES], BF16)
-        gather_plane(wd_low, wd_window[0], 0)
+        gather_plane(wd_planes, wd_window[0], 0)
         dy_q = operand("dy", E5M2)
         quantise(dy_q, dy_woven)
-        gather_plane(wd_low, wd_window[1], 1)
-        deal_pair(on_scalar, wd_woven, wd_low, 0)
-        gather_plane(wd_high, wd_window[2], 0)
-
-        up_factor = tile("up_factor", [P, N // RUN, LANES, RUN], F32, "down2")
+        gather_plane(wd_planes, wd_window[1], 1)
+        gather_plane(wd_planes, wd_window[2], 2)
+        gather_plane(wd_planes, wd_window[3], 3)
+        deal(wd_woven, wd_planes, 0)
+        up_factor = tile("up_factor", [P, N // RUN, LANES, RUN], F32, "down3")
         for t in range(LANES):
-            nc.vector.scalar_tensor_tensor(out=up_factor[:, :, t, :], in0=runs(ag[t][:]), scalar=tgtu[:, t : t + 1],
-                                           in1=runs(sig[t][:]), op0=ALU.mult, op1=ALU.mult)
-        gather_plane(wd_high, wd_window[3], 1)
-        deal_pair(on_vector, wd_woven, wd_high, 1)
-        wd_q = operand("wd", E4M3)
-        quantise(wd_q, wd_woven)
+            nc.vector.tensor_tensor(out=up_factor[:, :, t, :], in0=runs(ag[t][:]), in1=runs(sig_row[:, t, :]), op=ALU.mult)
 
-        gate_part = tile("gate_part", [P, N // RUN, LANES, RUN], F32)
-        silu = tile("silu", [P, LANES, N], F32, "wd_low")
+        gate_part = tile("gate_part", [P, LANES, N], F32, "tu_window")
+        silu = tile("silu", [P, LANES, N], F32, "tg_columns")
+        slope = tile("slope", [P, LANES, N], F32)
         for t in range(LANES):
-            nc.scalar.activation(out=silu[:, t, :], in_=z[t][:], func=ACT.Silu, scale=-1.0)
-            slope = tile("slope%d" % t, [P, N], F32, "z%d" % t)
-            nc.scalar.activation(out=slope[:], in_=silu[:, t, :], func=ACT.Identity,
-                                 scale=less_tgtu[:, t : t + 1], bias=tgtu[:, t : t + 1])
-            nc.gpsimd.tensor_tensor(out=gate_part[:, :, t, :], in0=runs(slope[:]), in1=runs(sig[t][:]), op=ALU.mult)
+            nc.scalar.activation(out=silu[:, t, :], in_=z[:, t, :], func=ACT.Silu, scale=less_tg[:, t : t + 1])
+            nc.scalar.activation(out=slope[:, t, :], in_=silu[:, t, :], func=ACT.Copy, scale=-1.0, bias=1.0)
+            nc.gpsimd.tensor_tensor(out=gate_part[:, t, :], in0=slope[:, t, :], in1=sig_row[:, t, :], op=ALU.mult)
 
-        wu_low = tile("wu_low", [P, 2, N], BF16)
-        wu_high = tile("wu_high", [P, 2, N], BF16)
+        wu_planes = tile("wu_planes", [P, LANES, N], BF16)
         wu_woven = tile("wu_woven", [P, N, LANES], BF16)
         wu_turned = tile("wu_turned", [P, N, LANES], BF16)
         dh_scaled = tile("dh_scaled", [P, N // RUN, LANES, RUN], F32, "tg_window")
@@ -228,38 +218,34 @@ def tile_attend_gglu_x_pl_kernel(tc, xT, wg, wu, dyT, wd, us, tg, tu, wt, offs, 
         def bank_runs(acc):
             return acc[:].rearrange("q (t c i) -> q c t i", t=LANES, i=RUN)
 
+        gather_plane(wu_planes, wu_window[0], 0)
+        wd_q = operand("wd", E4M3, "gate_up0")
+        quantise(wd_q, wd_woven)
         dh = []
-        for k in range(LANES):
-            acc = bank(LANES + k)
-            product(acc[:], dy_q, k, wd_q)
-            rows = tile("dh_rows%d" % k, [P, N], F32)
-            nc.scalar.activation(out=rows[:], in_=acc[:], func=ACT.Copy, scale=wt_us2[:, k : k + 1])
-            dh.append(bank(k))
-            for t in range(LANES):
-                nc.tensor.transpose(dh[k][:, block(t)], rows[:, block(t)], ident[:])
-            nc.scalar.copy(out=dh_scaled[:, groups(k), :, :], in_=bank_runs(dh[k]))
-        gather_plane(wu_low, wu_window[0], 0)
-        gather_plane(wu_low, wu_window[1], 1)
+        for t in range(LANES):
+            dh.append(bank(LANES + t))
+            product(dh[t][:], wd_q, t, dy_q)
+        gather_plane(wu_planes, wu_window[1], 1)
         gate_factor = tile("gate_factor", [P, N // RUN, LANES, RUN], F32, "gate_up1")
-        for k in range(LANES):
-            nc.vector.tensor_tensor(out=gate_factor[:, groups(k), :, :], in0=bank_runs(dh[k]), in1=gate_part[:, groups(k), :, :], op=ALU.mult)
+        for t in range(LANES):
+            nc.scalar.activation(out=dh_scaled[:, :, t, :], in_=runs(dh[t][:]), func=ACT.Copy, scale=tgtu[:, t : t + 1])
+            other = (t + 2) % LANES
+            nc.vector.scalar_tensor_tensor(out=gate_factor[:, :, other, :], in0=runs(dh[other][:]), scalar=tgtu[:, other : other + 1],
+                                           in1=runs(gate_part[:, other, :]), op0=ALU.mult, op1=ALU.mult)
 
-        du = tile("du", [P, N, LANES], BF16)
+        grads = tile("grads", [P, 2 * N, LANES], BF16)
         for k in range(LANES):
-            nc.gpsimd.tensor_tensor(out=by_runs(du, k), in0=dh_scaled[:, groups(k), :, :], in1=up_factor[:, groups(k), :, :], op=ALU.mult)
+            nc.gpsimd.tensor_tensor(out=by_runs(grads, 2 * k), in0=dh_scaled[:, groups(k), :, :], in1=up_factor[:, groups(k), :, :], op=ALU.mult)
 
-        deal_pair(on_scalar, wu_woven, wu_low, 0)
-        turn_pair(4, wu_turned, wu_low, 0)
+        turn_pair(0, wu_turned, wu_planes, 0)
         wu_turned_q = operand("wu_turned", E4M3)
         quantise(wu_turned_q, wu_turned, halves[0])
-        gather_plane(wu_high, wu_window[2], 0)
-        gather_plane(wu_high, wu_window[3], 1)
-        deal_pair(on_vector, wu_woven, wu_high, 1)
+        gather_plane(wu_planes, wu_window[2], 2)
+        gather_plane(wu_planes, wu_window[3], 3)
+        deal(wu_woven, wu_planes, SPLIT)
         wu_q = operand("wu", E4M3)
         quantise(wu_q, wu_woven)
-        turn_pair(7, wu_turned, wu_high, 1)
-        du_q = operand("du", E5M2, "wu_woven")
-        quantise(du_q, du)
+        turn_pair(7, wu_turned, wu_planes, 1)
         quantise(wu_turned_q, wu_turned, halves[1])
 
         au = []
@@ -267,29 +253,26 @@ def tile_attend_gglu_x_pl_kernel(tc, xT, wg, wu, dyT, wd, us, tg, tu, wt, offs, 
             au.append(bank(k))
             for t in range(LANES):
                 product(au[k][:, block(t)], wu_q, t, x_q, block(k))
-        sums = []
-        for k in range(LANES):
-            sums.append(bank(LANES + k))
-            product(sums[k][:], du_q, k, wu_turned_q, start=True, stop=False)
+        sums = [bank(LANES + k) for k in range(LANES)]
 
-        result = [tile("result%d" % h, [P, 2, N], F32) for h in range(2)]
+        result = tile("result", [P, LANES, N], F32)
         result_woven = tile("result_woven", [P, N, LANES], BF16)
         out_rows = out_0.rearrange("(m t) d -> m t d", t=LANES)
-        dg = tile("dg", [P, N, LANES], BF16)
-        dg_q = operand("dg", E5M2)
+        grads_q = tile("grads_codes", [P, 2 * N], U32), tile("grads_scales", [P, 2 * N], U8), E5M2
 
         def gate_gradient(k):
-            nc.vector.tensor_tensor(out=by_runs(dg, k), in0=bank_runs(au[k]),
+            nc.vector.tensor_tensor(out=by_runs(grads, 2 * k + 1), in0=bank_runs(au[k]),
                                     in1=gate_factor[:, groups(k), :, :], op=ALU.mult)
 
         def finish(k):
-            quantise(dg_q, dg, block(k))
-            product(sums[k][:], dg_q, k, wg_turned_q, start=False, stop=True)
-            by_feature = result[k // 2][:, k % 2, :].rearrange("m (p j) -> m p j", j=LANES)
-            by_plane = sums[k][:].rearrange("m (j p) -> m p j", j=LANES)
-            for rows in [slice(0, P // 2), slice(P // 2, P)] if k == LANES - 1 else [slice(0, P)]:
-                nc.scalar.copy(out=by_feature[:, rows, :], in_=by_plane[:, rows, :])
-            nc.sync.dma_start(out=out_rows[:, k, :], in_=result[k // 2][:, k % 2, :])
+            quantise(grads_q, grads, slice(2 * P * k, 2 * P * (k + 1)))
+            product(sums[k][:], grads_q, 2 * k, wu_turned_q, start=True, stop=False)
+            product(sums[k][:], grads_q, 2 * k + 1, wg_turned_q, start=False, stop=True)
+            by_feature = result[:, k, :].rearrange("m (c i j) -> m c j i", i=2, j=LANES)
+            by_plane = sums[k][:].rearrange("m (j c i) -> m c j i", i=2, j=LANES)
+            for rows in [slice(0, P // 4), slice(P // 4, P // 2)] if k == LANES - 1 else [slice(0, P // 2)]:
+                nc.scalar.copy(out=by_feature[:, rows, :, :], in_=by_plane[:, rows, :, :])
+            nc.sync.dma_start(out=out_rows[:, k, :], in_=result[:, k, :])
 
         for step in range(LANES + 1):
             if step < LANES:
@@ -297,12 +280,12 @@ def tile_attend_gglu_x_pl_kernel(tc, xT, wg, wu, dyT, wd, us, tg, tu, wt, offs, 
             if step > 0:
                 finish(step - 1)
 
-        weave_pair(on_vector, result_woven, result[0], 0, slice(0, N))
         out_codes = tile("out_codes", [P, N], U32)
         out_scales = tile("out_scales", [P, N], U8)
         codes_hbm = out_1[0].rearrange("p c lane -> p (c lane)").bitcast(I32)
-        for columns in halves:
-            weave_pair(on_vector, result_woven, result[1], 1, columns)
+        for copy, columns in ((on_vector, halves[0]), (on_vector, slice(N // 2, 3 * N // 4)), (on_scalar, slice(3 * N // 4, N))):
+            copy(out=result_woven[:, columns, :].rearrange("p (c i) j -> p c j i", i=RUN),
+                 in_=result[:, :, columns].rearrange("p j (c i) -> p c j i", i=RUN))
         for columns in halves:
             quantise((out_codes, out_scales, E4M3), result_woven, columns)
             nc.sync.dma_start(out=codes_hbm[:, columns], in_=out_codes[:, columns].bitcast(I32))

@@ -29,6 +29,7 @@ def tile_attend_gglu_x_pl_kernel(tc, xT, wg, wu, dyT, wd, us, tg, tu, wt, offs, 
     on_vector, on_scalar = nc.vector.tensor_copy, nc.scalar.copy
     with ExitStack() as ctx:
         sb = ctx.enter_context(tc.tile_pool(name="sb", bufs=1))
+        late = ctx.enter_context(tc.tile_pool(name="late", bufs=1))
         ps = ctx.enter_context(tc.psum_pool(name="ps", bufs=1))
 
         def tile(name, shape, dtype, tag=None):
@@ -74,7 +75,7 @@ def tile_attend_gglu_x_pl_kernel(tc, xT, wg, wu, dyT, wd, us, tg, tu, wt, offs, 
             nc.vector.tensor_copy(out=pair[:, e, :], in_=window[:].indirect(offsets[:]))
 
         def deal(woven, planes, split):
-            for copy, share in ((on_vector, slice(0, split)), (on_scalar, slice(split, P)))[split == 0 :]:
+            for copy, share in ((on_vector, slice(0, split)), (on_scalar, slice(split, P)))[: 1 + (split < P)]:
                 copy(out=woven[:].rearrange("p (t q) j -> p q j t", t=LANES)[:, share, :, :],
                      in_=planes[:].rearrange("p j (q t) -> p q j t", t=LANES)[:, share, :, :])
 
@@ -99,9 +100,6 @@ def tile_attend_gglu_x_pl_kernel(tc, xT, wg, wu, dyT, wd, us, tg, tu, wt, offs, 
             full = tile(name, [P, N], F32)
             nc.scalar.copy(out=full[:], in_=acc[:])
             return full
-
-        def runs(x):
-            return x.rearrange("q (a i) -> q a i", i=RUN)
 
         halves = [slice(0, N // 2), slice(N // 2, N)]
 
@@ -143,6 +141,8 @@ def tile_attend_gglu_x_pl_kernel(tc, xT, wg, wu, dyT, wd, us, tg, tu, wt, offs, 
         wg_turned = tile("wg_turned", [P, N, LANES], BF16)
         tgtu = tile("tgtu", [P, LANES], F32)
         nc.vector.tensor_tensor(out=tgtu[:], in0=listed["tg"][:], in1=listed["tu"][:], op=ALU.mult)
+        less_tgtu = tile("less_tgtu", [P, LANES], F32)
+        nc.vector.tensor_scalar(out=less_tgtu[:], in0=tgtu[:], scalar1=-1.0, scalar2=None, op0=ALU.mult)
         less_tg = tile("less_tg", [P, LANES], F32)
         nc.vector.tensor_scalar(out=less_tg[:], in0=listed["tg"][:], scalar1=-1.0, scalar2=None, op0=ALU.mult)
         gather_plane(wg_planes, wg_window[1], 1)
@@ -159,7 +159,6 @@ def tile_attend_gglu_x_pl_kernel(tc, xT, wg, wu, dyT, wd, us, tg, tu, wt, offs, 
         nc.gpsimd.tensor_tensor(out=wt_us[:], in0=us_rows[:], in1=wt_rows[:], op=ALU.mult)
         nc.gpsimd.tensor_tensor(out=wt_us2[:], in0=wt_us[:], in1=us_rows[:], op=ALU.mult)
         us_full = spread("us_full", us_rows, 6)
-        wt_us2_full = spread("wt_us2_full", wt_us2, 7)
         turn_pair(5, wg_turned, wg_planes, 1)
 
         wg_turned_q = operand("wg_turned", E4M3)
@@ -175,13 +174,15 @@ def tile_attend_gglu_x_pl_kernel(tc, xT, wg, wu, dyT, wd, us, tg, tu, wt, offs, 
         ag = []
         z = tile("z", [P, LANES, N], F32)
         sig = tile("sig", [P, LANES, N], F32)
-        sig_row = tile("sig_row", [P, LANES, N], F32)
+        ag_scaled = tile("ag_scaled", [P, LANES, N], F32, "tu_window")
+        up_factor = tile("up_factor", [P, LANES, N], F32, "tg_window")
         for t in range(LANES):
             ag.append(bank(t))
             product(ag[t][:], wg_q, t, x_q)
             nc.vector.tensor_tensor(out=z[:, t, :], in0=ag[t][:], in1=us_full[:], op=ALU.mult)
             nc.scalar.activation(out=sig[:, t, :], in_=z[:, t, :], func=ACT.Sigmoid, scale=listed["tg"][:, t : t + 1])
-            nc.gpsimd.tensor_tensor(out=sig_row[:, t, :], in0=sig[:, t, :], in1=wt_us2_full[:], op=ALU.mult)
+            nc.scalar.activation(out=ag_scaled[:, t, :], in_=ag[t][:], func=ACT.Copy, scale=tgtu[:, t : t + 1])
+            nc.gpsimd.tensor_tensor(out=up_factor[:, t, :], in0=sig[:, t, :], in1=ag_scaled[:, t, :], op=ALU.mult)
 
         wd_planes = tile("wd_planes", [P, LANES, N], BF16)
         wd_woven = tile("wd_woven", [P, N, LANES], BF16)
@@ -191,83 +192,95 @@ def tile_attend_gglu_x_pl_kernel(tc, xT, wg, wu, dyT, wd, us, tg, tu, wt, offs, 
         gather_plane(wd_planes, wd_window[1], 1)
         gather_plane(wd_planes, wd_window[2], 2)
         gather_plane(wd_planes, wd_window[3], 3)
-        deal(wd_woven, wd_planes, 0)
-        up_factor = tile("up_factor", [P, N // RUN, LANES, RUN], F32, "down3")
-        for t in range(LANES):
-            nc.vector.tensor_tensor(out=up_factor[:, :, t, :], in0=runs(ag[t][:]), in1=runs(sig_row[:, t, :]), op=ALU.mult)
+        deal(wd_woven, wd_planes, P)
+        wd_q = operand("wd", E4M3)
+        quantise(wd_q, wd_woven)
 
-        gate_part = tile("gate_part", [P, LANES, N], F32, "tu_window")
+        gate_part = tile("gate_part", [P, LANES, N], F32, "wd_woven")
         silu = tile("silu", [P, LANES, N], F32, "tg_columns")
-        slope = tile("slope", [P, LANES, N], F32)
+        slope = [tile("slope%d" % t, [P, N], F32) for t in range(LANES)]
         for t in range(LANES):
             nc.scalar.activation(out=silu[:, t, :], in_=z[:, t, :], func=ACT.Silu, scale=less_tg[:, t : t + 1])
-            nc.scalar.activation(out=slope[:, t, :], in_=silu[:, t, :], func=ACT.Copy, scale=-1.0, bias=1.0)
-            nc.gpsimd.tensor_tensor(out=gate_part[:, t, :], in0=slope[:, t, :], in1=sig_row[:, t, :], op=ALU.mult)
+            nc.scalar.activation(out=slope[t][:], in_=silu[:, t, :], func=ACT.Identity,
+                                 scale=less_tgtu[:, t : t + 1], bias=tgtu[:, t : t + 1])
+            nc.gpsimd.tensor_tensor(out=gate_part[:, t, :], in0=slope[t][:], in1=sig[:, t, :], op=ALU.mult)
 
         wu_planes = tile("wu_planes", [P, LANES, N], BF16)
-        wu_woven = tile("wu_woven", [P, N, LANES], BF16)
+        wu_woven = late.tile([P, N, LANES], BF16, name="wu_woven", offset=0, align_bytes=64)
         wu_turned = tile("wu_turned", [P, N, LANES], BF16)
-        dh_scaled = tile("dh_scaled", [P, N // RUN, LANES, RUN], F32, "tg_window")
 
         def by_runs(woven, k):
             return woven[:, block(k), :].rearrange("q (c i) t -> q c t i", i=RUN)
 
-        def groups(k):
-            return slice(k * P // RUN, (k + 1) * P // RUN)
+        def lanes_by_runs(x):
+            return x.rearrange("q t (c i) -> q c t i", i=RUN)
 
-        def bank_runs(acc):
-            return acc[:].rearrange("q (t c i) -> q c t i", t=LANES, i=RUN)
+        def by_lane(acc):
+            return acc[:].rearrange("q (t m) -> q t m", t=LANES)
+
+        dh = []
+        for k in range(LANES):
+            acc = bank(LANES + k % 2)
+            product(acc[:], dy_q, k, wd_q)
+            rows = tile("dh_rows%d" % k, [P, N], F32)
+            nc.scalar.activation(out=rows[:], in_=acc[:], func=ACT.Copy, scale=wt_us2[:, k : k + 1])
+            dh.append(bank(k))
+            for t in range(LANES):
+                nc.tensor.transpose(dh[k][:, block(t)], rows[:, block(t)], ident[:])
 
         gather_plane(wu_planes, wu_window[0], 0)
-        wd_q = operand("wd", E4M3, "gate_up0")
-        quantise(wd_q, wd_woven)
-        dh = []
-        for t in range(LANES):
-            dh.append(bank(LANES + t))
-            product(dh[t][:], wd_q, t, dy_q)
-        gather_plane(wu_planes, wu_window[1], 1)
-        gate_factor = tile("gate_factor", [P, N // RUN, LANES, RUN], F32, "gate_up1")
-        for t in range(LANES):
-            nc.scalar.activation(out=dh_scaled[:, :, t, :], in_=runs(dh[t][:]), func=ACT.Copy, scale=tgtu[:, t : t + 1])
-            other = (t + 2) % LANES
-            nc.vector.scalar_tensor_tensor(out=gate_factor[:, :, other, :], in0=runs(dh[other][:]), scalar=tgtu[:, other : other + 1],
-                                           in1=runs(gate_part[:, other, :]), op0=ALU.mult, op1=ALU.mult)
+        du = []
+        for h in range(2):
+            gather_plane(wu_planes, wu_window[1 + h], 1 + h)
+            du.append(tile("du%d" % h, [P, N // 2, LANES], BF16, "gate_up%d" % (1 + h)))
+            for k in (2 * h, 2 * h + 1):
+                nc.vector.tensor_tensor(out=by_runs(du[h], k % 2), in0=lanes_by_runs(by_lane(dh[k])),
+                                        in1=lanes_by_runs(up_factor[:, :, block(k)]), op=ALU.mult)
+            if h == 0:
+                turn_pair(6, wu_turned, wu_planes, 0)
 
-        grads = tile("grads", [P, 2 * N, LANES], BF16)
-        for k in range(LANES):
-            nc.gpsimd.tensor_tensor(out=by_runs(grads, 2 * k), in0=dh_scaled[:, groups(k), :, :], in1=up_factor[:, groups(k), :, :], op=ALU.mult)
-
-        turn_pair(0, wu_turned, wu_planes, 0)
-        wu_turned_q = operand("wu_turned", E4M3)
-        quantise(wu_turned_q, wu_turned, halves[0])
-        gather_plane(wu_planes, wu_window[2], 2)
         gather_plane(wu_planes, wu_window[3], 3)
         deal(wu_woven, wu_planes, SPLIT)
         wu_q = operand("wu", E4M3)
         quantise(wu_q, wu_woven)
         turn_pair(7, wu_turned, wu_planes, 1)
-        quantise(wu_turned_q, wu_turned, halves[1])
 
         au = []
         for k in range(LANES):
-            au.append(bank(k))
+            au.append(bank(LANES + k))
             for t in range(LANES):
                 product(au[k][:, block(t)], wu_q, t, x_q, block(k))
-        sums = [bank(LANES + k) for k in range(LANES)]
+
+        gate_factor = late.tile([P, LANES, LANES, P], F32, name="gate_factor", offset=3072, align_bytes=64)
+        du_q = late.tile([P, N], U32, name="du_codes", offset=0, align_bytes=64), tile("du_scales", [P, N], U8), E5M2
+        wu_turned_q = operand("wu_turned", E4M3, "gate_up3")
+
+        def gate(k):
+            nc.vector.tensor_tensor(out=gate_factor[:, k, :, :], in0=by_lane(dh[k]), in1=gate_part[:, :, block(k)], op=ALU.mult)
+
+        gate(0)
+        for h in range(2):
+            nc.vector.quantize_mx(out=du_q[0][:, halves[h]].bitcast(E5M2), scales=du_q[1][:, halves[h]], in_=flat(du[h][:]))
+        quantise(wu_turned_q, wu_turned)
 
         result = tile("result", [P, LANES, N], F32)
         result_woven = tile("result_woven", [P, N, LANES], BF16)
         out_rows = out_0.rearrange("(m t) d -> m t d", t=LANES)
-        grads_q = tile("grads_codes", [P, 2 * N], U32), tile("grads_scales", [P, 2 * N], U8), E5M2
+        dg = tile("dg", [P, N, LANES], BF16)
+        dg_q = operand("dg", E5M2)
+        sums = []
 
         def gate_gradient(k):
-            nc.vector.tensor_tensor(out=by_runs(grads, 2 * k + 1), in0=bank_runs(au[k]),
-                                    in1=gate_factor[:, groups(k), :, :], op=ALU.mult)
+            if k + 1 < LANES:
+                gate(k + 1)
+            nc.vector.tensor_tensor(out=by_runs(dg, k), in0=lanes_by_runs(by_lane(au[k])),
+                                    in1=lanes_by_runs(gate_factor[:, k, :, :]), op=ALU.mult)
+            sums.append(bank(k))
+            product(sums[k][:], du_q, k, wu_turned_q, start=True, stop=False)
 
         def finish(k):
-            quantise(grads_q, grads, slice(2 * P * k, 2 * P * (k + 1)))
-            product(sums[k][:], grads_q, 2 * k, wu_turned_q, start=True, stop=False)
-            product(sums[k][:], grads_q, 2 * k + 1, wg_turned_q, start=False, stop=True)
+            quantise(dg_q, dg, block(k))
+            product(sums[k][:], dg_q, k, wg_turned_q, start=False, stop=True)
             by_feature = result[:, k, :].rearrange("m (c i j) -> m c j i", i=2, j=LANES)
             by_plane = sums[k][:].rearrange("m (j c i) -> m c j i", i=2, j=LANES)
             for rows in [slice(0, P // 4), slice(P // 4, P // 2)] if k == LANES - 1 else [slice(0, P // 2)]:

@@ -66,16 +66,17 @@ def tile_attend_gglu_x_pl_kernel(tc, xT, wg, wu, dyT, wd, us, tg, tu, wt, offs, 
             return [load_plane(name, w, tag, j) for j in range(LANES)]
 
         def load_rows(name, a):
-            raw = [tile("%s_raw%d" % (name, h), [P, LANES, N // 2], F32) for h in range(2)]
-            for h in range(2):
-                nc.sync.dma_start(out=raw[h][:], in_=a.rearrange("(p j) r -> p j r", j=LANES)[:, :, halves[h]])
+            raw = tile(name + "_raw", [P, LANES, N], F32)
+            nc.sync.dma_start(out=raw[:], in_=a.rearrange("(p j) r -> p j r", j=LANES))
             return raw
 
         def gather_plane(pair, window, e):
             nc.vector.tensor_copy(out=pair[:, e, :], in_=window[:].indirect(offsets[:]))
 
         def deal(woven, planes, split):
-            for copy, share in ((on_vector, slice(0, split)), (on_scalar, slice(split, P)))[: 1 + (split < P)]:
+            for copy, share in ((on_vector, slice(0, split)), (on_scalar, slice(split, P))):
+                if share.start == share.stop:
+                    continue
                 copy(out=woven[:].rearrange("p (t q) j -> p q j t", t=LANES)[:, share, :, :],
                      in_=planes[:].rearrange("p j (q t) -> p q j t", t=LANES)[:, share, :, :])
 
@@ -88,10 +89,6 @@ def tile_attend_gglu_x_pl_kernel(tc, xT, wg, wu, dyT, wd, us, tg, tu, wt, offs, 
             half = flat(turned[:, halves[h], :]).bitcast(F32).rearrange("q (e p u) -> q e p u", e=2, u=2)
             nc.scalar.copy(out=half, in_=acc[:].rearrange("q (e u p) -> q e p u", e=2, u=2))
 
-        def deal_rows(woven, raw, copies):
-            for h in range(2):
-                copies[h](out=woven[:].rearrange("p (t m) j -> p m j t", t=LANES)[:, h * P // 2 : (h + 1) * P // 2, :, :],
-                               in_=raw[h][:].rearrange("p j (m t) -> p m j t", t=LANES))
 
         def spread(name, columns, b):
             acc = bank(b)
@@ -140,16 +137,16 @@ def tile_attend_gglu_x_pl_kernel(tc, xT, wg, wu, dyT, wd, us, tg, tu, wt, offs, 
         wg_woven = tile("wg_woven", [P, N, LANES], BF16)
         wg_turned = tile("wg_turned", [P, N, LANES], BF16)
         tgtu = tile("tgtu", [P, LANES], F32)
-        nc.vector.tensor_tensor(out=tgtu[:], in0=listed["tg"][:], in1=listed["tu"][:], op=ALU.mult)
+        nc.gpsimd.tensor_tensor(out=tgtu[:], in0=listed["tg"][:], in1=listed["tu"][:], op=ALU.mult)
         less_tgtu = tile("less_tgtu", [P, LANES], F32)
-        nc.vector.tensor_scalar(out=less_tgtu[:], in0=tgtu[:], scalar1=-1.0, scalar2=None, op0=ALU.mult)
+        nc.gpsimd.tensor_scalar(out=less_tgtu[:], in0=tgtu[:], scalar1=-1.0, scalar2=0.0, op0=ALU.mult, op1=ALU.add)
         less_tg = tile("less_tg", [P, LANES], F32)
-        nc.vector.tensor_scalar(out=less_tg[:], in0=listed["tg"][:], scalar1=-1.0, scalar2=None, op0=ALU.mult)
+        nc.gpsimd.tensor_scalar(out=less_tg[:], in0=listed["tg"][:], scalar1=-1.0, scalar2=0.0, op0=ALU.mult, op1=ALU.add)
         gather_plane(wg_planes, wg_window[1], 1)
         turn_pair(4, wg_turned, wg_planes, 0)
         gather_plane(wg_planes, wg_window[2], 2)
         gather_plane(wg_planes, wg_window[3], 3)
-        deal(wg_woven, wg_planes, SPLIT)
+        deal(wg_woven, wg_planes, P)
         wg_q = operand("wg", E4M3)
         quantise(wg_q, wg_woven)
         wu_window = load_planes("wu", wu, "gate_up")
@@ -159,17 +156,16 @@ def tile_attend_gglu_x_pl_kernel(tc, xT, wg, wu, dyT, wd, us, tg, tu, wt, offs, 
         nc.gpsimd.tensor_tensor(out=wt_us[:], in0=us_rows[:], in1=wt_rows[:], op=ALU.mult)
         nc.gpsimd.tensor_tensor(out=wt_us2[:], in0=wt_us[:], in1=us_rows[:], op=ALU.mult)
         us_full = spread("us_full", us_rows, 6)
-        turn_pair(5, wg_turned, wg_planes, 1)
-
-        wg_turned_q = operand("wg_turned", E4M3)
-        quantise(wg_turned_q, wg_turned)
         x_woven = tile("x_woven", [P, N, LANES], BF16)
-        deal_rows(x_woven, x_raw, (on_scalar, on_vector))
+        deal(x_woven, x_raw, P // 2)
         x_q = operand("x", E4M3)
         quantise(x_q, x_woven)
+        turn_pair(5, wg_turned, wg_planes, 1)
+        wg_turned_q = operand("wg_turned", E4M3, "x_woven")
+        quantise(wg_turned_q, wg_turned)
 
         dy_woven = tile("dy_woven", [P, N, LANES], BF16)
-        deal_rows(dy_woven, dy_raw, (on_scalar, on_scalar))
+        deal(dy_woven, dy_raw, 0)
 
         ag = []
         z = tile("z", [P, LANES, N], F32)
@@ -186,9 +182,9 @@ def tile_attend_gglu_x_pl_kernel(tc, xT, wg, wu, dyT, wd, us, tg, tu, wt, offs, 
 
         wd_planes = tile("wd_planes", [P, LANES, N], BF16)
         wd_woven = tile("wd_woven", [P, N, LANES], BF16)
-        gather_plane(wd_planes, wd_window[0], 0)
         dy_q = operand("dy", E5M2)
         quantise(dy_q, dy_woven)
+        gather_plane(wd_planes, wd_window[0], 0)
         gather_plane(wd_planes, wd_window[1], 1)
         gather_plane(wd_planes, wd_window[2], 2)
         gather_plane(wd_planes, wd_window[3], 3)
@@ -198,12 +194,13 @@ def tile_attend_gglu_x_pl_kernel(tc, xT, wg, wu, dyT, wd, us, tg, tu, wt, offs, 
 
         gate_part = tile("gate_part", [P, LANES, N], F32, "wd_woven")
         silu = tile("silu", [P, LANES, N], F32, "tg_columns")
-        slope = [tile("slope%d" % t, [P, N], F32) for t in range(LANES)]
+        slopes = [tile("slope_low", [P, 2, N], F32), tile("slope_high", [P, 2, N], F32)]
+        slope = [slopes[t // 2][:, t % 2, :] for t in range(LANES)]
         for t in range(LANES):
             nc.scalar.activation(out=silu[:, t, :], in_=z[:, t, :], func=ACT.Silu, scale=less_tg[:, t : t + 1])
-            nc.scalar.activation(out=slope[t][:], in_=silu[:, t, :], func=ACT.Identity,
+            nc.scalar.activation(out=slope[t], in_=silu[:, t, :], func=ACT.Identity,
                                  scale=less_tgtu[:, t : t + 1], bias=tgtu[:, t : t + 1])
-            nc.gpsimd.tensor_tensor(out=gate_part[:, t, :], in0=slope[t][:], in1=sig[:, t, :], op=ALU.mult)
+            nc.gpsimd.tensor_tensor(out=gate_part[:, t, :], in0=slope[t], in1=sig[:, t, :], op=ALU.mult)
 
         wu_planes = tile("wu_planes", [P, LANES, N], BF16)
         wu_woven = late.tile([P, N, LANES], BF16, name="wu_woven", offset=0, align_bytes=64)
@@ -219,6 +216,7 @@ def tile_attend_gglu_x_pl_kernel(tc, xT, wg, wu, dyT, wd, us, tg, tu, wt, offs, 
             return acc[:].rearrange("q (t m) -> q t m", t=LANES)
 
         dh = []
+        gate_low = tile("gate_low", [P, 1, LANES, P], F32)
         for k in range(LANES):
             acc = bank(LANES + k % 2)
             product(acc[:], dy_q, k, wd_q)
@@ -227,6 +225,10 @@ def tile_attend_gglu_x_pl_kernel(tc, xT, wg, wu, dyT, wd, us, tg, tu, wt, offs, 
             dh.append(bank(k))
             for t in range(LANES):
                 nc.tensor.transpose(dh[k][:, block(t)], rows[:, block(t)], ident[:])
+            if k < 1:
+                turned = tile("dh_turned%d" % k, [P, N], F32)
+                nc.scalar.copy(out=turned[:], in_=dh[k][:])
+                nc.gpsimd.tensor_tensor(out=gate_low[:, k, :, :], in0=by_lane(turned), in1=gate_part[:, :, block(k)], op=ALU.mult)
 
         gather_plane(wu_planes, wu_window[0], 0)
         du = []
@@ -251,14 +253,15 @@ def tile_attend_gglu_x_pl_kernel(tc, xT, wg, wu, dyT, wd, us, tg, tu, wt, offs, 
             for t in range(LANES):
                 product(au[k][:, block(t)], wu_q, t, x_q, block(k))
 
-        gate_factor = late.tile([P, LANES, LANES, P], F32, name="gate_factor", offset=3072, align_bytes=64)
+        gate_high = late.tile([P, 3, LANES, P], F32, name="gate_high", offset=3072, align_bytes=64)
+        gate_factor = [gate_low[:, 0, :, :]] + [gate_high[:, k, :, :] for k in range(3)]
         du_q = late.tile([P, N], U32, name="du_codes", offset=0, align_bytes=64), tile("du_scales", [P, N], U8), E5M2
         wu_turned_q = operand("wu_turned", E4M3, "gate_up3")
 
         def gate(k):
-            nc.vector.tensor_tensor(out=gate_factor[:, k, :, :], in0=by_lane(dh[k]), in1=gate_part[:, :, block(k)], op=ALU.mult)
+            nc.vector.tensor_tensor(out=gate_factor[k], in0=by_lane(dh[k]), in1=gate_part[:, :, block(k)], op=ALU.mult)
 
-        gate(0)
+        gate(1)
         for h in range(2):
             nc.vector.quantize_mx(out=du_q[0][:, halves[h]].bitcast(E5M2), scales=du_q[1][:, halves[h]], in_=flat(du[h][:]))
         quantise(wu_turned_q, wu_turned)
@@ -271,10 +274,10 @@ def tile_attend_gglu_x_pl_kernel(tc, xT, wg, wu, dyT, wd, us, tg, tu, wt, offs, 
         sums = []
 
         def gate_gradient(k):
-            if k + 1 < LANES:
+            if k in (1, 2):
                 gate(k + 1)
             nc.vector.tensor_tensor(out=by_runs(dg, k), in0=lanes_by_runs(by_lane(au[k])),
-                                    in1=lanes_by_runs(gate_factor[:, k, :, :]), op=ALU.mult)
+                                    in1=lanes_by_runs(gate_factor[k]), op=ALU.mult)
             sums.append(bank(k))
             product(sums[k][:], du_q, k, wu_turned_q, start=True, stop=False)
 

@@ -29,7 +29,6 @@ def tile_attend_gglu_x_pl_kernel(tc, xT, wg, wu, dyT, wd, us, tg, tu, wt, offs, 
     on_vector, on_scalar = nc.vector.tensor_copy, nc.scalar.copy
     with ExitStack() as ctx:
         sb = ctx.enter_context(tc.tile_pool(name="sb", bufs=1))
-        late = ctx.enter_context(tc.tile_pool(name="late", bufs=1))
         ps = ctx.enter_context(tc.psum_pool(name="ps", bufs=1))
 
         def tile(name, shape, dtype, tag=None):
@@ -66,26 +65,29 @@ def tile_attend_gglu_x_pl_kernel(tc, xT, wg, wu, dyT, wd, us, tg, tu, wt, offs, 
             return [load_plane(name, w, tag, j) for j in range(LANES)]
 
         def load_rows(name, a):
-            raw = tile(name + "_raw", [P, LANES, N], F32)
-            nc.sync.dma_start(out=raw[:], in_=a.rearrange("(p j) r -> p j r", j=LANES))
+            raw = tile(name + "_raw", [P, LANES * N], F32)
+            nc.sync.dma_start(out=raw[:], in_=a.rearrange("(p j) r -> p (j r)", j=LANES))
             return raw
 
         def gather_plane(pair, window, e):
-            nc.vector.tensor_copy(out=pair[:, e, :], in_=window[:].indirect(offsets[:]))
+            nc.vector.tensor_copy(out=pair[:, N * e : N * (e + 1)], in_=window[:].indirect(offsets[:]))
 
         def deal(woven, planes, split):
             for copy, share in ((on_vector, slice(0, split)), (on_scalar, slice(split, P))):
                 if share.start == share.stop:
                     continue
                 copy(out=woven[:].rearrange("p (t q) j -> p q j t", t=LANES)[:, share, :, :],
-                     in_=planes[:].rearrange("p j (q t) -> p q j t", t=LANES)[:, share, :, :])
+                     in_=planes[:].rearrange("p (j q t) -> p q j t", j=LANES, t=LANES)[:, share, :, :])
 
-        def turn_pair(b, turned, pair, h):
+        def turn_pair(b, pair, h):
             acc = bank(b)
-            words = pair[:, 2 * h : 2 * h + 2, :].rearrange("p e c -> p (e c)").bitcast(F32)
+            words = pair[:, 2 * N * h : 2 * N * (h + 1)].bitcast(F32)
             for e in range(2):
                 for u in range(2):
                     nc.tensor.transpose(acc[:, block(2 * e + u)], words[:, WORDS * e + u : WORDS * (e + 1) : 2], ident[:])
+            return acc
+
+        def store_turned(acc, turned, h):
             half = flat(turned[:, halves[h], :]).bitcast(F32).rearrange("q (e p u) -> q e p u", e=2, u=2)
             nc.scalar.copy(out=half, in_=acc[:].rearrange("q (e u p) -> q e p u", e=2, u=2))
 
@@ -122,7 +124,7 @@ def tile_attend_gglu_x_pl_kernel(tc, xT, wg, wu, dyT, wd, us, tg, tu, wt, offs, 
         dy_raw = load_rows("dy", dyT)
         wd_window = load_planes("wd", wd, "down")
 
-        wg_planes = tile("wg_planes", [P, LANES, N], BF16)
+        wg_planes = tile("wg_planes", [P, LANES * N], BF16)
         gather_plane(wg_planes, wg_window[0], 0)
         listed = {}
         for name, window, b in (("tg", tg_window, 0), ("tu", tu_window, 1)):
@@ -143,7 +145,7 @@ def tile_attend_gglu_x_pl_kernel(tc, xT, wg, wu, dyT, wd, us, tg, tu, wt, offs, 
         less_tg = tile("less_tg", [P, LANES], F32)
         nc.gpsimd.tensor_scalar(out=less_tg[:], in0=listed["tg"][:], scalar1=-1.0, scalar2=0.0, op0=ALU.mult, op1=ALU.add)
         gather_plane(wg_planes, wg_window[1], 1)
-        turn_pair(4, wg_turned, wg_planes, 0)
+        store_turned(turn_pair(4, wg_planes, 0), wg_turned, 0)
         gather_plane(wg_planes, wg_window[2], 2)
         gather_plane(wg_planes, wg_window[3], 3)
         deal(wg_woven, wg_planes, P)
@@ -160,12 +162,12 @@ def tile_attend_gglu_x_pl_kernel(tc, xT, wg, wu, dyT, wd, us, tg, tu, wt, offs, 
         deal(x_woven, x_raw, P // 2)
         x_q = operand("x", E4M3)
         quantise(x_q, x_woven)
-        turn_pair(5, wg_turned, wg_planes, 1)
+        store_turned(turn_pair(5, wg_planes, 1), wg_turned, 1)
         wg_turned_q = operand("wg_turned", E4M3, "x_woven")
         quantise(wg_turned_q, wg_turned)
 
         dy_woven = tile("dy_woven", [P, N, LANES], BF16)
-        deal(dy_woven, dy_raw, 0)
+        deal(dy_woven, dy_raw, P // 2)
 
         ag = []
         z = tile("z", [P, LANES, N], F32)
@@ -180,7 +182,7 @@ def tile_attend_gglu_x_pl_kernel(tc, xT, wg, wu, dyT, wd, us, tg, tu, wt, offs, 
             nc.scalar.activation(out=ag_scaled[:, t, :], in_=ag[t][:], func=ACT.Copy, scale=tgtu[:, t : t + 1])
             nc.gpsimd.tensor_tensor(out=up_factor[:, t, :], in0=sig[:, t, :], in1=ag_scaled[:, t, :], op=ALU.mult)
 
-        wd_planes = tile("wd_planes", [P, LANES, N], BF16)
+        wd_planes = tile("wd_planes", [P, LANES * N], BF16)
         wd_woven = tile("wd_woven", [P, N, LANES], BF16)
         dy_q = operand("dy", E5M2)
         quantise(dy_q, dy_woven)
@@ -202,9 +204,8 @@ def tile_attend_gglu_x_pl_kernel(tc, xT, wg, wu, dyT, wd, us, tg, tu, wt, offs, 
                                  scale=less_tgtu[:, t : t + 1], bias=tgtu[:, t : t + 1])
             nc.gpsimd.tensor_tensor(out=gate_part[:, t, :], in0=slope[t], in1=sig[:, t, :], op=ALU.mult)
 
-        wu_planes = tile("wu_planes", [P, LANES, N], BF16)
-        wu_woven = late.tile([P, N, LANES], BF16, name="wu_woven", offset=0, align_bytes=64)
-        wu_turned = tile("wu_turned", [P, N, LANES], BF16)
+        wu_planes = tile("wu_planes", [P, LANES * N], BF16)
+        wu_woven = tile("wu_woven", [P, N, LANES], BF16)
 
         def by_runs(woven, k):
             return woven[:, block(k), :].rearrange("q (c i) t -> q c t i", i=RUN)
@@ -225,27 +226,41 @@ def tile_attend_gglu_x_pl_kernel(tc, xT, wg, wu, dyT, wd, us, tg, tu, wt, offs, 
             dh.append(bank(k))
             for t in range(LANES):
                 nc.tensor.transpose(dh[k][:, block(t)], rows[:, block(t)], ident[:])
-            if k < 1:
-                turned = tile("dh_turned%d" % k, [P, N], F32)
-                nc.scalar.copy(out=turned[:], in_=dh[k][:])
-                nc.gpsimd.tensor_tensor(out=gate_low[:, k, :, :], in0=by_lane(turned), in1=gate_part[:, :, block(k)], op=ALU.mult)
+
+        def up_gradient(woven, k):
+            nc.vector.tensor_tensor(out=woven.rearrange("q (c i) t -> q c t i", i=RUN), in0=lanes_by_runs(by_lane(dh[k])),
+                                    in1=lanes_by_runs(up_factor[:, :, block(k)]), op=ALU.mult)
+
+        def quantise_into(q, columns, woven):
+            nc.vector.quantize_mx(out=q[0][:, columns].bitcast(q[2]), scales=q[1][:, columns], in_=flat(woven))
 
         gather_plane(wu_planes, wu_window[0], 0)
-        du = []
-        for h in range(2):
-            gather_plane(wu_planes, wu_window[1 + h], 1 + h)
-            du.append(tile("du%d" % h, [P, N // 2, LANES], BF16, "gate_up%d" % (1 + h)))
-            for k in (2 * h, 2 * h + 1):
-                nc.vector.tensor_tensor(out=by_runs(du[h], k % 2), in0=lanes_by_runs(by_lane(dh[k])),
-                                        in1=lanes_by_runs(up_factor[:, :, block(k)]), op=ALU.mult)
-            if h == 0:
-                turn_pair(6, wu_turned, wu_planes, 0)
+        du_q = operand("du", E5M2)
+        du_early = []
+        for k in range(2):
+            gather_plane(wu_planes, wu_window[1 + k], 1 + k)
+            du_early.append(tile("du%d" % k, [P, P, LANES], BF16, "gate_up%d" % (1 + k)))
+            up_gradient(du_early[k][:], k)
+            if k == 0:
+                turned = tile("dh_turned", [P, N], F32)
+                nc.scalar.copy(out=turned[:], in_=dh[k][:])
+                nc.gpsimd.tensor_tensor(out=gate_low[:, k, :, :], in0=by_lane(turned), in1=gate_part[:, :, block(k)], op=ALU.mult)
+        for k in range(2):
+            quantise_into(du_q, block(k), du_early[k][:])
+
+        dh_copies = {}
+        for k in (2, 3):
+            dh_copies[k] = tile("dh_turned%d" % k, [P, N], F32)
+            nc.scalar.copy(out=dh_copies[k][:], in_=dh[k][:])
 
         gather_plane(wu_planes, wu_window[3], 3)
         deal(wu_woven, wu_planes, SPLIT)
         wu_q = operand("wu", E4M3)
         quantise(wu_q, wu_woven)
-        turn_pair(7, wu_turned, wu_planes, 1)
+        turns = [turn_pair(6 + h, wu_planes, h) for h in range(2)]
+        wu_turned = tile("wu_turned", [P, N, LANES], BF16, "wu_planes")
+        for h in range(2):
+            store_turned(turns[h], wu_turned, h)
 
         au = []
         for k in range(LANES):
@@ -253,53 +268,55 @@ def tile_attend_gglu_x_pl_kernel(tc, xT, wg, wu, dyT, wd, us, tg, tu, wt, offs, 
             for t in range(LANES):
                 product(au[k][:, block(t)], wu_q, t, x_q, block(k))
 
-        gate_high = late.tile([P, 3, LANES, P], F32, name="gate_high", offset=3072, align_bytes=64)
+        behind = tile("behind_wu", [P, UNITS], F32, "wu_woven")
+        du_late = behind[:, 0:N].bitcast(BF16).rearrange("q (c t) -> q c t", t=LANES)
+        gate_high = behind[:, N:UNITS].rearrange("q (k t m) -> q k t m", t=LANES, m=P)
         gate_factor = [gate_low[:, 0, :, :]] + [gate_high[:, k, :, :] for k in range(3)]
-        du_q = late.tile([P, N], U32, name="du_codes", offset=0, align_bytes=64), tile("du_scales", [P, N], U8), E5M2
         wu_turned_q = operand("wu_turned", E4M3, "gate_up3")
-
-        def gate(k):
-            nc.vector.tensor_tensor(out=gate_factor[k], in0=by_lane(dh[k]), in1=gate_part[:, :, block(k)], op=ALU.mult)
-
-        gate(1)
-        for h in range(2):
-            nc.vector.quantize_mx(out=du_q[0][:, halves[h]].bitcast(E5M2), scales=du_q[1][:, halves[h]], in_=flat(du[h][:]))
-        quantise(wu_turned_q, wu_turned)
 
         result = tile("result", [P, LANES, N], F32)
         result_woven = tile("result_woven", [P, N, LANES], BF16)
         out_rows = out_0.rearrange("(m t) d -> m t d", t=LANES)
         dg = tile("dg", [P, N, LANES], BF16)
         dg_q = operand("dg", E5M2)
-        sums = []
+
+        def gate(k):
+            nc.vector.tensor_tensor(out=gate_factor[k], in0=by_lane(dh[k]), in1=gate_part[:, :, block(k)], op=ALU.mult)
 
         def gate_gradient(k):
-            if k in (1, 2):
-                gate(k + 1)
             nc.vector.tensor_tensor(out=by_runs(dg, k), in0=lanes_by_runs(by_lane(au[k])),
                                     in1=lanes_by_runs(gate_factor[k]), op=ALU.mult)
-            sums.append(bank(k))
-            product(sums[k][:], du_q, k, wu_turned_q, start=True, stop=False)
 
         def finish(k):
             quantise(dg_q, dg, block(k))
-            product(sums[k][:], dg_q, k, wg_turned_q, start=False, stop=True)
+            acc = bank(k)
+            product(acc[:], du_q, k, wu_turned_q, start=True, stop=False)
+            product(acc[:], dg_q, k, wg_turned_q, start=False, stop=True)
             by_feature = result[:, k, :].rearrange("m (c i j) -> m c j i", i=2, j=LANES)
-            by_plane = sums[k][:].rearrange("m (j c i) -> m c j i", i=2, j=LANES)
+            by_plane = acc[:].rearrange("m (j c i) -> m c j i", i=2, j=LANES)
             for rows in [slice(0, P // 4), slice(P // 4, P // 2)] if k == LANES - 1 else [slice(0, P // 2)]:
                 nc.scalar.copy(out=by_feature[:, rows, :, :], in_=by_plane[:, rows, :, :])
             nc.sync.dma_start(out=out_rows[:, k, :], in_=result[:, k, :])
 
-        for step in range(LANES + 1):
-            if step < LANES:
-                gate_gradient(step)
-            if step > 0:
-                finish(step - 1)
+        for k in (2, 3):
+            nc.gpsimd.tensor_tensor(out=gate_factor[k], in0=by_lane(dh_copies[k]), in1=gate_part[:, :, block(k)], op=ALU.mult)
+            up_gradient(du_late[:, block(k - 2), :], k)
+        gate_gradient(0)
+        gate(1)
+        gate_gradient(1)
+        quantise(wu_turned_q, wu_turned)
+        finish(0)
+        gate_gradient(2)
+        finish(1)
+        quantise_into(du_q, halves[1], du_late)
+        gate_gradient(3)
+        finish(2)
+        finish(3)
 
         out_codes = tile("out_codes", [P, N], U32)
         out_scales = tile("out_scales", [P, N], U8)
         codes_hbm = out_1[0].rearrange("p c lane -> p (c lane)").bitcast(I32)
-        for copy, columns in ((on_vector, halves[0]), (on_vector, slice(N // 2, 3 * N // 4)), (on_scalar, slice(3 * N // 4, N))):
+        for copy, columns in ((on_vector, halves[0]), (on_vector, slice(N // 2, 5 * N // 8)), (on_scalar, slice(5 * N // 8, N))):
             copy(out=result_woven[:, columns, :].rearrange("p (c i) j -> p c j i", i=RUN),
                  in_=result[:, :, columns].rearrange("p j (c i) -> p c j i", i=RUN))
         for columns in halves:

@@ -76,7 +76,7 @@ def tile_attend_gglu_x_pl_kernel(tc, xT, wg, wu, dyT, wd, us, tg, tu, wt, offs, 
             for copy, share in ((on_vector, slice(0, split)), (on_scalar, slice(split, P))):
                 if share.start == share.stop:
                     continue
-                copy(out=woven[:].rearrange("p (t q) j -> p q j t", t=LANES)[:, share, :, :],
+                copy(out=woven[:, :, :].rearrange("p (t q) j -> p q j t", t=LANES)[:, share, :, :],
                      in_=planes[:].rearrange("p (j q t) -> p q j t", j=LANES, t=LANES)[:, share, :, :])
 
         def turn_pair(b, pair, h):
@@ -169,11 +169,14 @@ def tile_attend_gglu_x_pl_kernel(tc, xT, wg, wu, dyT, wd, us, tg, tu, wt, offs, 
         dy_woven = tile("dy_woven", [P, N, LANES], BF16)
         deal(dy_woven, dy_raw, P // 2)
 
+        dy_q = operand("dy", E5M2)
+        quantise(dy_q, dy_woven)
+
         ag = []
         z = tile("z", [P, LANES, N], F32)
         sig = tile("sig", [P, LANES, N], F32)
         ag_scaled = tile("ag_scaled", [P, LANES, N], F32, "tu_window")
-        up_factor = tile("up_factor", [P, LANES, N], F32, "tg_window")
+        up_factor = tile("up_factor", [P, LANES, N], F32, "dy_woven")
         for t in range(LANES):
             ag.append(bank(t))
             product(ag[t][:], wg_q, t, x_q)
@@ -183,9 +186,9 @@ def tile_attend_gglu_x_pl_kernel(tc, xT, wg, wu, dyT, wd, us, tg, tu, wt, offs, 
             nc.gpsimd.tensor_tensor(out=up_factor[:, t, :], in0=sig[:, t, :], in1=ag_scaled[:, t, :], op=ALU.mult)
 
         wd_planes = tile("wd_planes", [P, LANES * N], BF16)
-        wd_woven = tile("wd_woven", [P, N, LANES], BF16)
-        dy_q = operand("dy", E5M2)
-        quantise(dy_q, dy_woven)
+        gate_bytes = tile("gate_part", [P, LANES * N], F32, "tg_window")
+        gate_part = gate_bytes[:].rearrange("q (t r) -> q t r", t=LANES)
+        wd_woven = gate_bytes[:, N : 3 * N].bitcast(BF16).rearrange("p (c j) -> p c j", j=LANES)
         gather_plane(wd_planes, wd_window[0], 0)
         gather_plane(wd_planes, wd_window[1], 1)
         gather_plane(wd_planes, wd_window[2], 2)
@@ -194,7 +197,6 @@ def tile_attend_gglu_x_pl_kernel(tc, xT, wg, wu, dyT, wd, us, tg, tu, wt, offs, 
         wd_q = operand("wd", E4M3)
         quantise(wd_q, wd_woven)
 
-        gate_part = tile("gate_part", [P, LANES, N], F32, "wd_woven")
         silu = tile("silu", [P, LANES, N], F32, "tg_columns")
         slopes = [tile("slope_low", [P, 2, N], F32), tile("slope_high", [P, 2, N], F32)]
         slope = [slopes[t // 2][:, t % 2, :] for t in range(LANES)]
@@ -217,7 +219,7 @@ def tile_attend_gglu_x_pl_kernel(tc, xT, wg, wu, dyT, wd, us, tg, tu, wt, offs, 
             return acc[:].rearrange("q (t m) -> q t m", t=LANES)
 
         dh = []
-        gate_low = tile("gate_low", [P, 1, LANES, P], F32)
+        gate_low = tile("gate_low", [P, 2, LANES, P], F32)
         for k in range(LANES):
             acc = bank(LANES + k % 2)
             product(acc[:], dy_q, k, wd_q)
@@ -235,18 +237,14 @@ def tile_attend_gglu_x_pl_kernel(tc, xT, wg, wu, dyT, wd, us, tg, tu, wt, offs, 
             nc.vector.quantize_mx(out=q[0][:, columns].bitcast(q[2]), scales=q[1][:, columns], in_=flat(woven))
 
         gather_plane(wu_planes, wu_window[0], 0)
-        du_q = operand("du", E5M2)
         du_early = []
         for k in range(2):
             gather_plane(wu_planes, wu_window[1 + k], 1 + k)
             du_early.append(tile("du%d" % k, [P, P, LANES], BF16, "gate_up%d" % (1 + k)))
             up_gradient(du_early[k][:], k)
-            if k == 0:
-                turned = tile("dh_turned", [P, N], F32)
-                nc.scalar.copy(out=turned[:], in_=dh[k][:])
-                nc.gpsimd.tensor_tensor(out=gate_low[:, k, :, :], in0=by_lane(turned), in1=gate_part[:, :, block(k)], op=ALU.mult)
-        for k in range(2):
-            quantise_into(du_q, block(k), du_early[k][:])
+            turned = tile("dh_turned%d" % k, [P, N], F32)
+            nc.scalar.copy(out=turned[:], in_=dh[k][:])
+            nc.gpsimd.tensor_tensor(out=gate_low[:, k, :, :], in0=by_lane(turned), in1=gate_part[:, :, block(k)], op=ALU.mult)
 
         dh_copies = {}
         for k in (2, 3):
@@ -268,20 +266,18 @@ def tile_attend_gglu_x_pl_kernel(tc, xT, wg, wu, dyT, wd, us, tg, tu, wt, offs, 
             for t in range(LANES):
                 product(au[k][:, block(t)], wu_q, t, x_q, block(k))
 
-        behind = tile("behind_wu", [P, UNITS], F32, "wu_woven")
+        behind = tile("behind_wu", [P, 3 * N], F32, "wu_woven")
         du_late = behind[:, 0:N].bitcast(BF16).rearrange("q (c t) -> q c t", t=LANES)
-        gate_high = behind[:, N:UNITS].rearrange("q (k t m) -> q k t m", t=LANES, m=P)
-        gate_factor = [gate_low[:, 0, :, :]] + [gate_high[:, k, :, :] for k in range(3)]
-        wu_turned_q = operand("wu_turned", E4M3, "gate_up3")
+        gate_high = behind[:, N : 3 * N].rearrange("q (k t m) -> q k t m", t=LANES, m=P)
+        gate_factor = [(gate_low, gate_high)[k // 2][:, k % 2, :, :] for k in range(LANES)]
+        du_q = operand("du", E5M2, "gate_up3")
+        wu_turned_q = operand("wu_turned", E4M3)
 
         result = tile("result", [P, LANES, N], F32)
         result_woven = tile("result_woven", [P, N, LANES], BF16)
         out_rows = out_0.rearrange("(m t) d -> m t d", t=LANES)
         dg = tile("dg", [P, N, LANES], BF16)
         dg_q = operand("dg", E5M2)
-
-        def gate(k):
-            nc.vector.tensor_tensor(out=gate_factor[k], in0=by_lane(dh[k]), in1=gate_part[:, :, block(k)], op=ALU.mult)
 
         def gate_gradient(k):
             nc.vector.tensor_tensor(out=by_runs(dg, k), in0=lanes_by_runs(by_lane(au[k])),
@@ -301,13 +297,12 @@ def tile_attend_gglu_x_pl_kernel(tc, xT, wg, wu, dyT, wd, us, tg, tu, wt, offs, 
         for k in (2, 3):
             nc.gpsimd.tensor_tensor(out=gate_factor[k], in0=by_lane(dh_copies[k]), in1=gate_part[:, :, block(k)], op=ALU.mult)
             up_gradient(du_late[:, block(k - 2), :], k)
-        gate_gradient(0)
-        gate(1)
-        gate_gradient(1)
+        for k in range(3):
+            gate_gradient(k)
         quantise(wu_turned_q, wu_turned)
-        finish(0)
-        gate_gradient(2)
-        finish(1)
+        for k in range(2):
+            quantise_into(du_q, block(k), du_early[k][:])
+            finish(k)
         quantise_into(du_q, halves[1], du_late)
         gate_gradient(3)
         finish(2)

@@ -79,6 +79,16 @@ def tile_attend_gglu_x_pl_kernel(tc, xT, wg, wu, dyT, wd, us, tg, tu, wt, offs, 
                 copy(out=woven[:, :, :].rearrange("p (t q) j -> p q j t", t=LANES)[:, share, :, :],
                      in_=planes[:].rearrange("p (j q t) -> p q j t", j=LANES, t=LANES)[:, share, :, :])
 
+        def gather_in_halves(planes, window, j):
+            for h in range(2):
+                nc.vector.tensor_copy(out=planes[:, N * j + h * N // 2 : N * j + (h + 1) * N // 2],
+                                      in_=window[:].indirect(offsets[:, 16 * h : 16 * (h + 1)]))
+
+        def deal_part(copy, woven, planes, h, lanes):
+            groups = slice(h * P // 2, (h + 1) * P // 2)
+            copy(out=woven[:, :, :].rearrange("p (t q) j -> p q j t", t=LANES)[:, groups, :, lanes],
+                 in_=planes[:].rearrange("p (j q t) -> p q j t", j=LANES, t=LANES)[:, groups, :, lanes])
+
         def turn_pair(b, pair, h):
             acc = bank(b)
             words = pair[:, 2 * N * h : 2 * N * (h + 1)].bitcast(F32)
@@ -108,7 +118,8 @@ def tile_attend_gglu_x_pl_kernel(tc, xT, wg, wu, dyT, wd, us, tg, tu, wt, offs, 
         nc.vector.memset(tg_window[0 : P - 1, :], 0.0)
         ident = tile("ident", [P, P], F32)
         make_identity(nc, ident[:])
-        nc.gpsimd.memset(tu_window[0 : P - 1, :], 0.0)
+        nc.gpsimd.memset(tu_window[0 : P // 2 - 1, :], 0.0)
+        nc.gpsimd.memset(tu_window[P // 2 : P, :], 0.0)
 
         us_rows = tile("us_rows", [P, LANES], F32)
         wt_rows = tile("wt_rows", [P, LANES], F32)
@@ -116,7 +127,7 @@ def tile_attend_gglu_x_pl_kernel(tc, xT, wg, wu, dyT, wd, us, tg, tu, wt, offs, 
         wg_window = [load_plane("wg", wg, "gate_up", 0)]
         nc.sync.dma_start(offsets[:], offs)
         nc.sync.dma_start(out=tg_window[P - 1 : P, :], in_=tg[P - 1 : P, :])
-        nc.sync.dma_start(out=tu_window[P - 1 : P, :], in_=tu[P - 1 : P, :])
+        nc.sync.dma_start(out=tu_window[P // 2 - 1 : P // 2, :], in_=tu[0:1, :])
         nc.sync.dma_start(out=us_rows[:], in_=us.rearrange("(m t) o -> m (t o)", t=LANES))
         nc.sync.dma_start(out=wt_rows[:], in_=wt.rearrange("(m t) o -> m (t o)", t=LANES))
         wg_window.extend(load_plane("wg", wg, "gate_up", j) for j in range(1, LANES))
@@ -127,14 +138,14 @@ def tile_attend_gglu_x_pl_kernel(tc, xT, wg, wu, dyT, wd, us, tg, tu, wt, offs, 
         wg_planes = tile("wg_planes", [P, LANES * N], BF16)
         gather_plane(wg_planes, wg_window[0], 0)
         listed = {}
-        for name, window, b in (("tg", tg_window, 0), ("tu", tu_window, 1)):
+        for name, window, b, live in (("tg", tg_window, 0, P - 1), ("tu", tu_window, 1, P // 2 - 1)):
             row = tile(name + "_row", [P, N], F32)
             nc.vector.tensor_copy(out=row[:], in_=window[:].indirect(offsets[:]))
             acc = bank(b)
             for t in range(LANES):
                 nc.tensor.transpose(acc[:, block(t)], row[:, t:N:LANES], ident[:])
             listed[name] = tile(name + "_columns", [P, LANES], F32)
-            nc.scalar.copy(out=listed[name][:], in_=acc[:, P - 1 : N : P])
+            nc.scalar.copy(out=listed[name][:], in_=acc[:, live:N:P])
 
         wg_woven = tile("wg_woven", [P, N, LANES], BF16)
         wg_turned = tile("wg_turned", [P, N, LANES], BF16)
@@ -147,10 +158,13 @@ def tile_attend_gglu_x_pl_kernel(tc, xT, wg, wu, dyT, wd, us, tg, tu, wt, offs, 
         gather_plane(wg_planes, wg_window[1], 1)
         store_turned(turn_pair(4, wg_planes, 0), wg_turned, 0)
         gather_plane(wg_planes, wg_window[2], 2)
-        gather_plane(wg_planes, wg_window[3], 3)
-        deal(wg_woven, wg_planes, P)
+        gather_in_halves(wg_planes, wg_window[3], 3)
+        deal_part(on_vector, wg_woven, wg_planes, 0, slice(0, LANES))
+        for g in range(2):
+            deal_part(on_vector, wg_woven, wg_planes, 1, slice(2 * g, 2 * g + 2))
         wg_q = operand("wg", E4M3)
-        quantise(wg_q, wg_woven)
+        for columns in halves:
+            quantise(wg_q, wg_woven, columns)
         wu_window = load_planes("wu", wu, "gate_up")
 
         wt_us = tile("wt_us", [P, LANES], F32)
@@ -159,9 +173,12 @@ def tile_attend_gglu_x_pl_kernel(tc, xT, wg, wu, dyT, wd, us, tg, tu, wt, offs, 
         nc.gpsimd.tensor_tensor(out=wt_us2[:], in0=wt_us[:], in1=us_rows[:], op=ALU.mult)
         us_full = spread("us_full", us_rows, 6)
         x_woven = tile("x_woven", [P, N, LANES], BF16)
-        deal(x_woven, x_raw, P // 2)
+        deal_part(on_scalar, x_woven, x_raw, 0, slice(0, LANES))
+        for g in range(2):
+            deal_part(on_vector, x_woven, x_raw, 1, slice(2 * g, 2 * g + 2))
         x_q = operand("x", E4M3)
-        quantise(x_q, x_woven)
+        for columns in halves:
+            quantise(x_q, x_woven, columns)
         store_turned(turn_pair(5, wg_planes, 1), wg_turned, 1)
         wg_turned_q = operand("wg_turned", E4M3, "x_woven")
         quantise(wg_turned_q, wg_turned)
@@ -175,15 +192,19 @@ def tile_attend_gglu_x_pl_kernel(tc, xT, wg, wu, dyT, wd, us, tg, tu, wt, offs, 
         ag = []
         z = tile("z", [P, LANES, N], F32)
         sig = tile("sig", [P, LANES, N], F32)
-        ag_scaled = tile("ag_scaled", [P, LANES, N], F32, "tu_window")
+        ag_scaled = tile("ag_scaled", [P, LANES - 1, N], F32, "tu_window")
         up_factor = tile("up_factor", [P, LANES, N], F32, "dy_woven")
         for t in range(LANES):
             ag.append(bank(t))
             product(ag[t][:], wg_q, t, x_q)
             nc.vector.tensor_tensor(out=z[:, t, :], in0=ag[t][:], in1=us_full[:], op=ALU.mult)
             nc.scalar.activation(out=sig[:, t, :], in_=z[:, t, :], func=ACT.Sigmoid, scale=listed["tg"][:, t : t + 1])
-            nc.scalar.activation(out=ag_scaled[:, t, :], in_=ag[t][:], func=ACT.Copy, scale=tgtu[:, t : t + 1])
-            nc.gpsimd.tensor_tensor(out=up_factor[:, t, :], in0=sig[:, t, :], in1=ag_scaled[:, t, :], op=ALU.mult)
+            if t < LANES - 1:
+                nc.scalar.activation(out=ag_scaled[:, t, :], in_=ag[t][:], func=ACT.Copy, scale=tgtu[:, t : t + 1])
+                nc.gpsimd.tensor_tensor(out=up_factor[:, t, :], in0=sig[:, t, :], in1=ag_scaled[:, t, :], op=ALU.mult)
+            else:
+                nc.vector.scalar_tensor_tensor(out=up_factor[:, t, :], in0=ag[t][:], scalar=tgtu[:, t : t + 1], in1=sig[:, t, :],
+                                               op0=ALU.mult, op1=ALU.mult)
 
         wd_planes = tile("wd_planes", [P, LANES * N], BF16)
         gate_bytes = tile("gate_part", [P, LANES * N], F32, "tg_window")
@@ -192,19 +213,22 @@ def tile_attend_gglu_x_pl_kernel(tc, xT, wg, wu, dyT, wd, us, tg, tu, wt, offs, 
         gather_plane(wd_planes, wd_window[0], 0)
         gather_plane(wd_planes, wd_window[1], 1)
         gather_plane(wd_planes, wd_window[2], 2)
-        gather_plane(wd_planes, wd_window[3], 3)
-        deal(wd_woven, wd_planes, P)
+        gather_in_halves(wd_planes, wd_window[3], 3)
+        deal_part(on_vector, wd_woven, wd_planes, 0, slice(0, LANES))
+        for g in range(2):
+            deal_part(on_vector, wd_woven, wd_planes, 1, slice(2 * g, 2 * g + 2))
         wd_q = operand("wd", E4M3)
-        quantise(wd_q, wd_woven)
+        for columns in halves:
+            quantise(wd_q, wd_woven, columns)
 
         silu = tile("silu", [P, LANES, N], F32, "tg_columns")
-        slopes = [tile("slope_low", [P, 2, N], F32), tile("slope_high", [P, 2, N], F32)]
-        slope = [slopes[t // 2][:, t % 2, :] for t in range(LANES)]
+        slope = tile("slope", [P, LANES, N], F32)
         for t in range(LANES):
             nc.scalar.activation(out=silu[:, t, :], in_=z[:, t, :], func=ACT.Silu, scale=less_tg[:, t : t + 1])
-            nc.scalar.activation(out=slope[t], in_=silu[:, t, :], func=ACT.Identity,
+            nc.scalar.activation(out=slope[:, t, :], in_=silu[:, t, :], func=ACT.Identity,
                                  scale=less_tgtu[:, t : t + 1], bias=tgtu[:, t : t + 1])
-            nc.gpsimd.tensor_tensor(out=gate_part[:, t, :], in0=slope[t], in1=sig[:, t, :], op=ALU.mult)
+        for lanes in (slice(0, 1), slice(1, 3), slice(3, 4)):
+            nc.gpsimd.tensor_tensor(out=gate_part[:, lanes, :], in0=slope[:, lanes, :], in1=sig[:, lanes, :], op=ALU.mult)
 
         wu_planes = tile("wu_planes", [P, LANES * N], BF16)
         wu_woven = tile("wu_woven", [P, N, LANES], BF16)
@@ -216,7 +240,7 @@ def tile_attend_gglu_x_pl_kernel(tc, xT, wg, wu, dyT, wd, us, tg, tu, wt, offs, 
             return x.rearrange("q t (c i) -> q c t i", i=RUN)
 
         def by_lane(acc):
-            return acc[:].rearrange("q (t m) -> q t m", t=LANES)
+            return acc[:, :].rearrange("q (t m) -> q t m", t=LANES)
 
         dh = []
         gate_low = tile("gate_low", [P, 2, LANES, P], F32)
@@ -241,22 +265,29 @@ def tile_attend_gglu_x_pl_kernel(tc, xT, wg, wu, dyT, wd, us, tg, tu, wt, offs, 
         for k in range(2):
             gather_plane(wu_planes, wu_window[1 + k], 1 + k)
             du_early.append(tile("du%d" % k, [P, P, LANES], BF16, "gate_up%d" % (1 + k)))
-            up_gradient(du_early[k][:], k)
+            if k == 0:
+                up_gradient(du_early[k][:], k)
             turned = tile("dh_turned%d" % k, [P, N], F32)
             nc.scalar.copy(out=turned[:], in_=dh[k][:])
             nc.gpsimd.tensor_tensor(out=gate_low[:, k, :, :], in0=by_lane(turned), in1=gate_part[:, :, block(k)], op=ALU.mult)
+            if k == 1:
+                up_gradient(du_early[k][:], k)
 
-        dh_copies = {}
-        for k in (2, 3):
-            dh_copies[k] = tile("dh_turned%d" % k, [P, N], F32)
-            nc.scalar.copy(out=dh_copies[k][:], in_=dh[k][:])
+        dh_copies = {2: tile("dh_turned2", [P, N], F32)[:, :]}
+        nc.scalar.copy(out=dh_copies[2], in_=dh[2][:])
 
-        gather_plane(wu_planes, wu_window[3], 3)
-        deal(wu_woven, wu_planes, SPLIT)
+        gather_in_halves(wu_planes, wu_window[3], 3)
+        deal_part(on_scalar, wu_woven, wu_planes, 0, slice(0, LANES))
+        for g in range(2):
+            deal_part(on_vector, wu_woven, wu_planes, 1, slice(2 * g, 2 * g + 2))
         wu_q = operand("wu", E4M3)
-        quantise(wu_q, wu_woven)
+        for columns in halves:
+            quantise(wu_q, wu_woven, columns)
         turns = [turn_pair(6 + h, wu_planes, h) for h in range(2)]
-        wu_turned = tile("wu_turned", [P, N, LANES], BF16, "wu_planes")
+        behind_weave = tile("behind_weave", [P, 3 * N], F32, "wu_planes")
+        wu_turned = behind_weave[:, 0 : 2 * N].bitcast(BF16).rearrange("q (c j) -> q c j", j=LANES)
+        dh_copies[3] = behind_weave[:, 2 * N :]
+        nc.scalar.copy(out=dh_copies[3], in_=dh[3][:])
         for h in range(2):
             store_turned(turns[h], wu_turned, h)
 

@@ -321,7 +321,7 @@ def tile_attend_gglu_x_pl_kernel(tc, xT, wg, wu, dyT, wd, us, tg, tu, wt, offs, 
             product(acc[:], dg_q, k, wg_turned_q, start=False, stop=True)
             by_feature = result[:, k, :].rearrange("m (c i j) -> m c j i", i=2, j=LANES)
             by_plane = acc[:].rearrange("m (j c i) -> m c j i", i=2, j=LANES)
-            for rows in [slice(0, P // 4), slice(P // 4, P // 2)] if k == LANES - 1 else [slice(0, P // 2)]:
+            for rows in [slice(0, P // 8), slice(P // 8, P // 4), slice(P // 4, P // 2)] if k == LANES - 1 else [slice(0, P // 2)]:
                 nc.scalar.copy(out=by_feature[:, rows, :, :], in_=by_plane[:, rows, :, :])
             nc.sync.dma_start(out=out_rows[:, k, :], in_=result[:, k, :])
 
@@ -330,6 +330,8 @@ def tile_attend_gglu_x_pl_kernel(tc, xT, wg, wu, dyT, wd, us, tg, tu, wt, offs, 
             up_gradient(du_late[:, block(k - 2), :], k)
         for k in range(3):
             gate_gradient(k)
+            if k > 0:
+                product(bank(LANES + k)[:], x_q, 0, wg_q)
         quantise(wu_turned_q, wu_turned)
         for k in range(2):
             quantise_into(du_q, block(k), du_early[k][:])
@@ -342,7 +344,7 @@ def tile_attend_gglu_x_pl_kernel(tc, xT, wg, wu, dyT, wd, us, tg, tu, wt, offs, 
         out_codes = tile("out_codes", [P, N], U32)
         out_scales = tile("out_scales", [P, N], U8)
         codes_hbm = out_1[0].rearrange("p c lane -> p (c lane)").bitcast(I32)
-        for copy, columns in ((on_vector, halves[0]), (on_vector, slice(N // 2, 5 * N // 8)), (on_scalar, slice(5 * N // 8, N))):
+        for copy, columns in ((on_vector, slice(0, N // 4)), (on_vector, slice(N // 4, N // 2)), (on_vector, slice(N // 2, 11 * N // 16)), (on_scalar, slice(11 * N // 16, N))):
             copy(out=result_woven[:, columns, :].rearrange("p (c i) j -> p c j i", i=RUN),
                  in_=result[:, :, columns].rearrange("p j (c i) -> p c j i", i=RUN))
         for columns in halves:

@@ -227,7 +227,7 @@ def tile_attend_gglu_x_pl_kernel(tc, xT, wg, wu, dyT, wd, us, tg, tu, wt, offs, 
             nc.scalar.activation(out=silu[:, t, :], in_=z[:, t, :], func=ACT.Silu, scale=less_tg[:, t : t + 1])
             nc.scalar.activation(out=slope[:, t, :], in_=silu[:, t, :], func=ACT.Identity,
                                  scale=less_tgtu[:, t : t + 1], bias=tgtu[:, t : t + 1])
-        for lanes in (slice(0, 1), slice(1, 3), slice(3, 4)):
+        for lanes in (slice(0, 1), slice(1, LANES)):
             nc.gpsimd.tensor_tensor(out=gate_part[:, lanes, :], in0=slope[:, lanes, :], in1=sig[:, lanes, :], op=ALU.mult)
 
         wu_planes = tile("wu_planes", [P, LANES * N], BF16)
@@ -245,7 +245,7 @@ def tile_attend_gglu_x_pl_kernel(tc, xT, wg, wu, dyT, wd, us, tg, tu, wt, offs, 
         dh = []
         gate_low = tile("gate_low", [P, 2, LANES, P], F32)
         for k in range(LANES):
-            acc = bank(LANES + k % 2)
+            acc = bank(LANES + k % 3)
             product(acc[:], dy_q, k, wd_q)
             rows = tile("dh_rows%d" % k, [P, N], F32)
             nc.scalar.activation(out=rows[:], in_=acc[:], func=ACT.Copy, scale=wt_us2[:, k : k + 1])
@@ -262,19 +262,21 @@ def tile_attend_gglu_x_pl_kernel(tc, xT, wg, wu, dyT, wd, us, tg, tu, wt, offs, 
 
         gather_plane(wu_planes, wu_window[0], 0)
         du_early = []
+        turned = tile("dh_turned_low", [P, 2, N], F32)
         for k in range(2):
             gather_plane(wu_planes, wu_window[1 + k], 1 + k)
             du_early.append(tile("du%d" % k, [P, P, LANES], BF16, "gate_up%d" % (1 + k)))
             if k == 0:
                 up_gradient(du_early[k][:], k)
-            turned = tile("dh_turned%d" % k, [P, N], F32)
-            nc.scalar.copy(out=turned[:], in_=dh[k][:])
-            nc.gpsimd.tensor_tensor(out=gate_low[:, k, :, :], in0=by_lane(turned), in1=gate_part[:, :, block(k)], op=ALU.mult)
+            nc.scalar.copy(out=turned[:, k, :], in_=dh[k][:])
+            nc.gpsimd.tensor_tensor(out=gate_low[:, k, :, :], in0=by_lane(turned[:, k, :]), in1=gate_part[:, :, block(k)], op=ALU.mult)
             if k == 1:
                 up_gradient(du_early[k][:], k)
 
-        dh_copies = {2: tile("dh_turned2", [P, N], F32)[:, :]}
-        nc.scalar.copy(out=dh_copies[2], in_=dh[2][:])
+        dh_copies = {}
+        for k in (2, 3):
+            dh_copies[k] = tile("dh_turned%d" % k, [P, N], F32)
+            nc.scalar.copy(out=dh_copies[k][:], in_=dh[k][:])
 
         gather_in_halves(wu_planes, wu_window[3], 3)
         deal_part(on_scalar, wu_woven, wu_planes, 0, slice(0, LANES))
@@ -284,10 +286,7 @@ def tile_attend_gglu_x_pl_kernel(tc, xT, wg, wu, dyT, wd, us, tg, tu, wt, offs, 
         for columns in halves:
             quantise(wu_q, wu_woven, columns)
         turns = [turn_pair(6 + h, wu_planes, h) for h in range(2)]
-        behind_weave = tile("behind_weave", [P, 3 * N], F32, "wu_planes")
-        wu_turned = behind_weave[:, 0 : 2 * N].bitcast(BF16).rearrange("q (c j) -> q c j", j=LANES)
-        dh_copies[3] = behind_weave[:, 2 * N :]
-        nc.scalar.copy(out=dh_copies[3], in_=dh[3][:])
+        wu_turned = tile("wu_turned", [P, N, LANES], BF16, "wu_planes")
         for h in range(2):
             store_turned(turns[h], wu_turned, h)
 

@@ -19,7 +19,7 @@ LANES = 4
 N = P * LANES
 UNITS = 2048
 WORDS = N // 2
-RUN = 4
+RUN = 2
 SPLIT = 84
 FLOPS = 5 * 2 * N * N * N
 
@@ -313,6 +313,10 @@ def tile_attend_gglu_x_pl_kernel(tc, xT, wg, wu, dyT, wd, us, tg, tu, wt, offs, 
             nc.vector.tensor_tensor(out=by_runs(dg, k), in0=lanes_by_runs(by_lane(au[k])),
                                     in1=lanes_by_runs(gate_factor[k]), op=ALU.mult)
 
+        def weave_result(copy, columns, lanes):
+            copy(out=result_woven[:, columns, lanes].rearrange("p (c i) j -> p c j i", i=2),
+                 in_=result[:, lanes, columns].rearrange("p j (c i) -> p c j i", i=2))
+
         def finish(k):
             quantise(dg_q, dg, block(k))
             acc = bank(k)
@@ -339,13 +343,13 @@ def tile_attend_gglu_x_pl_kernel(tc, xT, wg, wu, dyT, wd, us, tg, tu, wt, offs, 
         gate_gradient(3)
         finish(2)
         finish(3)
+        weave_result(on_vector, slice(0, N), slice(0, 2))
 
         out_codes = tile("out_codes", [P, N], U32)
         out_scales = tile("out_scales", [P, N], U8)
         codes_hbm = out_1[0].rearrange("p c lane -> p (c lane)").bitcast(I32)
-        for copy, columns in ((on_vector, slice(0, N // 4)), (on_vector, slice(N // 4, N // 2)), (on_vector, slice(N // 2, 11 * N // 16)), (on_scalar, slice(11 * N // 16, N))):
-            copy(out=result_woven[:, columns, :].rearrange("p (c i) j -> p c j i", i=RUN),
-                 in_=result[:, :, columns].rearrange("p j (c i) -> p c j i", i=RUN))
+        for copy, columns in ((on_vector, slice(0, N // 4)), (on_vector, slice(N // 4, N // 2)), (on_vector, slice(N // 2, 3 * N // 4)), (on_scalar, slice(3 * N // 4, N))):
+            weave_result(copy, columns, slice(2, 4))
         for columns in halves:
             quantise((out_codes, out_scales, E4M3), result_woven, columns)
             nc.sync.dma_start(out=codes_hbm[:, columns], in_=out_codes[:, columns].bitcast(I32))

@@ -121,15 +121,16 @@ def tile_attend_gglu_x_pl_kernel(tc, xT, wg, wu, dyT, wd, us, tg, tu, wt, offs, 
         nc.gpsimd.memset(tu_window[0 : P // 2 - 1, :], 0.0)
         nc.gpsimd.memset(tu_window[P // 2 : P, :], 0.0)
 
-        us_rows = tile("us_rows", [P, LANES], F32)
-        wt_rows = tile("wt_rows", [P, LANES], F32)
+        row_scales = tile("row_scales", [P, N], F32)
+        nc.gpsimd.memset(row_scales[0 : P // 2 - 1, :], 0.0)
+        nc.gpsimd.memset(row_scales[P // 2 : P - 1, :], 0.0)
 
         wg_window = [load_plane("wg", wg, "gate_up", 0)]
         nc.sync.dma_start(offsets[:], offs)
         nc.sync.dma_start(out=tg_window[P - 1 : P, :], in_=tg[P - 1 : P, :])
         nc.sync.dma_start(out=tu_window[P // 2 - 1 : P // 2, :], in_=tu[0:1, :])
-        nc.sync.dma_start(out=us_rows[:], in_=us.rearrange("(m t) o -> m (t o)", t=LANES))
-        nc.sync.dma_start(out=wt_rows[:], in_=wt.rearrange("(m t) o -> m (t o)", t=LANES))
+        nc.sync.dma_start(out=row_scales[P // 2 - 1 : P // 2, :], in_=us.rearrange("r o -> o r"))
+        nc.sync.dma_start(out=row_scales[P - 1 : P, :], in_=wt.rearrange("r o -> o r"))
         wg_window.extend(load_plane("wg", wg, "gate_up", j) for j in range(1, LANES))
         x_raw = load_rows("x", xT)
         dy_raw = load_rows("dy", dyT)
@@ -167,6 +168,13 @@ def tile_attend_gglu_x_pl_kernel(tc, xT, wg, wu, dyT, wd, us, tg, tu, wt, offs, 
             quantise(wg_q, wg_woven, columns)
         wu_window = load_planes("wu", wu, "gate_up")
 
+        acc = bank(2)
+        for k in range(LANES):
+            nc.tensor.transpose(acc[:, block(k)], row_scales[:, k:N:LANES], ident[:])
+        us_rows = tile("us_rows", [P, LANES], F32)
+        wt_rows = tile("wt_rows", [P, LANES], F32)
+        nc.scalar.copy(out=us_rows[:], in_=acc[:, P // 2 - 1 : N : P])
+        nc.scalar.copy(out=wt_rows[:], in_=acc[:, P - 1 : N : P])
         wt_us = tile("wt_us", [P, LANES], F32)
         wt_us2 = tile("wt_us2", [P, LANES], F32)
         nc.gpsimd.tensor_tensor(out=wt_us[:], in0=us_rows[:], in1=wt_rows[:], op=ALU.mult)
@@ -339,9 +347,10 @@ def tile_attend_gglu_x_pl_kernel(tc, xT, wg, wu, dyT, wd, us, tg, tu, wt, offs, 
         for k in range(2):
             quantise_into(du_q, block(k), du_early[k][:])
             finish(k)
-        quantise_into(du_q, halves[1], du_late)
-        gate_gradient(3)
+        quantise_into(du_q, block(2), du_late[:, block(0), :])
         finish(2)
+        gate_gradient(3)
+        quantise_into(du_q, block(3), du_late[:, block(1), :])
         finish(3)
         weave_result(on_vector, slice(0, N), slice(0, 2))
 

@@ -76,8 +76,8 @@ def tile_attend_gglu_x_pl_kernel(tc, xT, wg, wu, dyT, wd, us, tg, tu, wt, offs, 
             for copy, share in ((on_vector, slice(0, split)), (on_scalar, slice(split, P))):
                 if share.start == share.stop:
                     continue
-                copy(out=woven[:, :, :].rearrange("p (t q) j -> p q j t", t=LANES)[:, share, :, :],
-                     in_=planes[:].rearrange("p (j q t) -> p q j t", j=LANES, t=LANES)[:, share, :, :])
+                copy(out=woven[:, :, :].rearrange("p (t q) (h e) -> p q h t e", t=LANES, e=2)[:, share, :, :, :],
+                     in_=planes[:].rearrange("p (h e q t) -> p q h t e", h=2, e=2, t=LANES)[:, share, :, :, :])
 
         def gather_in_halves(planes, window, j):
             for h in range(2):
@@ -86,8 +86,8 @@ def tile_attend_gglu_x_pl_kernel(tc, xT, wg, wu, dyT, wd, us, tg, tu, wt, offs, 
 
         def deal_part(copy, woven, planes, h, lanes):
             groups = slice(h * P // 2, (h + 1) * P // 2)
-            copy(out=woven[:, :, :].rearrange("p (t q) j -> p q j t", t=LANES)[:, groups, :, lanes],
-                 in_=planes[:].rearrange("p (j q t) -> p q j t", j=LANES, t=LANES)[:, groups, :, lanes])
+            copy(out=woven[:, :, :].rearrange("p (t q) (h e) -> p q h t e", t=LANES, e=2)[:, groups, :, lanes, :],
+                 in_=planes[:].rearrange("p (h e q t) -> p q h t e", h=2, e=2, t=LANES)[:, groups, :, lanes, :])
 
         def turn_pair(b, pair, h):
             acc = bank(b)

@@ -20,7 +20,7 @@ N = P * LANES
 UNITS = 2048
 WORDS = N // 2
 RUN = 2
-SPLIT = 84
+SPLIT = 88
 FLOPS = 5 * 2 * N * N * N
 
 
@@ -69,46 +69,55 @@ def tile_attend_gglu_x_pl_kernel(tc, xT, wg, wu, dyT, wd, us, tg, tu, wt, offs, 
             nc.sync.dma_start(out=raw[:], in_=a.rearrange("(p j) r -> p (j r)", j=LANES))
             return raw
 
-        def gather_plane(pair, window, e):
-            nc.vector.tensor_copy(out=pair[:, N * e : N * (e + 1)], in_=window[:].indirect(offsets[:]))
+        def gather(engine, planes, window, j, part=slice(0, N)):
+            out = planes[:, N * j + part.start : N * j + part.stop]
+            listed_columns = window[:].indirect(offsets[:, part.start // 16 : part.stop // 16])
+            if engine == "vector":
+                nc.vector.tensor_copy(out=out, in_=listed_columns)
+            else:
+                nc.scalar.activation(out=out, in_=listed_columns, func=ACT.Copy)
 
-        def deal(woven, planes, split):
-            for copy, share in ((on_vector, slice(0, split)), (on_scalar, slice(split, P))):
-                if share.start == share.stop:
-                    continue
-                copy(out=woven[:, :, :].rearrange("p (t q) (h e) -> p q h t e", t=LANES, e=2)[:, share, :, :, :],
-                     in_=planes[:].rearrange("p (h e q t) -> p q h t e", h=2, e=2, t=LANES)[:, share, :, :, :])
+        def deal(copy, woven, planes, groups, blocks=slice(0, LANES)):
+            copy(out=woven[:, :, :].rearrange("p (t q) (h e) -> p q h t e", t=LANES, e=2)[:, groups, :, blocks, :],
+                 in_=planes[:].rearrange("p (h e q t) -> p q h t e", h=2, e=2, t=LANES)[:, groups, :, blocks, :])
 
-        def gather_in_halves(planes, window, j):
-            for h in range(2):
-                nc.vector.tensor_copy(out=planes[:, N * j + h * N // 2 : N * j + (h + 1) * N // 2],
-                                      in_=window[:].indirect(offsets[:, 16 * h : 16 * (h + 1)]))
+        def deal_shared(woven, planes, first=0):
+            for blocks in (slice(0, 2), slice(2, LANES)):
+                deal(on_vector, woven, planes, slice(first, SPLIT), blocks)
+                deal(on_scalar, woven, planes, slice(SPLIT, P), blocks)
 
-        def deal_part(copy, woven, planes, h, lanes):
-            groups = slice(h * P // 2, (h + 1) * P // 2)
-            copy(out=woven[:, :, :].rearrange("p (t q) (h e) -> p q h t e", t=LANES, e=2)[:, groups, :, lanes, :],
-                 in_=planes[:].rearrange("p (h e q t) -> p q h t e", h=2, e=2, t=LANES)[:, groups, :, lanes, :])
+        def last_plane(q, woven, planes, window):
+            for engine, quarter in (("vector", 0), ("scalar", 2), ("vector", 1), ("scalar", 3)):
+                gather(engine, planes, window, LANES - 1, block(quarter))
+            deal(on_vector, woven, planes, slice(0, P // LANES))
+            deal_shared(woven, planes, P // LANES)
+            for columns in halves:
+                quantise(q, woven, columns)
 
-        def turn_pair(b, pair, h):
+        def turn_pair(name, b, planes, h):
             acc = bank(b)
-            words = pair[:, 2 * N * h : 2 * N * (h + 1)].bitcast(F32)
+            words = planes[:, 2 * N * h : 2 * N * (h + 1)].bitcast(F32)
             for e in range(2):
                 for u in range(2):
                     nc.tensor.transpose(acc[:, block(2 * e + u)], words[:, WORDS * e + u : WORDS * (e + 1) : 2], ident[:])
-            return acc
+            turned = tile("%s_turned%d" % (name, h), [P, N // 2, LANES], BF16)
+            nc.scalar.copy(out=flat(turned[:]).bitcast(F32).rearrange("q (e p u) -> q e p u", e=2, u=2),
+                           in_=acc[:].rearrange("q (e u p) -> q e p u", e=2, u=2))
+            return turned
 
-        def store_turned(acc, turned, h):
-            half = flat(turned[:, halves[h], :]).bitcast(F32).rearrange("q (e p u) -> q e p u", e=2, u=2)
-            nc.scalar.copy(out=half, in_=acc[:].rearrange("q (e u p) -> q e p u", e=2, u=2))
+        def quantise_into(q, columns, woven):
+            nc.vector.quantize_mx(out=q[0][:, columns].bitcast(q[2]), scales=q[1][:, columns], in_=flat(woven))
 
-
-        def spread(name, columns, b):
+        def spread(columns, b):
             acc = bank(b)
             for k in range(LANES):
                 nc.tensor.transpose(acc[:, block(k)], columns[:, k : k + 1].to_broadcast([P, P]), ident[:])
-            full = tile(name, [P, N], F32)
-            nc.scalar.copy(out=full[:], in_=acc[:])
-            return full
+            return acc
+
+        def scaled(name, columns, factor):
+            out = tile(name, [P, LANES], F32)
+            nc.gpsimd.tensor_scalar(out=out[:], in0=columns[:], scalar1=factor, scalar2=0.0, op0=ALU.mult, op1=ALU.add)
+            return out
 
         halves = [slice(0, N // 2), slice(N // 2, N)]
 
@@ -121,23 +130,29 @@ def tile_attend_gglu_x_pl_kernel(tc, xT, wg, wu, dyT, wd, us, tg, tu, wt, offs, 
         nc.gpsimd.memset(tu_window[0 : P // 2 - 1, :], 0.0)
         nc.gpsimd.memset(tu_window[P // 2 : P, :], 0.0)
 
-        row_scales = tile("row_scales", [P, N], F32)
-        nc.gpsimd.memset(row_scales[0 : P // 2 - 1, :], 0.0)
-        nc.gpsimd.memset(row_scales[P // 2 : P - 1, :], 0.0)
-
         wg_window = [load_plane("wg", wg, "gate_up", 0)]
         nc.sync.dma_start(offsets[:], offs)
         nc.sync.dma_start(out=tg_window[P - 1 : P, :], in_=tg[P - 1 : P, :])
         nc.sync.dma_start(out=tu_window[P // 2 - 1 : P // 2, :], in_=tu[0:1, :])
-        nc.sync.dma_start(out=row_scales[P // 2 - 1 : P // 2, :], in_=us.rearrange("r o -> o r"))
-        nc.sync.dma_start(out=row_scales[P - 1 : P, :], in_=wt.rearrange("r o -> o r"))
+        us_rows = tile("us_rows", [P, LANES], F32)
+        wt_rows = tile("wt_rows", [P, LANES], F32)
+        nc.sync.dma_start(out=us_rows[:], in_=us.rearrange("(m k) o -> m (k o)", k=LANES))
+        nc.sync.dma_start(out=wt_rows[:], in_=wt.rearrange("(m k) o -> m (k o)", k=LANES))
         wg_window.extend(load_plane("wg", wg, "gate_up", j) for j in range(1, LANES))
         x_raw = load_rows("x", xT)
         dy_raw = load_rows("dy", dyT)
         wd_window = load_planes("wd", wd, "down")
 
+        wt_us = tile("wt_us", [P, LANES], F32)
+        wt_us2 = tile("wt_us2", [P, LANES], F32)
+        nc.gpsimd.tensor_tensor(out=wt_us[:], in0=us_rows[:], in1=wt_rows[:], op=ALU.mult)
+        nc.gpsimd.tensor_tensor(out=wt_us2[:], in0=wt_us[:], in1=us_rows[:], op=ALU.mult)
+        us_full = tile("us_full", [P, N], F32)
+        nc.scalar.copy(out=us_full[:], in_=spread(us_rows, 7)[:])
+        row_factor = spread(wt_us2, 4)
+
         wg_planes = tile("wg_planes", [P, LANES * N], BF16)
-        gather_plane(wg_planes, wg_window[0], 0)
+        gather("vector", wg_planes, wg_window[0], 0)
         listed = {}
         for name, window, b, live in (("tg", tg_window, 0, P - 1), ("tu", tu_window, 1, P // 2 - 1)):
             row = tile(name + "_row", [P, N], F32)
@@ -147,99 +162,78 @@ def tile_attend_gglu_x_pl_kernel(tc, xT, wg, wu, dyT, wd, us, tg, tu, wt, offs, 
                 nc.tensor.transpose(acc[:, block(t)], row[:, t:N:LANES], ident[:])
             listed[name] = tile(name + "_columns", [P, LANES], F32)
             nc.scalar.copy(out=listed[name][:], in_=acc[:, live:N:P])
-
-        wg_woven = tile("wg_woven", [P, N, LANES], BF16)
-        wg_turned = tile("wg_turned", [P, N, LANES], BF16)
+            if name == "tg":
+                half_tg, less_tg = tile("half_tg", [P, LANES], F32), tile("less_tg", [P, LANES], F32)
+                nc.scalar.activation(out=half_tg[:], in_=acc[:, live:N:P], func=ACT.Copy, scale=0.5)
+                nc.scalar.activation(out=less_tg[:], in_=acc[:, live:N:P], func=ACT.Copy, scale=-1.0)
         tgtu = tile("tgtu", [P, LANES], F32)
         nc.gpsimd.tensor_tensor(out=tgtu[:], in0=listed["tg"][:], in1=listed["tu"][:], op=ALU.mult)
-        less_tgtu = tile("less_tgtu", [P, LANES], F32)
-        nc.gpsimd.tensor_scalar(out=less_tgtu[:], in0=tgtu[:], scalar1=-1.0, scalar2=0.0, op0=ALU.mult, op1=ALU.add)
-        less_tg = tile("less_tg", [P, LANES], F32)
-        nc.gpsimd.tensor_scalar(out=less_tg[:], in0=listed["tg"][:], scalar1=-1.0, scalar2=0.0, op0=ALU.mult, op1=ALU.add)
-        gather_plane(wg_planes, wg_window[1], 1)
-        store_turned(turn_pair(4, wg_planes, 0), wg_turned, 0)
-        gather_plane(wg_planes, wg_window[2], 2)
-        gather_in_halves(wg_planes, wg_window[3], 3)
-        deal_part(on_vector, wg_woven, wg_planes, 0, slice(0, LANES))
-        for g in range(2):
-            deal_part(on_vector, wg_woven, wg_planes, 1, slice(2 * g, 2 * g + 2))
+        half_tgtu, less_half_tgtu = scaled("half_tgtu", tgtu, 0.5), scaled("less_half_tgtu", tgtu, -0.5)
+
+        gather("vector", wg_planes, wg_window[1], 1)
+        wg_turned_early = turn_pair("wg", 5, wg_planes, 0)
+        gather("vector", wg_planes, wg_window[2], 2)
+        wg_woven = tile("wg_woven", [P, N, LANES], BF16)
         wg_q = operand("wg", E4M3)
-        for columns in halves:
-            quantise(wg_q, wg_woven, columns)
+        last_plane(wg_q, wg_woven, wg_planes, wg_window[3])
+        wg_turned_late = turn_pair("wg", 6, wg_planes, 1)
         wu_window = load_planes("wu", wu, "gate_up")
 
-        acc = bank(2)
-        for k in range(LANES):
-            nc.tensor.transpose(acc[:, block(k)], row_scales[:, k:N:LANES], ident[:])
-        us_rows = tile("us_rows", [P, LANES], F32)
-        wt_rows = tile("wt_rows", [P, LANES], F32)
-        nc.scalar.copy(out=us_rows[:], in_=acc[:, P // 2 - 1 : N : P])
-        nc.scalar.copy(out=wt_rows[:], in_=acc[:, P - 1 : N : P])
-        wt_us = tile("wt_us", [P, LANES], F32)
-        wt_us2 = tile("wt_us2", [P, LANES], F32)
-        nc.gpsimd.tensor_tensor(out=wt_us[:], in0=us_rows[:], in1=wt_rows[:], op=ALU.mult)
-        nc.gpsimd.tensor_tensor(out=wt_us2[:], in0=wt_us[:], in1=us_rows[:], op=ALU.mult)
-        us_full = spread("us_full", us_rows, 6)
         x_woven = tile("x_woven", [P, N, LANES], BF16)
-        deal_part(on_scalar, x_woven, x_raw, 0, slice(0, LANES))
-        for g in range(2):
-            deal_part(on_vector, x_woven, x_raw, 1, slice(2 * g, 2 * g + 2))
+        deal_shared(x_woven, x_raw)
         x_q = operand("x", E4M3)
         for columns in halves:
             quantise(x_q, x_woven, columns)
-        store_turned(turn_pair(5, wg_planes, 1), wg_turned, 1)
         wg_turned_q = operand("wg_turned", E4M3, "x_woven")
-        quantise(wg_turned_q, wg_turned)
-
-        dy_woven = tile("dy_woven", [P, N, LANES], BF16)
-        deal(dy_woven, dy_raw, P // 2)
-
-        dy_q = operand("dy", E5M2)
-        quantise(dy_q, dy_woven)
+        quantise_into(wg_turned_q, halves[0], wg_turned_early[:])
+        quantise_into(wg_turned_q, halves[1], wg_turned_late[:])
 
         ag = []
         z = tile("z", [P, LANES, N], F32)
-        sig = tile("sig", [P, LANES, N], F32)
-        ag_scaled = tile("ag_scaled", [P, LANES - 1, N], F32, "tu_window")
-        up_factor = tile("up_factor", [P, LANES, N], F32, "dy_woven")
+        silu = tile("silu", [P, LANES, N], F32)
+        tanh = tile("tanh", [P, LANES, N], F32)
         for t in range(LANES):
             ag.append(bank(t))
             product(ag[t][:], wg_q, t, x_q)
             nc.vector.tensor_tensor(out=z[:, t, :], in0=ag[t][:], in1=us_full[:], op=ALU.mult)
-            nc.scalar.activation(out=sig[:, t, :], in_=z[:, t, :], func=ACT.Sigmoid, scale=listed["tg"][:, t : t + 1])
-            if t < LANES - 1:
-                nc.scalar.activation(out=ag_scaled[:, t, :], in_=ag[t][:], func=ACT.Copy, scale=tgtu[:, t : t + 1])
-                nc.gpsimd.tensor_tensor(out=up_factor[:, t, :], in0=sig[:, t, :], in1=ag_scaled[:, t, :], op=ALU.mult)
-            else:
-                nc.vector.scalar_tensor_tensor(out=up_factor[:, t, :], in0=ag[t][:], scalar=tgtu[:, t : t + 1], in1=sig[:, t, :],
-                                               op0=ALU.mult, op1=ALU.mult)
-
-        wd_planes = tile("wd_planes", [P, LANES * N], BF16)
-        gate_bytes = tile("gate_part", [P, LANES * N], F32, "tg_window")
-        gate_part = gate_bytes[:].rearrange("q (t r) -> q t r", t=LANES)
-        wd_woven = gate_bytes[:, N : 3 * N].bitcast(BF16).rearrange("p (c j) -> p c j", j=LANES)
-        gather_plane(wd_planes, wd_window[0], 0)
-        gather_plane(wd_planes, wd_window[1], 1)
-        gather_plane(wd_planes, wd_window[2], 2)
-        gather_in_halves(wd_planes, wd_window[3], 3)
-        deal_part(on_vector, wd_woven, wd_planes, 0, slice(0, LANES))
-        for g in range(2):
-            deal_part(on_vector, wd_woven, wd_planes, 1, slice(2 * g, 2 * g + 2))
-        wd_q = operand("wd", E4M3)
-        for columns in halves:
-            quantise(wd_q, wd_woven, columns)
-
-        silu = tile("silu", [P, LANES, N], F32, "tg_columns")
-        slope = tile("slope", [P, LANES, N], F32)
-        for t in range(LANES):
             nc.scalar.activation(out=silu[:, t, :], in_=z[:, t, :], func=ACT.Silu, scale=less_tg[:, t : t + 1])
-            nc.scalar.activation(out=slope[:, t, :], in_=silu[:, t, :], func=ACT.Identity,
-                                 scale=less_tgtu[:, t : t + 1], bias=tgtu[:, t : t + 1])
-        for lanes in (slice(0, 1), slice(1, LANES)):
-            nc.gpsimd.tensor_tensor(out=gate_part[:, lanes, :], in0=slope[:, lanes, :], in1=sig[:, lanes, :], op=ALU.mult)
+        for t in range(LANES):
+            nc.scalar.activation(out=tanh[:, t, :], in_=z[:, t, :], func=ACT.Tanh, scale=half_tg[:, t : t + 1])
 
-        wu_planes = tile("wu_planes", [P, LANES * N], BF16)
-        wu_woven = tile("wu_woven", [P, N, LANES], BF16)
+        dy_woven = tile("dy_woven", [P, N, LANES], BF16)
+        dy_q = operand("dy", E5M2)
+        for blocks in (slice(0, 2), slice(2, LANES)):
+            deal(on_vector, dy_woven, dy_raw, slice(0, P), blocks)
+        for columns in halves:
+            quantise(dy_q, dy_woven, columns)
+
+        slope = tile("slope", [P, LANES, N], F32, "dy_woven")
+        sig = tile("sig", [P, LANES, N], F32, "dy_raw")
+        up_factor = tile("up_factor", [P, LANES, N], F32, "tg_window")
+        for t in range(LANES):
+            nc.gpsimd.tensor_scalar(out=slope[:, t, :], in0=silu[:, t, :], scalar1=less_half_tgtu[:, t : t + 1],
+                                    scalar2=half_tgtu[:, t : t + 1], op0=ALU.mult, op1=ALU.add)
+            nc.vector.scalar_tensor_tensor(out=sig[:, t, :], in0=tanh[:, t, :], scalar=1.0, in1=row_factor[:],
+                                           op0=ALU.add, op1=ALU.mult)
+        for t in range(LANES):
+            nc.vector.scalar_tensor_tensor(out=up_factor[:, t, :], in0=ag[t][:], scalar=half_tgtu[:, t : t + 1], in1=sig[:, t, :],
+                                           op0=ALU.mult, op1=ALU.mult)
+
+        def gate_parts(name, tag, pair):
+            parts = tile(name, [P, 2, LANES, P], F32, tag)
+            for i in range(2):
+                rows = block(2 * pair + i)
+                nc.gpsimd.tensor_tensor(out=parts[:, i, :, :], in0=slope[:, :, rows], in1=sig[:, :, rows], op=ALU.mult)
+            return [parts[:, i, :, :] for i in range(2)]
+
+        gate_part = gate_parts("gate_part_low", None, 0)
+        wd_planes = tile("wd_planes", [P, LANES * N], BF16)
+        wd_woven = tile("wd_woven", [P, N, LANES], BF16)
+        wd_q = operand("wd", E4M3)
+        for j in range(LANES - 1):
+            gather("scalar", wd_planes, wd_window[j], j)
+        last_plane(wd_q, wd_woven, wd_planes, wd_window[3])
+        gate_part.extend(gate_parts("gate_part_high", "wd_woven", 1))
 
         def by_runs(woven, k):
             return woven[:, block(k), :].rearrange("q (c i) t -> q c t i", i=RUN)
@@ -251,65 +245,43 @@ def tile_attend_gglu_x_pl_kernel(tc, xT, wg, wu, dyT, wd, us, tg, tu, wt, offs, 
             return acc[:, :].rearrange("q (t m) -> q t m", t=LANES)
 
         dh = []
-        gate_low = tile("gate_low", [P, 2, LANES, P], F32)
+        du = tile("du", [P, N, LANES], BF16)
         for k in range(LANES):
-            acc = bank(LANES + k % 3)
-            product(acc[:], dy_q, k, wd_q)
-            rows = tile("dh_rows%d" % k, [P, N], F32)
-            nc.scalar.activation(out=rows[:], in_=acc[:], func=ACT.Copy, scale=wt_us2[:, k : k + 1])
-            dh.append(bank(k))
+            dh.append(bank(LANES + k))
             for t in range(LANES):
-                nc.tensor.transpose(dh[k][:, block(t)], rows[:, block(t)], ident[:])
-
-        def up_gradient(woven, k):
-            nc.vector.tensor_tensor(out=woven.rearrange("q (c i) t -> q c t i", i=RUN), in0=lanes_by_runs(by_lane(dh[k])),
+                product(dh[k][:, block(t)], wd_q, t, dy_q, block(k))
+            nc.vector.tensor_tensor(out=by_runs(du, k), in0=lanes_by_runs(by_lane(dh[k])),
                                     in1=lanes_by_runs(up_factor[:, :, block(k)]), op=ALU.mult)
+        gate_factor = tile("gate_factor", [P, LANES, LANES, P], F32, "z")
+        for k in range(LANES):
+            nc.vector.tensor_tensor(out=gate_factor[:, k, :, :], in0=by_lane(dh[k]), in1=gate_part[k], op=ALU.mult)
 
-        def quantise_into(q, columns, woven):
-            nc.vector.quantize_mx(out=q[0][:, columns].bitcast(q[2]), scales=q[1][:, columns], in_=flat(woven))
-
-        gather_plane(wu_planes, wu_window[0], 0)
-        du_early = []
-        turned = tile("dh_turned_low", [P, 2, N], F32)
-        for k in range(2):
-            gather_plane(wu_planes, wu_window[1 + k], 1 + k)
-            du_early.append(tile("du%d" % k, [P, P, LANES], BF16, "gate_up%d" % (1 + k)))
-            if k == 0:
-                up_gradient(du_early[k][:], k)
-            nc.scalar.copy(out=turned[:, k, :], in_=dh[k][:])
-            nc.gpsimd.tensor_tensor(out=gate_low[:, k, :, :], in0=by_lane(turned[:, k, :]), in1=gate_part[:, :, block(k)], op=ALU.mult)
-            if k == 1:
-                up_gradient(du_early[k][:], k)
-
-        dh_copies = {}
-        for k in (2, 3):
-            dh_copies[k] = tile("dh_turned%d" % k, [P, N], F32)
-            nc.scalar.copy(out=dh_copies[k][:], in_=dh[k][:])
-
-        gather_in_halves(wu_planes, wu_window[3], 3)
-        deal_part(on_scalar, wu_woven, wu_planes, 0, slice(0, LANES))
-        for g in range(2):
-            deal_part(on_vector, wu_woven, wu_planes, 1, slice(2 * g, 2 * g + 2))
+        wu_planes = tile("wu_planes", [P, LANES * N], BF16)
+        wu_woven = tile("wu_woven", [P, N, LANES], BF16)
         wu_q = operand("wu", E4M3)
+        wu_turned_q = operand("wu_turned", E4M3)
+        du_q = operand("du", E5M2)
+        for j in range(2):
+            gather("scalar", wu_planes, wu_window[j], j)
+        wu_turned_early = turn_pair("wu", 0, wu_planes, 0)
+        gather("scalar", wu_planes, wu_window[2], 2)
         for columns in halves:
-            quantise(wu_q, wu_woven, columns)
-        turns = [turn_pair(6 + h, wu_planes, h) for h in range(2)]
-        wu_turned = tile("wu_turned", [P, N, LANES], BF16, "wu_planes")
-        for h in range(2):
-            store_turned(turns[h], wu_turned, h)
+            quantise(du_q, du, columns)
+        quantise_into(wu_turned_q, halves[0], wu_turned_early[:])
+        sums = []
+        for k in range(LANES):
+            sums.append(bank(LANES + k))
+            product(sums[k][:, halves[0]], du_q, k, wu_turned_q, halves[0], start=True, stop=False)
 
+        last_plane(wu_q, wu_woven, wu_planes, wu_window[3])
+        quantise_into(wu_turned_q, halves[1], turn_pair("wu", 3, wu_planes, 1)[:])
         au = []
         for k in range(LANES):
-            au.append(bank(LANES + k))
+            au.append(bank(k))
             for t in range(LANES):
                 product(au[k][:, block(t)], wu_q, t, x_q, block(k))
-
-        behind = tile("behind_wu", [P, 3 * N], F32, "wu_woven")
-        du_late = behind[:, 0:N].bitcast(BF16).rearrange("q (c t) -> q c t", t=LANES)
-        gate_high = behind[:, N : 3 * N].rearrange("q (k t m) -> q k t m", t=LANES, m=P)
-        gate_factor = [(gate_low, gate_high)[k // 2][:, k % 2, :, :] for k in range(LANES)]
-        du_q = operand("du", E5M2, "gate_up3")
-        wu_turned_q = operand("wu_turned", E4M3)
+        for k in range(LANES):
+            product(sums[k][:, halves[1]], du_q, k, wu_turned_q, halves[1], start=False, stop=False)
 
         result = tile("result", [P, LANES, N], F32)
         result_woven = tile("result_woven", [P, N, LANES], BF16)
@@ -317,18 +289,16 @@ def tile_attend_gglu_x_pl_kernel(tc, xT, wg, wu, dyT, wd, us, tg, tu, wt, offs, 
         dg = tile("dg", [P, N, LANES], BF16)
         dg_q = operand("dg", E5M2)
 
-        def gate_gradient(k):
-            nc.vector.tensor_tensor(out=by_runs(dg, k), in0=lanes_by_runs(by_lane(au[k])),
-                                    in1=lanes_by_runs(gate_factor[k]), op=ALU.mult)
+        def gate_gradient(k, part=slice(0, P // RUN)):
+            nc.vector.tensor_tensor(out=by_runs(dg, k)[:, part, :, :], in0=lanes_by_runs(by_lane(au[k]))[:, part, :, :],
+                                    in1=lanes_by_runs(gate_factor[:, k, :, :])[:, part, :, :], op=ALU.mult)
 
         def weave_result(copy, columns, lanes):
             copy(out=result_woven[:, columns, lanes].rearrange("p (c i) j -> p c j i", i=2),
                  in_=result[:, lanes, columns].rearrange("p j (c i) -> p c j i", i=2))
 
         def finish(k):
-            quantise(dg_q, dg, block(k))
-            acc = bank(k)
-            product(acc[:], du_q, k, wu_turned_q, start=True, stop=False)
+            acc = sums[k]
             product(acc[:], dg_q, k, wg_turned_q, start=False, stop=True)
             by_feature = result[:, k, :].rearrange("m (c i j) -> m c j i", i=2, j=LANES)
             by_plane = acc[:].rearrange("m (j c i) -> m c j i", i=2, j=LANES)
@@ -336,22 +306,18 @@ def tile_attend_gglu_x_pl_kernel(tc, xT, wg, wu, dyT, wd, us, tg, tu, wt, offs, 
                 nc.scalar.copy(out=by_feature[:, rows, :, :], in_=by_plane[:, rows, :, :])
             nc.sync.dma_start(out=out_rows[:, k, :], in_=result[:, k, :])
 
-        for k in (2, 3):
-            nc.gpsimd.tensor_tensor(out=gate_factor[k], in0=by_lane(dh_copies[k]), in1=gate_part[:, :, block(k)], op=ALU.mult)
-            up_gradient(du_late[:, block(k - 2), :], k)
-        for k in range(3):
+        gate_gradient(0)
+        for k in range(1, LANES - 1):
             gate_gradient(k)
-            if k > 0:
-                product(bank(LANES + k)[:], x_q, 0, wg_q)
-        quantise(wu_turned_q, wu_turned)
-        for k in range(2):
-            quantise_into(du_q, block(k), du_early[k][:])
-            finish(k)
-        quantise_into(du_q, block(2), du_late[:, block(0), :])
-        finish(2)
-        gate_gradient(3)
-        quantise_into(du_q, block(3), du_late[:, block(1), :])
-        finish(3)
+            quantise(dg_q, dg, block(k - 1))
+            finish(k - 1)
+        gate_gradient(LANES - 1, slice(0, P // RUN // 2))
+        quantise(dg_q, dg, block(LANES - 2))
+        finish(LANES - 2)
+        gate_gradient(LANES - 1, slice(P // RUN // 2, P // RUN))
+        for h in range(2):
+            quantise(dg_q, dg, slice(N - P + h * P // 2, N - P + (h + 1) * P // 2))
+        finish(LANES - 1)
         weave_result(on_vector, slice(0, N), slice(0, 2))
 
         out_codes = tile("out_codes", [P, N], U32)

@@ -127,6 +127,8 @@ def tile_attend_gglu_x_pl_kernel(tc, xT, wg, wu, dyT, wd, us, tg, tu, wt, offs, 
         nc.vector.memset(tg_window[0 : P - 1, :], 0.0)
         ident = tile("ident", [P, P], F32)
         make_identity(nc, ident[:])
+        table_warm = tile("table_warm", [P, 1], F32)
+        nc.scalar.activation(out=table_warm[:], in_=ident[:, 0:1], func=ACT.Silu)
         nc.gpsimd.memset(tu_window[0 : P // 2 - 1, :], 0.0)
         nc.gpsimd.memset(tu_window[P // 2 : P, :], 0.0)
 
@@ -140,7 +142,11 @@ def tile_attend_gglu_x_pl_kernel(tc, xT, wg, wu, dyT, wd, us, tg, tu, wt, offs, 
         nc.sync.dma_start(out=wt_rows[:], in_=wt.rearrange("(m k) o -> m (k o)", k=LANES))
         wg_window.extend(load_plane("wg", wg, "gate_up", j) for j in range(1, LANES))
         x_raw = load_rows("x", xT)
-        dy_raw = load_rows("dy", dyT)
+        dy_raw = []
+        for h in range(2):
+            dy_raw.append(tile("dy_raw%d" % h, [P, LANES * N // 2], F32))
+            nc.sync.dma_start(out=dy_raw[h][:].rearrange("p (j r) -> p j r", j=LANES),
+                              in_=dyT.rearrange("(p j) r -> p j r", j=LANES)[:, :, halves[h]])
         wd_window = load_planes("wd", wd, "down")
 
         wt_us = tile("wt_us", [P, LANES], F32)
@@ -188,9 +194,14 @@ def tile_attend_gglu_x_pl_kernel(tc, xT, wg, wu, dyT, wd, us, tg, tu, wt, offs, 
         quantise_into(wg_turned_q, halves[0], wg_turned_early[:])
         quantise_into(wg_turned_q, halves[1], wg_turned_late[:])
 
+        dy_woven = tile("dy_woven", [P, N, LANES], BF16)
+        for h in range(2):
+            nc.scalar.copy(out=dy_woven[:].rearrange("p (t g q) (h e) -> p g q h t e", t=LANES, g=2, e=2)[:, h, :, :, :, :],
+                           in_=dy_raw[h][:].rearrange("p (h e q t) -> p q h t e", h=2, e=2, t=LANES))
+
         ag = []
         z = tile("z", [P, LANES, N], F32)
-        silu = tile("silu", [P, LANES, N], F32)
+        silu = tile("silu", [P, LANES, N], F32, "dy_raw1")
         tanh = tile("tanh", [P, LANES, N], F32)
         for t in range(LANES):
             ag.append(bank(t))
@@ -200,40 +211,43 @@ def tile_attend_gglu_x_pl_kernel(tc, xT, wg, wu, dyT, wd, us, tg, tu, wt, offs, 
         for t in range(LANES):
             nc.scalar.activation(out=tanh[:, t, :], in_=z[:, t, :], func=ACT.Tanh, scale=half_tg[:, t : t + 1])
 
-        dy_woven = tile("dy_woven", [P, N, LANES], BF16)
         dy_q = operand("dy", E5M2)
-        for blocks in (slice(0, 2), slice(2, LANES)):
-            deal(on_vector, dy_woven, dy_raw, slice(0, P), blocks)
         for columns in halves:
             quantise(dy_q, dy_woven, columns)
 
         slope = tile("slope", [P, LANES, N], F32, "dy_woven")
-        sig = tile("sig", [P, LANES, N], F32, "dy_raw")
-        up_factor = tile("up_factor", [P, LANES, N], F32, "tg_window")
+        sig = tile("sig", [P, LANES, N], F32, "tu_window")
         for t in range(LANES):
             nc.gpsimd.tensor_scalar(out=slope[:, t, :], in0=silu[:, t, :], scalar1=less_half_tgtu[:, t : t + 1],
                                     scalar2=half_tgtu[:, t : t + 1], op0=ALU.mult, op1=ALU.add)
             nc.vector.scalar_tensor_tensor(out=sig[:, t, :], in0=tanh[:, t, :], scalar=1.0, in1=row_factor[:],
                                            op0=ALU.add, op1=ALU.mult)
-        for t in range(LANES):
-            nc.vector.scalar_tensor_tensor(out=up_factor[:, t, :], in0=ag[t][:], scalar=half_tgtu[:, t : t + 1], in1=sig[:, t, :],
-                                           op0=ALU.mult, op1=ALU.mult)
 
-        def gate_parts(name, tag, pair):
-            parts = tile(name, [P, 2, LANES, P], F32, tag)
-            for i in range(2):
-                rows = block(2 * pair + i)
-                nc.gpsimd.tensor_tensor(out=parts[:, i, :, :], in0=slope[:, :, rows], in1=sig[:, :, rows], op=ALU.mult)
-            return [parts[:, i, :, :] for i in range(2)]
+        def up_factors(name, tag, h):
+            factors = tile(name, [P, LANES, N // 2], F32, tag)
+            for t in range(LANES):
+                nc.vector.scalar_tensor_tensor(out=factors[:, t, :], in0=ag[t][:, halves[h]], scalar=half_tgtu[:, t : t + 1],
+                                               in1=sig[:, t, halves[h]], op0=ALU.mult, op1=ALU.mult)
+            return [factors[:, :, block(i)] for i in range(2)]
 
-        gate_part = gate_parts("gate_part_low", None, 0)
+        def gate_parts(name, tag, tiles):
+            parts = tile(name, [P, len(tiles), LANES, P], F32, tag)
+            for i, k in enumerate(tiles):
+                nc.gpsimd.tensor_tensor(out=parts[:, i, :, :], in0=slope[:, :, block(k)], in1=sig[:, :, block(k)], op=ALU.mult)
+            return [parts[:, i, :, :] for i in range(len(tiles))]
+
+        up_factor = up_factors("up_factor_low", None, 0)
+        gate_part = gate_parts("gate_part_low", None, [0, 1])
         wd_planes = tile("wd_planes", [P, LANES * N], BF16)
         wd_woven = tile("wd_woven", [P, N, LANES], BF16)
         wd_q = operand("wd", E4M3)
-        for j in range(LANES - 1):
+        for j in range(2):
             gather("scalar", wd_planes, wd_window[j], j)
+        gather("vector", wd_planes, wd_window[2], 2, halves[0])
+        gather("scalar", wd_planes, wd_window[2], 2, halves[1])
         last_plane(wd_q, wd_woven, wd_planes, wd_window[3])
-        gate_part.extend(gate_parts("gate_part_high", "wd_woven", 1))
+        up_factor.extend(up_factors("up_factor_high", "wd_planes", 1))
+        gate_part.extend(gate_parts("gate_part_high", "wd_woven", [2, 3]))
 
         def by_runs(woven, k):
             return woven[:, block(k), :].rearrange("q (c i) t -> q c t i", i=RUN)
@@ -250,11 +264,22 @@ def tile_attend_gglu_x_pl_kernel(tc, xT, wg, wu, dyT, wd, us, tg, tu, wt, offs, 
             dh.append(bank(LANES + k))
             for t in range(LANES):
                 product(dh[k][:, block(t)], wd_q, t, dy_q, block(k))
+            if k == LANES - 1:
+                dh_last = tile("dh_last", [P, N], F32)
+                nc.scalar.copy(out=dh_last[:], in_=dh[k][:])
             nc.vector.tensor_tensor(out=by_runs(du, k), in0=lanes_by_runs(by_lane(dh[k])),
-                                    in1=lanes_by_runs(up_factor[:, :, block(k)]), op=ALU.mult)
-        gate_factor = tile("gate_factor", [P, LANES, LANES, P], F32, "z")
-        for k in range(LANES):
-            nc.vector.tensor_tensor(out=gate_factor[:, k, :, :], in0=by_lane(dh[k]), in1=gate_part[k], op=ALU.mult)
+                                    in1=lanes_by_runs(up_factor[k]), op=ALU.mult)
+
+        def gate_factors(name, tag, tiles):
+            factors = tile(name, [P, len(tiles), LANES, P], F32, tag)
+            for i, k in enumerate(tiles):
+                nc.vector.tensor_tensor(out=factors[:, i, :, :], in0=by_lane(dh[k]), in1=gate_part[k], op=ALU.mult)
+            return [factors[:, i, :, :] for i in range(len(tiles))]
+
+        gate_factor = gate_factors("gate_factor_early", "z", range(LANES - 1))
+        gate_factor_last = tile("gate_factor_last", [P, LANES, P], F32)
+        nc.gpsimd.tensor_tensor(out=gate_factor_last[:], in0=by_lane(dh_last), in1=gate_part[LANES - 1], op=ALU.mult)
+        gate_factor.append(gate_factor_last[:])
 
         wu_planes = tile("wu_planes", [P, LANES * N], BF16)
         wu_woven = tile("wu_woven", [P, N, LANES], BF16)
@@ -274,15 +299,13 @@ def tile_attend_gglu_x_pl_kernel(tc, xT, wg, wu, dyT, wd, us, tg, tu, wt, offs, 
             product(sums[k][:, halves[0]], du_q, k, wu_turned_q, halves[0], start=True, stop=False)
 
         last_plane(wu_q, wu_woven, wu_planes, wu_window[3])
-        quantise_into(wu_turned_q, halves[1], turn_pair("wu", 3, wu_planes, 1)[:])
+        wu_turned_late = turn_pair("wu", 3, wu_planes, 1)
+        quantise_into(wu_turned_q, halves[1], wu_turned_late[:])
         au = []
         for k in range(LANES):
             au.append(bank(k))
             for t in range(LANES):
                 product(au[k][:, block(t)], wu_q, t, x_q, block(k))
-        for k in range(LANES):
-            product(sums[k][:, halves[1]], du_q, k, wu_turned_q, halves[1], start=False, stop=False)
-
         result = tile("result", [P, LANES, N], F32)
         result_woven = tile("result_woven", [P, N, LANES], BF16)
         out_rows = out_0.rearrange("(m t) d -> m t d", t=LANES)
@@ -291,7 +314,7 @@ def tile_attend_gglu_x_pl_kernel(tc, xT, wg, wu, dyT, wd, us, tg, tu, wt, offs, 
 
         def gate_gradient(k, part=slice(0, P // RUN)):
             nc.vector.tensor_tensor(out=by_runs(dg, k)[:, part, :, :], in0=lanes_by_runs(by_lane(au[k]))[:, part, :, :],
-                                    in1=lanes_by_runs(gate_factor[:, k, :, :])[:, part, :, :], op=ALU.mult)
+                                    in1=lanes_by_runs(gate_factor[k])[:, part, :, :], op=ALU.mult)
 
         def weave_result(copy, columns, lanes):
             copy(out=result_woven[:, columns, lanes].rearrange("p (c i) j -> p c j i", i=2),
@@ -307,6 +330,8 @@ def tile_attend_gglu_x_pl_kernel(tc, xT, wg, wu, dyT, wd, us, tg, tu, wt, offs, 
             nc.sync.dma_start(out=out_rows[:, k, :], in_=result[:, k, :])
 
         gate_gradient(0)
+        for k in range(LANES):
+            product(sums[k][:, halves[1]], du_q, k, wu_turned_q, halves[1], start=False, stop=False)
         for k in range(1, LANES - 1):
             gate_gradient(k)
             quantise(dg_q, dg, block(k - 1))

@@ -21,6 +21,7 @@ UNITS = 2048
 WORDS = N // 2
 RUN = 2
 SPLIT = 88
+WU_SHARE = 160
 FLOPS = 5 * 2 * N * N * N
 
 
@@ -94,15 +95,15 @@ def tile_attend_gglu_x_pl_kernel(tc, xT, wg, wu, dyT, wd, us, tg, tu, wt, offs, 
             for columns in halves:
                 quantise(q, woven, columns)
 
-        def turn_pair(name, b, planes, h):
+        def turn_pair(name, b, planes, h, copy=on_scalar, tag=None):
             acc = bank(b)
             words = planes[:, 2 * N * h : 2 * N * (h + 1)].bitcast(F32)
             for e in range(2):
                 for u in range(2):
                     nc.tensor.transpose(acc[:, block(2 * e + u)], words[:, WORDS * e + u : WORDS * (e + 1) : 2], ident[:])
-            turned = tile("%s_turned%d" % (name, h), [P, N // 2, LANES], BF16)
-            nc.scalar.copy(out=flat(turned[:]).bitcast(F32).rearrange("q (e p u) -> q e p u", e=2, u=2),
-                           in_=acc[:].rearrange("q (e u p) -> q e p u", e=2, u=2))
+            turned = tile("%s_turned%d" % (name, h), [P, N // 2, LANES], BF16, tag)
+            copy(out=flat(turned[:]).bitcast(F32).rearrange("q (e p u) -> q e p u", e=2, u=2),
+                 in_=acc[:].rearrange("q (e u p) -> q e p u", e=2, u=2))
             return turned
 
         def quantise_into(q, columns, woven):
@@ -134,8 +135,8 @@ def tile_attend_gglu_x_pl_kernel(tc, xT, wg, wu, dyT, wd, us, tg, tu, wt, offs, 
 
         wg_window = [load_plane("wg", wg, "gate_up", 0)]
         nc.sync.dma_start(offsets[:], offs)
-        nc.sync.dma_start(out=tg_window[P - 1 : P, :], in_=tg[P - 1 : P, :])
-        nc.sync.dma_start(out=tu_window[P // 2 - 1 : P // 2, :], in_=tu[0:1, :])
+        nc.scalar.dma_start(out=tg_window[P - 1 : P, :], in_=tg[P - 1 : P, :])
+        nc.scalar.dma_start(out=tu_window[P // 2 - 1 : P // 2, :], in_=tu[0:1, :])
         us_rows = tile("us_rows", [P, LANES], F32)
         wt_rows = tile("wt_rows", [P, LANES], F32)
         nc.sync.dma_start(out=us_rows[:], in_=us.rearrange("(m k) o -> m (k o)", k=LANES))
@@ -182,7 +183,6 @@ def tile_attend_gglu_x_pl_kernel(tc, xT, wg, wu, dyT, wd, us, tg, tu, wt, offs, 
         wg_woven = tile("wg_woven", [P, N, LANES], BF16)
         wg_q = operand("wg", E4M3)
         last_plane(wg_q, wg_woven, wg_planes, wg_window[3])
-        wg_turned_late = turn_pair("wg", 6, wg_planes, 1)
         wu_window = load_planes("wu", wu, "gate_up")
 
         x_woven = tile("x_woven", [P, N, LANES], BF16)
@@ -190,6 +190,7 @@ def tile_attend_gglu_x_pl_kernel(tc, xT, wg, wu, dyT, wd, us, tg, tu, wt, offs, 
         x_q = operand("x", E4M3)
         for columns in halves:
             quantise(x_q, x_woven, columns)
+        wg_turned_late = turn_pair("wg", 6, wg_planes, 1, on_vector, "x_raw")
         wg_turned_q = operand("wg_turned", E4M3, "x_woven")
         quantise_into(wg_turned_q, halves[0], wg_turned_early[:])
         quantise_into(wg_turned_q, halves[1], wg_turned_late[:])
@@ -201,15 +202,14 @@ def tile_attend_gglu_x_pl_kernel(tc, xT, wg, wu, dyT, wd, us, tg, tu, wt, offs, 
 
         ag = []
         z = tile("z", [P, LANES, N], F32)
-        silu = tile("silu", [P, LANES, N], F32, "dy_raw1")
-        tanh = tile("tanh", [P, LANES, N], F32)
+        silu = tile("silu", [P, LANES, N], F32)
+        tanh = tile("tanh", [P, LANES, N], F32, "dy_raw1")
         for t in range(LANES):
             ag.append(bank(t))
             product(ag[t][:], wg_q, t, x_q)
             nc.vector.tensor_tensor(out=z[:, t, :], in0=ag[t][:], in1=us_full[:], op=ALU.mult)
-            nc.scalar.activation(out=silu[:, t, :], in_=z[:, t, :], func=ACT.Silu, scale=less_tg[:, t : t + 1])
-        for t in range(LANES):
             nc.scalar.activation(out=tanh[:, t, :], in_=z[:, t, :], func=ACT.Tanh, scale=half_tg[:, t : t + 1])
+            nc.scalar.activation(out=silu[:, t, :], in_=z[:, t, :], func=ACT.Silu, scale=less_tg[:, t : t + 1])
 
         dy_q = operand("dy", E5M2)
         for columns in halves:
@@ -223,12 +223,13 @@ def tile_attend_gglu_x_pl_kernel(tc, xT, wg, wu, dyT, wd, us, tg, tu, wt, offs, 
             nc.vector.scalar_tensor_tensor(out=sig[:, t, :], in0=tanh[:, t, :], scalar=1.0, in1=row_factor[:],
                                            op0=ALU.add, op1=ALU.mult)
 
-        def up_factors(name, tag, h):
-            factors = tile(name, [P, LANES, N // 2], F32, tag)
+        def up_factors(name, tag, first, count):
+            rows = slice(P * first, P * (first + count))
+            factors = tile(name, [P, LANES, P * count], F32, tag)
             for t in range(LANES):
-                nc.vector.scalar_tensor_tensor(out=factors[:, t, :], in0=ag[t][:, halves[h]], scalar=half_tgtu[:, t : t + 1],
-                                               in1=sig[:, t, halves[h]], op0=ALU.mult, op1=ALU.mult)
-            return [factors[:, :, block(i)] for i in range(2)]
+                nc.vector.scalar_tensor_tensor(out=factors[:, t, :], in0=ag[t][:, rows], scalar=half_tgtu[:, t : t + 1],
+                                               in1=sig[:, t, rows], op0=ALU.mult, op1=ALU.mult)
+            return [factors[:, :, block(i)] for i in range(count)]
 
         def gate_parts(name, tag, tiles):
             parts = tile(name, [P, len(tiles), LANES, P], F32, tag)
@@ -236,17 +237,17 @@ def tile_attend_gglu_x_pl_kernel(tc, xT, wg, wu, dyT, wd, us, tg, tu, wt, offs, 
                 nc.gpsimd.tensor_tensor(out=parts[:, i, :, :], in0=slope[:, :, block(k)], in1=sig[:, :, block(k)], op=ALU.mult)
             return [parts[:, i, :, :] for i in range(len(tiles))]
 
-        up_factor = up_factors("up_factor_low", None, 0)
+        up_factor = up_factors("up_factor_low", None, 0, LANES - 1)
         gate_part = gate_parts("gate_part_low", None, [0, 1])
         wd_planes = tile("wd_planes", [P, LANES * N], BF16)
         wd_woven = tile("wd_woven", [P, N, LANES], BF16)
         wd_q = operand("wd", E4M3)
         for j in range(2):
             gather("scalar", wd_planes, wd_window[j], j)
-        gather("vector", wd_planes, wd_window[2], 2, halves[0])
-        gather("scalar", wd_planes, wd_window[2], 2, halves[1])
+        gather("vector", wd_planes, wd_window[2], 2, slice(0, N - P))
+        gather("scalar", wd_planes, wd_window[2], 2, slice(N - P, N))
         last_plane(wd_q, wd_woven, wd_planes, wd_window[3])
-        up_factor.extend(up_factors("up_factor_high", "wd_planes", 1))
+        up_factor.extend(up_factors("up_factor_high", "wd_planes", LANES - 1, 1))
         gate_part.extend(gate_parts("gate_part_high", "wd_woven", [2, 3]))
 
         def by_runs(woven, k):
@@ -258,17 +259,19 @@ def tile_attend_gglu_x_pl_kernel(tc, xT, wg, wu, dyT, wd, us, tg, tu, wt, offs, 
         def by_lane(acc):
             return acc[:, :].rearrange("q (t m) -> q t m", t=LANES)
 
+        wu_planes = tile("wu_planes", [P, LANES * N], BF16)
         dh = []
         du = tile("du", [P, N, LANES], BF16)
         for k in range(LANES):
             dh.append(bank(LANES + k))
             for t in range(LANES):
                 product(dh[k][:, block(t)], wd_q, t, dy_q, block(k))
-            if k == LANES - 1:
-                dh_last = tile("dh_last", [P, N], F32)
-                nc.scalar.copy(out=dh_last[:], in_=dh[k][:])
             nc.vector.tensor_tensor(out=by_runs(du, k), in0=lanes_by_runs(by_lane(dh[k])),
                                     in1=lanes_by_runs(up_factor[k]), op=ALU.mult)
+            if k == 0:
+                gather("scalar", wu_planes, wu_window[0], 0)
+                dh_first = tile("dh_first", [P, N], F32, "gate_up0")
+                nc.scalar.copy(out=dh_first[:], in_=dh[k][:])
 
         def gate_factors(name, tag, tiles):
             factors = tile(name, [P, len(tiles), LANES, P], F32, tag)
@@ -276,23 +279,21 @@ def tile_attend_gglu_x_pl_kernel(tc, xT, wg, wu, dyT, wd, us, tg, tu, wt, offs, 
                 nc.vector.tensor_tensor(out=factors[:, i, :, :], in0=by_lane(dh[k]), in1=gate_part[k], op=ALU.mult)
             return [factors[:, i, :, :] for i in range(len(tiles))]
 
-        gate_factor = gate_factors("gate_factor_early", "z", range(LANES - 1))
-        gate_factor_last = tile("gate_factor_last", [P, LANES, P], F32)
-        nc.gpsimd.tensor_tensor(out=gate_factor_last[:], in0=by_lane(dh_last), in1=gate_part[LANES - 1], op=ALU.mult)
-        gate_factor.append(gate_factor_last[:])
+        gate_factor_first = tile("gate_factor_first", [P, LANES, P], F32)
+        nc.gpsimd.tensor_tensor(out=gate_factor_first[:], in0=by_lane(dh_first), in1=gate_part[0], op=ALU.mult)
+        gate_factor = [gate_factor_first[:]] + gate_factors("gate_factor_rest", "z", range(1, LANES))
 
-        wu_planes = tile("wu_planes", [P, LANES * N], BF16)
         wu_woven = tile("wu_woven", [P, N, LANES], BF16)
         wu_q = operand("wu", E4M3)
         wu_turned_q = operand("wu_turned", E4M3)
         du_q = operand("du", E5M2)
-        for j in range(2):
-            gather("scalar", wu_planes, wu_window[j], j)
+        gather("scalar", wu_planes, wu_window[1], 1)
         wu_turned_early = turn_pair("wu", 0, wu_planes, 0)
-        gather("scalar", wu_planes, wu_window[2], 2)
+        gather("scalar", wu_planes, wu_window[2], 2, slice(WU_SHARE, N))
         for columns in halves:
             quantise(du_q, du, columns)
         quantise_into(wu_turned_q, halves[0], wu_turned_early[:])
+        gather("vector", wu_planes, wu_window[2], 2, slice(0, WU_SHARE))
         sums = []
         for k in range(LANES):
             sums.append(bank(LANES + k))

@@ -21,7 +21,7 @@ UNITS = 2048
 WORDS = N // 2
 RUN = 2
 SPLIT = 88
-WU_SHARE = 160
+LAST_SPLIT = 88
 FLOPS = 5 * 2 * N * N * N
 
 
@@ -40,6 +40,8 @@ def tile_attend_gglu_x_pl_kernel(tc, xT, wg, wu, dyT, wd, us, tg, tu, wt, offs, 
 
         def block(k):
             return slice(P * k, P * (k + 1))
+
+        halves = [slice(0, N // 2), slice(N // 2, N)]
 
         def flat(woven):
             return woven.rearrange("p c j -> p (c j)")
@@ -82,17 +84,23 @@ def tile_attend_gglu_x_pl_kernel(tc, xT, wg, wu, dyT, wd, us, tg, tu, wt, offs, 
             copy(out=woven[:, :, :].rearrange("p (t q) (h e) -> p q h t e", t=LANES, e=2)[:, groups, :, blocks, :],
                  in_=planes[:].rearrange("p (h e q t) -> p q h t e", h=2, e=2, t=LANES)[:, groups, :, blocks, :])
 
-        def deal_shared(woven, planes, first=0):
+        def deal_shared(woven, planes):
             for blocks in (slice(0, 2), slice(2, LANES)):
-                deal(on_vector, woven, planes, slice(first, SPLIT), blocks)
+                deal(on_vector, woven, planes, slice(0, SPLIT), blocks)
                 deal(on_scalar, woven, planes, slice(SPLIT, P), blocks)
 
-        def last_plane(q, woven, planes, window):
-            for engine, quarter in (("vector", 0), ("scalar", 2), ("vector", 1), ("scalar", 3)):
+        def last_plane(q, woven, planes, window, pieces=halves):
+            for engine, quarter in (("vector", 0), ("scalar", 3), ("vector", 1), ("scalar", 2)):
                 gather(engine, planes, window, LANES - 1, block(quarter))
-            deal(on_vector, woven, planes, slice(0, P // LANES))
-            deal_shared(woven, planes, P // LANES)
-            for columns in halves:
+            low, high = slice(0, 2), slice(2, LANES)
+            first, last = P // LANES, P - P // LANES
+            deal(on_vector, woven, planes, slice(0, first))
+            deal(on_scalar, woven, planes, slice(last, P), low)
+            deal(on_vector, woven, planes, slice(first, LAST_SPLIT), low)
+            deal(on_scalar, woven, planes, slice(LAST_SPLIT, last), low)
+            deal(on_vector, woven, planes, slice(first, LAST_SPLIT), high)
+            deal(on_scalar, woven, planes, slice(LAST_SPLIT, P), high)
+            for columns in pieces:
                 quantise(q, woven, columns)
 
         def turn_pair(name, b, planes, h, copy=on_scalar, tag=None):
@@ -104,6 +112,17 @@ def tile_attend_gglu_x_pl_kernel(tc, xT, wg, wu, dyT, wd, us, tg, tu, wt, offs, 
             turned = tile("%s_turned%d" % (name, h), [P, N // 2, LANES], BF16, tag)
             copy(out=flat(turned[:]).bitcast(F32).rearrange("q (e p u) -> q e p u", e=2, u=2),
                  in_=acc[:].rearrange("q (e u p) -> q e p u", e=2, u=2))
+            return turned
+
+        def turn_planes(name, banks, planes, h, tag):
+            turned = tile("%s_turned%d" % (name, h), [P, N // 2, LANES], BF16, tag)
+            for e in range(2):
+                acc = bank(banks[e])
+                words = planes[:, N * (2 * h + e) : N * (2 * h + e + 1)].bitcast(F32)
+                for u in range(2):
+                    nc.tensor.transpose(acc[:, block(u)], words[:, u:WORDS:2], ident[:])
+                nc.scalar.copy(out=flat(turned[:, block(e), :]).bitcast(F32).rearrange("q (p u) -> q p u", u=2),
+                               in_=acc[:, halves[0]].rearrange("q (u p) -> q p u", u=2))
             return turned
 
         def quantise_into(q, columns, woven):
@@ -119,8 +138,6 @@ def tile_attend_gglu_x_pl_kernel(tc, xT, wg, wu, dyT, wd, us, tg, tu, wt, offs, 
             out = tile(name, [P, LANES], F32)
             nc.gpsimd.tensor_scalar(out=out[:], in0=columns[:], scalar1=factor, scalar2=0.0, op0=ALU.mult, op1=ALU.add)
             return out
-
-        halves = [slice(0, N // 2), slice(N // 2, N)]
 
         offsets = sb.tile([P, N // 16], U16, name="offsets")
         tg_window = tile("tg_window", [P, UNITS], F32)
@@ -288,19 +305,18 @@ def tile_attend_gglu_x_pl_kernel(tc, xT, wg, wu, dyT, wd, us, tg, tu, wt, offs, 
         wu_turned_q = operand("wu_turned", E4M3)
         du_q = operand("du", E5M2)
         gather("scalar", wu_planes, wu_window[1], 1)
-        wu_turned_early = turn_pair("wu", 0, wu_planes, 0)
-        gather("scalar", wu_planes, wu_window[2], 2, slice(WU_SHARE, N))
+        wu_turned_early = turn_planes("wu", (0, 1), wu_planes, 0, "gate_up1")
+        gather("scalar", wu_planes, wu_window[2], 2)
         for columns in halves:
             quantise(du_q, du, columns)
         quantise_into(wu_turned_q, halves[0], wu_turned_early[:])
-        gather("vector", wu_planes, wu_window[2], 2, slice(0, WU_SHARE))
         sums = []
         for k in range(LANES):
             sums.append(bank(LANES + k))
             product(sums[k][:, halves[0]], du_q, k, wu_turned_q, halves[0], start=True, stop=False)
 
-        last_plane(wu_q, wu_woven, wu_planes, wu_window[3])
-        wu_turned_late = turn_pair("wu", 3, wu_planes, 1)
+        last_plane(wu_q, wu_woven, wu_planes, wu_window[3], [halves[0], block(2), block(3)])
+        wu_turned_late = turn_planes("wu", (2, 3), wu_planes, 1, "gate_up3")
         quantise_into(wu_turned_q, halves[1], wu_turned_late[:])
         au = []
         for k in range(LANES):

from contextlib import ExitStack

import concourse.mybir as mybir
from concourse.masks import make_identity

F32 = mybir.dt.float32
BF16 = mybir.dt.bfloat16
I32 = mybir.dt.int32
U32 = mybir.dt.uint32
U16 = mybir.dt.uint16
U8 = mybir.dt.uint8
E4M3 = mybir.dt.float8_e4m3fn_x4
E5M2 = mybir.dt.float8_e5m2_x4
ACT = mybir.ActivationFunctionType
ALU = mybir.AluOpType

P = 128
LANES = 4
N = P * LANES
UNITS = 2048
WORDS = N // 2
RUN = 2
SPLIT = 88
LAST_SPLIT = 88
FLOPS = 5 * 2 * N * N * N


def tile_attend_gglu_x_pl_kernel(tc, xT, wg, wu, dyT, wd, us, tg, tu, wt, offs, out_0, out_1, out_2):
    nc = tc.nc
    on_vector, on_scalar = nc.vector.tensor_copy, nc.scalar.copy
    with ExitStack() as ctx:
        sb = ctx.enter_context(tc.tile_pool(name="sb", bufs=1))
        ps = ctx.enter_context(tc.psum_pool(name="ps", bufs=1))

        def tile(name, shape, dtype, tag=None):
            return sb.tile(shape, dtype, name=name, tag=tag or name, align_bytes=64)

        def bank(b):
            return ps.tile([P, N], F32, name="bank%d" % b)

        def block(k):
            return slice(P * k, P * (k + 1))

        halves = [slice(0, N // 2), slice(N // 2, N)]

        def flat(woven):
            return woven.rearrange("p c j -> p (c j)")

        def operand(name, fmt, tag=None):
            return tile(name + "_codes", [P, N], U32, tag), tile(name + "_scales", [P, N], U8), fmt

        def quantise(q, woven, columns=slice(0, N)):
            codes, scales, fmt = q
            nc.vector.quantize_mx(out=codes[:, columns].bitcast(fmt), scales=scales[:, columns], in_=flat(woven[:, columns, :]))

        def product(acc, stationary, k, moving, columns=slice(0, N), start=True, stop=True):
            s_codes, s_scales, s_fmt = stationary
            m_codes, m_scales, m_fmt = moving
            nc.tensor.matmul_mx(out=acc, lhsT=s_codes[:, block(k)].bitcast(s_fmt), lhsT_scale=s_scales[:, block(k)],
                                rhs=m_codes[:, columns].bitcast(m_fmt), rhs_scale=m_scales[:, columns], start=start, stop=stop)

        def load_plane(name, w, tag, j):
            window = tile("%s_window%d" % (name, j), [P, UNITS], F32, tag + str(j))
            nc.sync.dma_start(out=window[:], in_=w.rearrange("(p j) c -> p j c", j=LANES)[:, j, :])
            return window

        def load_planes(name, w, tag):
            return [load_plane(name, w, tag, j) for j in range(LANES)]

        def load_rows(name, a):
            raw = tile(name + "_raw", [P, LANES * N], F32)
            nc.sync.dma_start(out=raw[:], in_=a.rearrange("(p j) r -> p (j r)", j=LANES))
            return raw

        def gather(engine, planes, window, j, part=slice(0, N)):
            out = planes[:, N * j + part.start : N * j + part.stop]
            listed_columns = window[:].indirect(offsets[:, part.start // 16 : part.stop // 16])
            if engine == "vector":
                nc.vector.tensor_copy(out=out, in_=listed_columns)
            else:
                nc.scalar.activation(out=out, in_=listed_columns, func=ACT.Copy)

        def deal(copy, woven, planes, groups, blocks=slice(0, LANES)):
            copy(out=woven[:, :, :].rearrange("p (t q) (h e) -> p q h t e", t=LANES, e=2)[:, groups, :, blocks, :],
                 in_=planes[:].rearrange("p (h e q t) -> p q h t e", h=2, e=2, t=LANES)[:, groups, :, blocks, :])

        def deal_shared(woven, planes):
            for blocks in (slice(0, 2), slice(2, LANES)):
                deal(on_vector, woven, planes, slice(0, SPLIT), blocks)
                deal(on_scalar, woven, planes, slice(SPLIT, P), blocks)

        def last_plane(q, woven, planes, window, pieces=halves):
            for engine, quarter in (("vector", 0), ("scalar", 3), ("vector", 1), ("scalar", 2)):
                gather(engine, planes, window, LANES - 1, block(quarter))
            low, high = slice(0, 2), slice(2, LANES)
            first, last = P // LANES, P - P // LANES
            deal(on_vector, woven, planes, slice(0, first))
            deal(on_scalar, woven, planes, slice(last, P), low)
            deal(on_vector, woven, planes, slice(first, LAST_SPLIT), low)
            deal(on_scalar, woven, planes, slice(LAST_SPLIT, last), low)
            deal(on_vector, woven, planes, slice(first, LAST_SPLIT), high)
            deal(on_scalar, woven, planes, slice(LAST_SPLIT, P), high)
            for columns in pieces:
                quantise(q, woven, columns)

        def turn_pair(name, b, planes, h, copy=on_scalar, tag=None):
            acc = bank(b)
            words = planes[:, 2 * N * h : 2 * N * (h + 1)].bitcast(F32)
            for e in range(2):
                for u in range(2):
                    nc.tensor.transpose(acc[:, block(2 * e + u)], words[:, WORDS * e + u : WORDS * (e + 1) : 2], ident[:])
            turned = tile("%s_turned%d" % (name, h), [P, N // 2, LANES], BF16, tag)
            copy(out=flat(turned[:]).bitcast(F32).rearrange("q (e p u) -> q e p u", e=2, u=2),
                 in_=acc[:].rearrange("q (e u p) -> q e p u", e=2, u=2))
            return turned

        def turn_planes(name, banks, planes, h, tag):
            turned = tile("%s_turned%d" % (name, h), [P, N // 2, LANES], BF16, tag)
            for e in range(2):
                acc = bank(banks[e])
                words = planes[:, N * (2 * h + e) : N * (2 * h + e + 1)].bitcast(F32)
                for u in range(2):
                    nc.tensor.transpose(acc[:, block(u)], words[:, u:WORDS:2], ident[:])
                nc.scalar.copy(out=flat(turned[:, block(e), :]).bitcast(F32).rearrange("q (p u) -> q p u", u=2),
                               in_=acc[:, halves[0]].rearrange("q (u p) -> q p u", u=2))
            return turned

        def quantise_into(q, columns, woven):
            nc.vector.quantize_mx(out=q[0][:, columns].bitcast(q[2]), scales=q[1][:, columns], in_=flat(woven))

        def spread(columns, b):
            acc = bank(b)
            for k in range(LANES):
                nc.tensor.transpose(acc[:, block(k)], columns[:, k : k + 1].to_broadcast([P, P]), ident[:])
            return acc

        def scaled(name, columns, factor):
            out = tile(name, [P, LANES], F32)
            nc.gpsimd.tensor_scalar(out=out[:], in0=columns[:], scalar1=factor, scalar2=0.0, op0=ALU.mult, op1=ALU.add)
            return out

        offsets = sb.tile([P, N // 16], U16, name="offsets")
        tg_window = tile("tg_window", [P, UNITS], F32)
        tu_window = tile("tu_window", [P, UNITS], F32)
        nc.vector.memset(tg_window[0 : P - 1, :], 0.0)
        ident = tile("ident", [P, P], F32)
        make_identity(nc, ident[:])
        table_warm = tile("table_warm", [P, 1], F32)
        nc.scalar.activation(out=table_warm[:], in_=ident[:, 0:1], func=ACT.Silu)
        nc.gpsimd.memset(tu_window[0 : P // 2 - 1, :], 0.0)
        nc.gpsimd.memset(tu_window[P // 2 : P, :], 0.0)

        wg_window = [load_plane("wg", wg, "gate_up", 0)]
        nc.sync.dma_start(offsets[:], offs)
        nc.scalar.dma_start(out=tg_window[P - 1 : P, :], in_=tg[P - 1 : P, :])
        nc.scalar.dma_start(out=tu_window[P // 2 - 1 : P // 2, :], in_=tu[0:1, :])
        us_rows = tile("us_rows", [P, LANES], F32)
        wt_rows = tile("wt_rows", [P, LANES], F32)
        nc.sync.dma_start(out=us_rows[:], in_=us.rearrange("(m k) o -> m (k o)", k=LANES))
        nc.sync.dma_start(out=wt_rows[:], in_=wt.rearrange("(m k) o -> m (k o)", k=LANES))
        wg_window.extend(load_plane("wg", wg, "gate_up", j) for j in range(1, LANES))
        x_raw = load_rows("x", xT)
        dy_raw = []
        for h in range(2):
            dy_raw.append(tile("dy_raw%d" % h, [P, LANES * N // 2], F32))
            nc.sync.dma_start(out=dy_raw[h][:].rearrange("p (j r) -> p j r", j=LANES),
                              in_=dyT.rearrange("(p j) r -> p j r", j=LANES)[:, :, halves[h]])
        wd_window = load_planes("wd", wd, "down")

        wt_us = tile("wt_us", [P, LANES], F32)
        wt_us2 = tile("wt_us2", [P, LANES], F32)
        nc.gpsimd.tensor_tensor(out=wt_us[:], in0=us_rows[:], in1=wt_rows[:], op=ALU.mult)
        nc.gpsimd.tensor_tensor(out=wt_us2[:], in0=wt_us[:], in1=us_rows[:], op=ALU.mult)
        us_full = tile("us_full", [P, N], F32)
        nc.scalar.copy(out=us_full[:], in_=spread(us_rows, 7)[:])
        row_factor = spread(wt_us2, 4)

        wg_planes = tile("wg_planes", [P, LANES * N], BF16)
        gather("vector", wg_planes, wg_window[0], 0)
        listed = {}
        for name, window, b, live in (("tg", tg_window, 0, P - 1), ("tu", tu_window, 1, P // 2 - 1)):
            row = tile(name + "_row", [P, N], F32)
            nc.vector.tensor_copy(out=row[:], in_=window[:].indirect(offsets[:]))
            acc = bank(b)
            for t in range(LANES):
                nc.tensor.transpose(acc[:, block(t)], row[:, t:N:LANES], ident[:])
            listed[name] = tile(name + "_columns", [P, LANES], F32)
            nc.scalar.copy(out=listed[name][:], in_=acc[:, live:N:P])
            if name == "tg":
                half_tg, less_tg = tile("half_tg", [P, LANES], F32), tile("less_tg", [P, LANES], F32)
                nc.scalar.activation(out=half_tg[:], in_=acc[:, live:N:P], func=ACT.Copy, scale=0.5)
                nc.scalar.activation(out=less_tg[:], in_=acc[:, live:N:P], func=ACT.Copy, scale=-1.0)
        tgtu = tile("tgtu", [P, LANES], F32)
        nc.gpsimd.tensor_tensor(out=tgtu[:], in0=listed["tg"][:], in1=listed["tu"][:], op=ALU.mult)
        half_tgtu, less_half_tgtu = scaled("half_tgtu", tgtu, 0.5), scaled("less_half_tgtu", tgtu, -0.5)

        gather("vector", wg_planes, wg_window[1], 1)
        wg_turned_early = turn_pair("wg", 5, wg_planes, 0)
        gather("vector", wg_planes, wg_window[2], 2)
        wg_woven = tile("wg_woven", [P, N, LANES], BF16)
        wg_q = operand("wg", E4M3)
        last_plane(wg_q, wg_woven, wg_planes, wg_window[3])
        wu_window = load_planes("wu", wu, "gate_up")

        x_woven = tile("x_woven", [P, N, LANES], BF16)
        deal_shared(x_woven, x_raw)
        x_q = operand("x", E4M3)
        for columns in halves:
            quantise(x_q, x_woven, columns)
        wg_turned_late = turn_pair("wg", 6, wg_planes, 1, on_vector, "x_raw")
        wg_turned_q = operand("wg_turned", E4M3, "x_woven")
        quantise_into(wg_turned_q, halves[0], wg_turned_early[:])
        quantise_into(wg_turned_q, halves[1], wg_turned_late[:])

        dy_woven = tile("dy_woven", [P, N, LANES], BF16)
        for h in range(2):
            nc.scalar.copy(out=dy_woven[:].rearrange("p (t g q) (h e) -> p g q h t e", t=LANES, g=2, e=2)[:, h, :, :, :, :],
                           in_=dy_raw[h][:].rearrange("p (h e q t) -> p q h t e", h=2, e=2, t=LANES))

        ag = []
        z = tile("z", [P, LANES, N], F32)
        silu = tile("silu", [P, LANES, N], F32)
        tanh = tile("tanh", [P, LANES, N], F32, "dy_raw1")
        for t in range(LANES):
            ag.append(bank(t))
            product(ag[t][:], wg_q, t, x_q)
            nc.vector.tensor_tensor(out=z[:, t, :], in0=ag[t][:], in1=us_full[:], op=ALU.mult)
            nc.scalar.activation(out=tanh[:, t, :], in_=z[:, t, :], func=ACT.Tanh, scale=half_tg[:, t : t + 1])
            nc.scalar.activation(out=silu[:, t, :], in_=z[:, t, :], func=ACT.Silu, scale=less_tg[:, t : t + 1])

        dy_q = operand("dy", E5M2)
        for columns in halves:
            quantise(dy_q, dy_woven, columns)

        slope = tile("slope", [P, LANES, N], F32, "dy_woven")
        sig = tile("sig", [P, LANES, N], F32, "tu_window")
        for t in range(LANES):
            nc.gpsimd.tensor_scalar(out=slope[:, t, :], in0=silu[:, t, :], scalar1=less_half_tgtu[:, t : t + 1],
                                    scalar2=half_tgtu[:, t : t + 1], op0=ALU.mult, op1=ALU.add)
            nc.vector.scalar_tensor_tensor(out=sig[:, t, :], in0=tanh[:, t, :], scalar=1.0, in1=row_factor[:],
                                           op0=ALU.add, op1=ALU.mult)

        def up_factors(name, tag, first, count):
            rows = slice(P * first, P * (first + count))
            factors = tile(name, [P, LANES, P * count], F32, tag)
            for t in range(LANES):
                nc.vector.scalar_tensor_tensor(out=factors[:, t, :], in0=ag[t][:, rows], scalar=half_tgtu[:, t : t + 1],
                                               in1=sig[:, t, rows], op0=ALU.mult, op1=ALU.mult)
            return [factors[:, :, block(i)] for i in range(count)]

        def gate_parts(name, tag, tiles):
            parts = tile(name, [P, len(tiles), LANES, P], F32, tag)
            for i, k in enumerate(tiles):
                nc.gpsimd.tensor_tensor(out=parts[:, i, :, :], in0=slope[:, :, block(k)], in1=sig[:, :, block(k)], op=ALU.mult)
            return [parts[:, i, :, :] for i in range(len(tiles))]

        up_factor = up_factors("up_factor_low", None, 0, LANES - 1)
        gate_part = gate_parts("gate_part_low", None, [0, 1])
        wd_planes = tile("wd_planes", [P, LANES * N], BF16)
        wd_woven = tile("wd_woven", [P, N, LANES], BF16)
        wd_q = operand("wd", E4M3)
        for j in range(2):
            gather("scalar", wd_planes, wd_window[j], j)
        gather("vector", wd_planes, wd_window[2], 2, slice(0, N - P))
        gather("scalar", wd_planes, wd_window[2], 2, slice(N - P, N))
        last_plane(wd_q, wd_woven, wd_planes, wd_window[3])
        up_factor.extend(up_factors("up_factor_high", "wd_planes", LANES - 1, 1))
        gate_part.extend(gate_parts("gate_part_high", "wd_woven", [2, 3]))

        def by_runs(woven, k):
            return woven[:, block(k), :].rearrange("q (c i) t -> q c t i", i=RUN)

        def lanes_by_runs(x):
            return x.rearrange("q t (c i) -> q c t i", i=RUN)

        def by_lane(acc):
            return acc[:, :].rearrange("q (t m) -> q t m", t=LANES)

        wu_planes = tile("wu_planes", [P, LANES * N], BF16)
        dh = []
        du = tile("du", [P, N, LANES], BF16)
        for k in range(LANES):
            dh.append(bank(LANES + k))
            for t in range(LANES):
                product(dh[k][:, block(t)], wd_q, t, dy_q, block(k))
            nc.vector.tensor_tensor(out=by_runs(du, k), in0=lanes_by_runs(by_lane(dh[k])),
                                    in1=lanes_by_runs(up_factor[k]), op=ALU.mult)
            if k == 0:
                gather("scalar", wu_planes, wu_window[0], 0)
                dh_first = tile("dh_first", [P, N], F32, "gate_up0")
                nc.scalar.copy(out=dh_first[:], in_=dh[k][:])

        def gate_factors(name, tag, tiles):
            factors = tile(name, [P, len(tiles), LANES, P], F32, tag)
            for i, k in enumerate(tiles):
                nc.vector.tensor_tensor(out=factors[:, i, :, :], in0=by_lane(dh[k]), in1=gate_part[k], op=ALU.mult)
            return [factors[:, i, :, :] for i in range(len(tiles))]

        gate_factor_first = tile("gate_factor_first", [P, LANES, P], F32)
        nc.gpsimd.tensor_tensor(out=gate_factor_first[:], in0=by_lane(dh_first), in1=gate_part[0], op=ALU.mult)
        gate_factor = [gate_factor_first[:]] + gate_factors("gate_factor_rest", "z", range(1, LANES))

        wu_woven = tile("wu_woven", [P, N, LANES], BF16)
        wu_q = operand("wu", E4M3)
        wu_turned_q = operand("wu_turned", E4M3)
        du_q = operand("du", E5M2)
        gather("scalar", wu_planes, wu_window[1], 1)
        wu_turned_early = turn_planes("wu", (0, 1), wu_planes, 0, "gate_up1")
        gather("scalar", wu_planes, wu_window[2], 2)
        for columns in halves:
            quantise(du_q, du, columns)
        quantise_into(wu_turned_q, halves[0], wu_turned_early[:])
        sums = []
        for k in range(LANES):
            sums.append(bank(LANES + k))
            product(sums[k][:, halves[0]], du_q, k, wu_turned_q, halves[0], start=True, stop=False)

        last_plane(wu_q, wu_woven, wu_planes, wu_window[3], [halves[0], block(2), block(3)])
        wu_turned_late = turn_planes("wu", (2, 3), wu_planes, 1, "gate_up3")
        quantise_into(wu_turned_q, halves[1], wu_turned_late[:])
        au = []
        for k in range(LANES):
            au.append(bank(k))
            for t in range(LANES):
                product(au[k][:, block(t)], wu_q, t, x_q, block(k))
        result = tile("result", [P, LANES, N], F32)
        result_woven = tile("result_woven", [P, N, LANES], BF16)
        out_rows = out_0.rearrange("(m t) d -> m t d", t=LANES)
        dg = tile("dg", [P, N, LANES], BF16)
        dg_q = operand("dg", E5M2)

        def gate_gradient(k, part=slice(0, P // RUN)):
            nc.vector.tensor_tensor(out=by_runs(dg, k)[:, part, :, :], in0=lanes_by_runs(by_lane(au[k]))[:, part, :, :],
                                    in1=lanes_by_runs(gate_factor[k])[:, part, :, :], op=ALU.mult)

        def weave_result(copy, columns, lanes):
            copy(out=result_woven[:, columns, lanes].rearrange("p (c i) j -> p c j i", i=2),
                 in_=result[:, lanes, columns].rearrange("p j (c i) -> p c j i", i=2))

        def finish(k):
            acc = sums[k]
            product(acc[:], dg_q, k, wg_turned_q, start=False, stop=True)
            by_feature = result[:, k, :].rearrange("m (c i j) -> m c j i", i=2, j=LANES)
            by_plane = acc[:].rearrange("m (j c i) -> m c j i", i=2, j=LANES)
            for rows in [slice(0, P // 8), slice(P // 8, P // 4), slice(P // 4, P // 2)] if k == LANES - 1 else [slice(0, P // 2)]:
                nc.scalar.copy(out=by_feature[:, rows, :, :], in_=by_plane[:, rows, :, :])
            nc.sync.dma_start(out=out_rows[:, k, :], in_=result[:, k, :])

        gate_gradient(0)
        for k in range(LANES):
            product(sums[k][:, halves[1]], du_q, k, wu_turned_q, halves[1], start=False, stop=False)
        for k in range(1, LANES - 1):
            gate_gradient(k)
            quantise(dg_q, dg, block(k - 1))
            finish(k - 1)
        gate_gradient(LANES - 1, slice(0, P // RUN // 2))
        quantise(dg_q, dg, block(LANES - 2))
        finish(LANES - 2)
        gate_gradient(LANES - 1, slice(P // RUN // 2, P // RUN))
        for h in range(2):
            quantise(dg_q, dg, slice(N - P + h * P // 2, N - P + (h + 1) * P // 2))
        finish(LANES - 1)
        weave_result(on_vector, slice(0, N), slice(0, 2))

        out_codes = tile("out_codes", [P, N], U32)
        out_scales = tile("out_scales", [P, N], U8)
        codes_hbm = out_1[0].rearrange("p c lane -> p (c lane)").bitcast(I32)
        for copy, columns in ((on_vector, slice(0, N // 4)), (on_vector, slice(N // 4, N // 2)), (on_vector, slice(N // 2, 3 * N // 4)), (on_scalar, slice(3 * N // 4, N))):
            weave_result(copy, columns, slice(2, 4))
        for columns in halves:
            quantise((out_codes, out_scales, E4M3), result_woven, columns)
            nc.sync.dma_start(out=codes_hbm[:, columns], in_=out_codes[:, columns].bitcast(I32))
        scales_hbm = out_2[0].bitcast(I32)
        for q in range(4):
            queue = nc.scalar if q % 2 else nc.sync
            queue.dma_start(out=scales_hbm[4 * q : 4 * q + 4, :], in_=out_scales[32 * q : 32 * q + 4, :].bitcast(I32))
